import numpy as np
import ml_dtypes


def mxq(x, axis, fmt="e4m3"):
    dtype, down = {"e4m3": (ml_dtypes.float8_e4m3fn, 7), "e5m2": (ml_dtypes.float8_e5m2, 14)}[fmt]
    v = np.moveaxis(np.asarray(x, np.float32).astype(ml_dtypes.bfloat16).astype(np.float64), axis, -1)
    blocks = v.reshape(v.shape[:-1] + (-1, 32))
    amax = np.abs(blocks).max(-1, keepdims=True)
    byte = np.maximum(np.where(amax > 0, np.frexp(amax)[1] - 1 + 127, 0) - down, 1)
    scale = np.exp2(byte - 127.0)
    codes = (blocks / scale).astype(np.float32).astype(dtype).astype(np.float64)
    return np.moveaxis((codes * scale).reshape(v.shape), -1, axis)


WIDE = False


def mx_kscale(k):
    if not WIDE:
        return np.ones(k)
    levels = np.array([10, -10, 5, -5, 0])
    if k % 512:
        return np.exp2(np.random.permutation(np.resize(levels, k // 32))).repeat(32)
    a = np.empty((k // 512, 16))
    for p in range(k // 512):
        a[p, :8] = np.random.permutation(np.resize(levels, 8))
        for g in range(8):
            far = levels[np.abs(levels - a[p, g]) >= 10]
            a[p, g + 8] = far[np.random.randint(len(far))]
    return np.exp2(a.ravel()).repeat(32)


def f64(x):
    return np.asarray(x).astype(np.float64)


def striped(idx):
    return np.tile(idx.reshape(-1, 16).T, (8, 1)).astype(np.uint16)


def unstriped(offs):
    return offs[:16].T.reshape(-1).astype(np.int64)


def silu(v):
    return v / (1.0 + np.exp(-np.maximum(v, -700.0)))


K, T, E, C, H, N = 1536, 1024, 2, 256, 512, 384


def by_expert(wq, xq):
    return np.concatenate([wq[e].T @ xq[:, e * C:(e + 1) * C] for e in range(E)], axis=1)


def setup_inputs():
    n = np.random.standard_normal
    s = mx_kscale(K)[:, None]
    u = mx_kscale(H)
    return {
        "xT": (n((K, T)) * s).astype(np.float32),
        "xr": n((N, T)).astype(np.float32),
        "w1": (n((E, K, H)) / np.sqrt(K) / s[None]).astype(np.float32),
        "w3": (n((E, K, H)) / np.sqrt(K) / s[None] * u[None, None, :]).astype(np.float32),
        "w2": (n((E, H, N)) / np.sqrt(H) / u[None, :, None]).astype(np.float32),
        "gate": np.tile(np.random.uniform(0.2, 1.0, E * C), (N, 1)).astype(np.float32),
        "offs": striped(np.random.permutation(T)[:E * C]),
    }


def reference(xT, xr, w1, w3, w2, gate, offs):
    idx = unstriped(offs)
    xq = mxq(f64(xT)[:, idx], 0, "e4m3")
    h = silu(by_expert(mxq(f64(w1), 1, "e4m3"), xq))
    h = h * by_expert(mxq(f64(w3), 1, "e4m3"), xq)
    y = by_expert(mxq(f64(w2), 1, "e4m3"), mxq(h, 0, "e4m3"))
    out = f64(xr).copy()
    out[:, idx] += f64(gate) * y
    return out

@@ -1,0 +1,277 @@
+from contextlib import ExitStack
+
+import concourse.mybir as mybir
+
+K, T, E, C, H, N = 1536, 1024, 2, 256, 512, 384
+
+F32 = mybir.dt.float32
+BF16 = mybir.dt.bfloat16
+U32 = mybir.dt.uint32
+U16 = mybir.dt.uint16
+U8 = mybir.dt.uint8
+FP8X4 = mybir.dt.float8_e4m3fn_x4
+MULT, ADD = mybir.AluOpType.mult, mybir.AluOpType.add
+SILU, COPY = mybir.ActivationFunctionType.Silu, mybir.ActivationFunctionType.Copy
+
+P = 128
+PACK = 4
+K_PASS = P * PACK
+PASSES = K // K_PASS
+H_TILES = H // P
+N_TILES = N // P
+SLOTS = E * C
+HALF = C // 2
+RUN = 4
+T_HALF = T // 2
+
+FLOPS = 2 * SLOTS * (2 * K * H + H * N)
+BYTES = 4 * (K * T + 2 * N * T + E * (2 * K * H + H * N) + SLOTS) + 2 * P * SLOTS // 16
+
+
+def tile_moe_res_glu_silu_kernel(tc, xT, xr, w1, w3, w2, gate, offs, out):
+    nc = tc.nc
+    by_vector, by_scalar = nc.vector.tensor_copy, nc.scalar.copy
+    with ExitStack() as ctx:
+        keep = ctx.enter_context(tc.tile_pool(name="keep", bufs=1))
+        token_pool = ctx.enter_context(tc.tile_pool(name="tokens", bufs=PASSES))
+        raw_pool = ctx.enter_context(tc.tile_pool(name="raw", bufs=8))
+        stage = ctx.enter_context(tc.tile_pool(name="stage", bufs=6))
+        mid = ctx.enter_context(tc.tile_pool(name="mid", bufs=2))
+        psum = ctx.enter_context(tc.psum_pool(name="psum", bufs=1))
+
+        offsets = keep.tile([P, SLOTS // 16], U16, name="offsets")
+        nc.sync.dma_start(offsets[:], offs)
+
+        warm = keep.tile([P, 1], F32, name="warm")
+        nc.gpsimd.memset(warm[:], 0.0)
+        warm_out = keep.tile([P, 1], F32, name="warm_out")
+        nc.scalar.activation(warm_out[:], warm[:], SILU)
+
+        x_words = [keep.tile([P, T], U32, name=f"x_words{s}", align_bytes=64) for s in range(PASSES)]
+        x_scales = keep.tile([P, T], U8, name="x_scales", align_bytes=64)
+        nc.gpsimd.memset(x_scales[:], 0)
+        windows = [keep.tile([P, T], F32, name=f"window{m}") for m in range(N_TILES)]
+        for m in range(N_TILES):
+            nc.gpsimd.memset(windows[m][:], 0.0)
+        slot_words = [keep.tile([P, SLOTS], U32, name=f"slot_words{s}", align_bytes=64) for s in range(PASSES)]
+        slot_scales = keep.tile([P, SLOTS], U8, name="slot_scales", align_bytes=64)
+
+        gate_sb = keep.tile([P, SLOTS], F32, name="gate_sb")
+        weights = {"w1": w1, "w3": w3}
+        raws, grouped, codes, scales = {}, {}, {}, {}
+        w2_raw, w2_grouped, w2_codes, w2_scales = {}, {}, {}, {}
+        residual = []
+
+        def load_tokens(s):
+            raws["x", s] = token_pool.tile([P, PACK, T], F32, name="tokens")
+            nc.sync.dma_start(raws["x", s][:], xT[s * K_PASS : (s + 1) * K_PASS, :].rearrange("(p j) t -> p j t", j=PACK))
+
+        def load_chunk(name, e, s):
+            raws[name, e, s] = raw_pool.tile([P, PACK, H], F32, name="raw")
+            rows = weights[name][e, s * K_PASS : (s + 1) * K_PASS, :]
+            nc.sync.dma_start(raws[name, e, s][:], rows.rearrange("(p j) i -> p j i", j=PACK))
+
+        def load_w2(e, pool, name):
+            w2_raw[e] = pool.tile([P, PACK, N], F32, name=name)
+            nc.sync.dma_start(w2_raw[e][:], w2[e].rearrange("(p j) n -> p j n", j=PACK))
+
+        def load_rest():
+            load_w2(1, raw_pool, "raw")
+            for m in range(N_TILES):
+                res = raw_pool.tile([P, T], F32, name="raw")
+                nc.sync.dma_start(res[:], xr[m * P : (m + 1) * P, :])
+                residual.append(res)
+
+        def copy_tokens(s, first, copy):
+            grouped["x", s, first] = stage.tile([P, T_HALF * PACK], BF16, name="grouped", align_bytes=64)
+            src = raws["x", s][:, :, first : first + T_HALF].rearrange("p j (c i) -> p c j i", i=RUN)
+            copy(grouped["x", s, first][:].rearrange("p (c i j) -> p c j i", i=RUN, j=PACK), src)
+
+        def quantise_tokens(s, first):
+            cols = slice(first, first + T_HALF)
+            nc.vector.quantize_mx(out=x_words[s][:, cols].bitcast(FP8X4), scales=x_scales[4 * s : P, cols], in_=grouped["x", s, first][:])
+
+        def copy_chunk(key, *cuts):
+            grouped[key] = stage.tile([P, H * PACK], BF16, name="grouped", align_bytes=64)
+            src = raws[key][:].rearrange("p j (m t) -> p m j t", t=H_TILES)
+            dst = grouped[key][:].rearrange("p (t m j) -> p m j t", t=H_TILES, j=PACK)
+            for copy, first, end in cuts:
+                copy(dst[:, first:end], src[:, first:end])
+            if later_loads:
+                later_loads.pop(0)()
+
+        def quantise_chunk(key, pieces=1):
+            codes[key] = keep.tile([P, H], U32, name="codes_%s_%d_%d" % key, align_bytes=64)
+            scales[key] = keep.tile([P, H], U8, name="scales_%s_%d_%d" % key, align_bytes=64)
+            width = H // pieces
+            for a in range(0, H, width):
+                cols = slice(a, a + width)
+                source = grouped[key][:, PACK * a : PACK * (a + width)]
+                nc.vector.quantize_mx(out=codes[key][:, cols].bitcast(FP8X4), scales=scales[key][:, cols], in_=source)
+
+        def prepare_w2(e):
+            w2_grouped[e] = keep.tile([P, N * PACK], BF16, name=f"w2_grouped{e}", align_bytes=64)
+            src = w2_raw[e][:].rearrange("p j (c i) -> p c j i", i=RUN)
+            nc.scalar.copy(w2_grouped[e][:].rearrange("p (c i j) -> p c j i", i=RUN, j=PACK), src)
+            w2_codes[e] = keep.tile([P, N], U32, name=f"w2_codes{e}", align_bytes=64)
+            w2_scales[e] = keep.tile([P, N], U8, name=f"w2_scales{e}", align_bytes=64)
+            for a, b in ((0, 256), (256, N)):
+                source = w2_grouped[e][:, PACK * a : PACK * b]
+                nc.vector.quantize_mx(out=w2_codes[e][:, a:b].bitcast(FP8X4), scales=w2_scales[e][:, a:b], in_=source)
+
+        def gather_words(s):
+            nc.vector.tensor_copy(slot_words[s][:], x_words[s][:].indirect(offsets[:]))
+
+        def gather_scales():
+            nc.vector.tensor_copy(slot_scales[:], x_scales[:].indirect(offsets[:]))
+
+        def first_layer(name, e):
+            banks = []
+            for half in range(2):
+                bank = psum.tile([P, H_TILES, HALF], F32, name=f"{name}_bank{half}")
+                slots = slice(e * C + half * HALF, e * C + (half + 1) * HALF)
+                for t in range(H_TILES):
+                    channels = slice(t * P, (t + 1) * P)
+                    for s in range(PASSES):
+                        nc.tensor.matmul_mx(
+                            out=bank[:, t, :],
+                            lhsT=codes[name, e, s][:, channels].bitcast(FP8X4),
+                            lhsT_scale=scales[name, e, s][:, channels],
+                            rhs=slot_words[s][:, slots].bitcast(FP8X4),
+                            rhs_scale=slot_scales[4 * s : P, slots],
+                            start=(s == 0),
+                            stop=(s == PASSES - 1),
+                        )
+                banks.append(bank)
+            return banks
+
+        def silu_of(banks):
+            acts = []
+            for bank in banks:
+                act = mid.tile([P, HALF, H_TILES], F32, name="act")
+                nc.scalar.activation(act[:], bank[:].rearrange("p t n -> p n t"), SILU)
+                acts.append(act)
+            return acts
+
+        def hidden(acts, banks):
+            halves = []
+            for act, bank in zip(acts, banks):
+                h = mid.tile([P, HALF, H_TILES], BF16, name="h", align_bytes=64)
+                nc.vector.tensor_tensor(h[:], bank[:].rearrange("p t n -> p n t"), act[:], MULT)
+                halves.append(h)
+            return halves
+
+        def quantise_hidden(halves):
+            packed = []
+            for h in halves:
+                h_codes = mid.tile([P, HALF], U32, name="h_codes", align_bytes=64)
+                h_scales = mid.tile([P, HALF], U8, name="h_scales", align_bytes=64)
+                nc.vector.quantize_mx(out=h_codes[:].bitcast(FP8X4), scales=h_scales[:], in_=h[:].rearrange("p n t -> p (n t)"))
+                packed.append((h_codes, h_scales))
+            return packed
+
+        def second_layer(e, packed):
+            banks = []
+            for half, (h_codes, h_scales) in enumerate(packed):
+                bank = psum.tile([P, N_TILES, HALF], F32, name=f"y_bank{half}")
+                for m in range(N_TILES):
+                    rows = slice(m * P, (m + 1) * P)
+                    nc.tensor.matmul_mx(
+                        out=bank[:, m, :],
+                        lhsT=w2_codes[e][:, rows].bitcast(FP8X4),
+                        lhsT_scale=w2_scales[e][:, rows],
+                        rhs=h_codes[:].bitcast(FP8X4),
+                        rhs_scale=h_scales[:],
+                        start=True,
+                        stop=True,
+                    )
+                banks.append(bank)
+            return banks
+
+        def take_y(y, banks):
+            for half, bank in enumerate(banks):
+                nc.scalar.activation(y[:, :, half * HALF : (half + 1) * HALF], bank[:], COPY)
+
+        def scatter(e, m, y, a=0, b=C):
+            first, end = e * C + a, e * C + b
+            window = windows[m][:].indirect(offsets[:, first // 16 : end // 16])
+            nc.vector.tensor_tensor(window, y[:, m, a:b], gate_sb[:, first:end], MULT)
+
+        def finish(m, parts=1):
+            width = T // parts
+            for a in range(0, T, width):
+                cols = slice(a, a + width)
+                nc.vector.tensor_tensor(residual[m][:, cols], windows[m][:, cols], residual[m][:, cols], ADD)
+                nc.sync.dma_start(out[m * P : (m + 1) * P, cols], residual[m][:, cols])
+
+        later_loads = [lambda key=key: load_chunk(*key) for key in (("w1", 1, 2), ("w3", 1, 0), ("w3", 1, 1), ("w3", 1, 2))]
+        later_loads.append(load_rest)
+        for s in range(PASSES):
+            load_tokens(s)
+            load_chunk("w1", 0, s)
+        for s in range(PASSES):
+            load_chunk("w3", 0, s)
+        load_w2(0, keep, "w2_raw0")
+        nc.sync.dma_start(gate_sb[:], gate[0:P, :])
+        load_chunk("w1", 1, 0)
+        load_chunk("w1", 1, 1)
+
+        for s in range(PASSES):
+            copy_tokens(s, 0, by_vector)
+            copy_tokens(s, T_HALF, by_scalar)
+            if s > 0:
+                gather_words(s - 1)
+                quantise_chunk(("w1", 0, s - 1))
+            quantise_tokens(s, 0)
+            quantise_tokens(s, T_HALF)
+            copy_chunk(("w1", 0, s), (by_scalar, 0, P))
+        copy_chunk(("w3", 0, 0), (by_scalar, 0, P))
+        gather_words(PASSES - 1)
+        quantise_chunk(("w1", 0, PASSES - 1))
+        gather_scales()
+        copy_chunk(("w3", 0, 1), (by_vector, 0, P))
+        quantise_chunk(("w3", 0, 0))
+        copy_chunk(("w3", 0, 2), (by_vector, 0, P // 2), (by_scalar, P // 2, P))
+        quantise_chunk(("w3", 0, 1))
+        quantise_chunk(("w3", 0, 2))
+
+        ys = [mid.tile([P, N_TILES, C], F32, name="y") for e in range(E)]
+
+        w1_banks = first_layer("w1", 0)
+        acts = silu_of(w1_banks)
+        packed = quantise_hidden(hidden(acts, first_layer("w3", 0)))
+        prepare_w2(0)
+        y_banks = second_layer(0, packed)
+
+        copy_chunk(("w1", 1, 0), (by_scalar, 0, P))
+        take_y(ys[0], y_banks)
+        quantise_chunk(("w1", 1, 0))
+        copy_chunk(("w1", 1, 1), (by_vector, 0, P))
+        scatter(0, 0, ys[0])
+        quantise_chunk(("w1", 1, 1))
+        copy_chunk(("w1", 1, 2), (by_scalar, 0, P))
+        scatter(0, 1, ys[0])
+        quantise_chunk(("w1", 1, 2))
+        w1_banks = first_layer("w1", 1)
+        copy_chunk(("w3", 1, 0), (by_scalar, 0, P))
+        acts = silu_of(w1_banks)
+        scatter(0, 2, ys[0])
+        quantise_chunk(("w3", 1, 0))
+        copy_chunk(("w3", 1, 1), (by_vector, 0, P))
+        quantise_chunk(("w3", 1, 1))
+        copy_chunk(("w3", 1, 2), (by_scalar, 0, 48), (by_vector, 48, P))
+        quantise_chunk(("w3", 1, 2), pieces=H_TILES)
+        packed = quantise_hidden(hidden(acts, first_layer("w3", 1)))
+        prepare_w2(1)
+        y_banks = second_layer(1, packed)
+        take_y(ys[1], y_banks)
+
+        for half in range(2):
+            for m in range(N_TILES - 1):
+                scatter(1, m, ys[1], half * HALF, (half + 1) * HALF)
+        last = N_TILES - 1
+        scatter(1, last, ys[1], 0, HALF)
+        finish(0)
+        scatter(1, last, ys[1], HALF, C)
+        finish(1)
+        finish(last, parts=2)

@@ -23,6 +23,7 @@ SLOTS = E * C
 HALF = C // 2
 RUN = 4
 T_HALF = T // 2
+KIB = 1024
 
 FLOPS = 2 * SLOTS * (2 * K * H + H * N)
 BYTES = 4 * (K * T + 2 * N * T + E * (2 * K * H + H * N) + SLOTS) + 2 * P * SLOTS // 16
@@ -33,11 +34,12 @@ def tile_moe_res_glu_silu_kernel(tc, xT, xr, w1, w3, w2, gate, offs, out):
     by_vector, by_scalar = nc.vector.tensor_copy, nc.scalar.copy
     with ExitStack() as ctx:
         keep = ctx.enter_context(tc.tile_pool(name="keep", bufs=1))
-        token_pool = ctx.enter_context(tc.tile_pool(name="tokens", bufs=PASSES))
-        raw_pool = ctx.enter_context(tc.tile_pool(name="raw", bufs=8))
-        stage = ctx.enter_context(tc.tile_pool(name="stage", bufs=6))
-        mid = ctx.enter_context(tc.tile_pool(name="mid", bufs=2))
+        loads = ctx.enter_context(tc.tile_pool(name="loads", bufs=1))
+        work = ctx.enter_context(tc.tile_pool(name="work", bufs=1))
         psum = ctx.enter_context(tc.psum_pool(name="psum", bufs=1))
+
+        def placed(pool, name, shape, dtype, at):
+            return pool.tile(shape, dtype, name=name, offset=at, align_bytes=64)
 
         offsets = keep.tile([P, SLOTS // 16], U16, name="offsets")
         nc.sync.dma_start(offsets[:], offs)
@@ -56,34 +58,32 @@ def tile_moe_res_glu_silu_kernel(tc, xT, xr, w1, w3, w2, gate, offs, out):
         slot_words = [keep.tile([P, SLOTS], U32, name=f"slot_words{s}", align_bytes=64) for s in range(PASSES)]
         slot_scales = keep.tile([P, SLOTS], U8, name="slot_scales", align_bytes=64)
 
-        gate_sb = keep.tile([P, SLOTS], F32, name="gate_sb")
         weights = {"w1": w1, "w3": w3}
+        chunks = [[(name, e, s) for name in ("w3", "w1") for s in range(PASSES)] for e in range(E)]
         raws, grouped, codes, scales = {}, {}, {}, {}
-        w2_raw, w2_grouped, w2_codes, w2_scales = {}, {}, {}, {}
+        w2_raw, w2_codes, w2_scales = {}, {}, {}
         residual = []
 
         def load_tokens(s):
-            raws["x", s] = token_pool.tile([P, PACK, T], F32, name="tokens")
+            raws["x", s] = placed(loads, f"tokens{s}", [P, PACK, T], F32, 16 * KIB * s)
             nc.sync.dma_start(raws["x", s][:], xT[s * K_PASS : (s + 1) * K_PASS, :].rearrange("(p j) t -> p j t", j=PACK))
 
-        def load_chunk(name, e, s):
-            raws[name, e, s] = raw_pool.tile([P, PACK, H], F32, name="raw")
+        def load_chunk(key, at):
+            name, e, s = key
+            raws[key] = placed(loads, "raw_%s_%d_%d" % key, [P, PACK, H], F32, at)
             rows = weights[name][e, s * K_PASS : (s + 1) * K_PASS, :]
-            nc.sync.dma_start(raws[name, e, s][:], rows.rearrange("(p j) i -> p j i", j=PACK))
+            nc.sync.dma_start(raws[key][:], rows.rearrange("(p j) i -> p j i", j=PACK))
 
-        def load_w2(e, pool, name):
-            w2_raw[e] = pool.tile([P, PACK, N], F32, name=name)
+        def load_w2(e, at):
+            w2_raw[e] = placed(loads, f"w2_raw{e}", [P, PACK, N], F32, at)
             nc.sync.dma_start(w2_raw[e][:], w2[e].rearrange("(p j) n -> p j n", j=PACK))
 
-        def load_rest():
-            load_w2(1, raw_pool, "raw")
-            for m in range(N_TILES):
-                res = raw_pool.tile([P, T], F32, name="raw")
-                nc.sync.dma_start(res[:], xr[m * P : (m + 1) * P, :])
-                residual.append(res)
+        def load_residual(m):
+            residual.append(placed(loads, f"residual{m}", [P, T], F32, 8 * KIB * (9 + m)))
+            nc.sync.dma_start(residual[m][:], xr[m * P : (m + 1) * P, :])
 
-        def copy_tokens(s, first, copy):
-            grouped["x", s, first] = stage.tile([P, T_HALF * PACK], BF16, name="grouped", align_bytes=64)
+        def copy_tokens(s, first, copy, at):
+            grouped["x", s, first] = placed(work, f"x_grouped{s}_{first}", [P, T_HALF * PACK], BF16, at)
             src = raws["x", s][:, :, first : first + T_HALF].rearrange("p j (c i) -> p c j i", i=RUN)
             copy(grouped["x", s, first][:].rearrange("p (c i j) -> p c j i", i=RUN, j=PACK), src)
 
@@ -91,17 +91,20 @@ def tile_moe_res_glu_silu_kernel(tc, xT, xr, w1, w3, w2, gate, offs, out):
             cols = slice(first, first + T_HALF)
             nc.vector.quantize_mx(out=x_words[s][:, cols].bitcast(FP8X4), scales=x_scales[4 * s : P, cols], in_=grouped["x", s, first][:])
 
-        def copy_chunk(key, *cuts):
-            grouped[key] = stage.tile([P, H * PACK], BF16, name="grouped", align_bytes=64)
+        def copy_chunk(key, vector_share, at):
+            grouped[key] = placed(work, "grouped_%s_%d_%d" % key, [P, H * PACK], BF16, at)
             src = raws[key][:].rearrange("p j (m t) -> p m j t", t=H_TILES)
             dst = grouped[key][:].rearrange("p (t m j) -> p m j t", t=H_TILES, j=PACK)
-            for copy, first, end in cuts:
-                copy(dst[:, first:end], src[:, first:end])
-            if later_loads:
-                later_loads.pop(0)()
+            if vector_share > 0:
+                by_vector(dst[:, :vector_share], src[:, :vector_share])
+            if vector_share < P:
+                by_scalar(dst[:, vector_share:], src[:, vector_share:])
 
-        def quantise_chunk(key, pieces=1):
-            codes[key] = keep.tile([P, H], U32, name="codes_%s_%d_%d" % key, align_bytes=64)
+        def quantise_chunk(key, pieces=1, at=None):
+            if at is None:
+                codes[key] = keep.tile([P, H], U32, name="codes_%s_%d_%d" % key, align_bytes=64)
+            else:
+                codes[key] = placed(work, "codes_%s_%d_%d" % key, [P, H], U32, at)
             scales[key] = keep.tile([P, H], U8, name="scales_%s_%d_%d" % key, align_bytes=64)
             width = H // pieces
             for a in range(0, H, width):
@@ -109,15 +112,20 @@ def tile_moe_res_glu_silu_kernel(tc, xT, xr, w1, w3, w2, gate, offs, out):
                 source = grouped[key][:, PACK * a : PACK * (a + width)]
                 nc.vector.quantize_mx(out=codes[key][:, cols].bitcast(FP8X4), scales=scales[key][:, cols], in_=source)
 
-        def prepare_w2(e):
-            w2_grouped[e] = keep.tile([P, N * PACK], BF16, name=f"w2_grouped{e}", align_bytes=64)
-            src = w2_raw[e][:].rearrange("p j (c i) -> p c j i", i=RUN)
-            nc.scalar.copy(w2_grouped[e][:].rearrange("p (c i j) -> p c j i", i=RUN, j=PACK), src)
-            w2_codes[e] = keep.tile([P, N], U32, name=f"w2_codes{e}", align_bytes=64)
+        W2_CUTS = ((0, 256), (256, N))
+
+        def copy_w2(e, copy, at):
+            grouped["w2", e] = placed(work, f"w2_grouped{e}", [P, N * PACK], BF16, at)
+            w2_codes[e] = placed(work, f"w2_codes{e}", [P, N], U32, 12 * KIB)
             w2_scales[e] = keep.tile([P, N], U8, name=f"w2_scales{e}", align_bytes=64)
-            for a, b in ((0, 256), (256, N)):
-                source = w2_grouped[e][:, PACK * a : PACK * b]
-                nc.vector.quantize_mx(out=w2_codes[e][:, a:b].bitcast(FP8X4), scales=w2_scales[e][:, a:b], in_=source)
+            for a, b in W2_CUTS:
+                src = w2_raw[e][:, :, a:b].rearrange("p j (c i) -> p c j i", i=RUN)
+                copy(grouped["w2", e][:, PACK * a : PACK * b].rearrange("p (c i j) -> p c j i", i=RUN, j=PACK), src)
+
+        def quantise_w2(e, part):
+            a, b = W2_CUTS[part]
+            source = grouped["w2", e][:, PACK * a : PACK * b]
+            nc.vector.quantize_mx(out=w2_codes[e][:, a:b].bitcast(FP8X4), scales=w2_scales[e][:, a:b], in_=source)
 
         def gather_words(s):
             nc.vector.tensor_copy(slot_words[s][:], x_words[s][:].indirect(offsets[:]))
@@ -125,153 +133,193 @@ def tile_moe_res_glu_silu_kernel(tc, xT, xr, w1, w3, w2, gate, offs, out):
         def gather_scales():
             nc.vector.tensor_copy(slot_scales[:], x_scales[:].indirect(offsets[:]))
 
-        def first_layer(name, e):
+        def first_layer_pass(bank, key, t, slots):
+            s = key[2]
+            channels = slice(t * P, (t + 1) * P)
+            nc.tensor.matmul_mx(
+                out=bank,
+                lhsT=codes[key][:, channels].bitcast(FP8X4),
+                lhsT_scale=scales[key][:, channels],
+                rhs=slot_words[s][:, slots].bitcast(FP8X4),
+                rhs_scale=slot_scales[4 * s : P, slots],
+                start=(s == 0),
+                stop=(s == PASSES - 1),
+            )
+
+        def linear_branch(e):
             banks = []
             for half in range(2):
-                bank = psum.tile([P, H_TILES, HALF], F32, name=f"{name}_bank{half}")
+                bank = psum.tile([P, H_TILES, HALF], F32, name=f"g_bank{half}")
                 slots = slice(e * C + half * HALF, e * C + (half + 1) * HALF)
                 for t in range(H_TILES):
-                    channels = slice(t * P, (t + 1) * P)
                     for s in range(PASSES):
-                        nc.tensor.matmul_mx(
-                            out=bank[:, t, :],
-                            lhsT=codes[name, e, s][:, channels].bitcast(FP8X4),
-                            lhsT_scale=scales[name, e, s][:, channels],
-                            rhs=slot_words[s][:, slots].bitcast(FP8X4),
-                            rhs_scale=slot_scales[4 * s : P, slots],
-                            start=(s == 0),
-                            stop=(s == PASSES - 1),
-                        )
+                        first_layer_pass(bank[:, t, :], ("w3", e, s), t, slots)
                 banks.append(bank)
             return banks
 
-        def silu_of(banks):
-            acts = []
-            for bank in banks:
-                act = mid.tile([P, HALF, H_TILES], F32, name="act")
-                nc.scalar.activation(act[:], bank[:].rearrange("p t n -> p n t"), SILU)
-                acts.append(act)
+        def silu_banks():
+            return [psum.tile([P, C], F32, name=f"a_bank{t}") for t in range(H_TILES)]
+
+        def silu_branch_pass(banks, e, s):
+            for t in range(H_TILES):
+                first_layer_pass(banks[t][:], ("w1", e, s), t, slice(e * C, (e + 1) * C))
+
+        def silu_of(e, banks):
+            acts = [placed(work, f"act{e}_{half}", [P, H_TILES, HALF], F32, 2 * KIB * (1 - half)) for half in range(2)]
+            for t in range(H_TILES):
+                for half in range(2):
+                    nc.scalar.activation(acts[half][:, t, :], banks[t][:, half * HALF : (half + 1) * HALF], SILU)
             return acts
 
-        def hidden(acts, banks):
+        def hidden(e, acts, banks):
             halves = []
-            for act, bank in zip(acts, banks):
-                h = mid.tile([P, HALF, H_TILES], BF16, name="h", align_bytes=64)
-                nc.vector.tensor_tensor(h[:], bank[:].rearrange("p t n -> p n t"), act[:], MULT)
+            for half in range(2):
+                h = placed(work, f"h{e}_{half}", [P, HALF * H_TILES], BF16, 16 * KIB + half * KIB)
+                nc.vector.tensor_tensor(
+                    h[:].rearrange("p (c i t) -> p c t i", i=2, t=H_TILES),
+                    banks[half][:].rearrange("p t (c i) -> p c t i", i=2),
+                    acts[half][:].rearrange("p t (c i) -> p c t i", i=2),
+                    MULT,
+                )
                 halves.append(h)
             return halves
 
-        def quantise_hidden(halves):
-            packed = []
-            for h in halves:
-                h_codes = mid.tile([P, HALF], U32, name="h_codes", align_bytes=64)
-                h_scales = mid.tile([P, HALF], U8, name="h_scales", align_bytes=64)
-                nc.vector.quantize_mx(out=h_codes[:].bitcast(FP8X4), scales=h_scales[:], in_=h[:].rearrange("p n t -> p (n t)"))
-                packed.append((h_codes, h_scales))
-            return packed
+        def quantise_hidden(e, half, h):
+            h_codes = placed(work, f"h_codes{e}_{half}", [P, HALF], U32, 24 * KIB + half * 512)
+            h_scales = placed(work, f"h_scales{e}_{half}", [P, HALF], U8, 25 * KIB + half * 128)
+            nc.vector.quantize_mx(out=h_codes[:].bitcast(FP8X4), scales=h_scales[:], in_=h[:])
+            return h_codes, h_scales
+
+        def second_layer_pass(bank, e, m, packed):
+            rows = slice(m * P, (m + 1) * P)
+            nc.tensor.matmul_mx(
+                out=bank,
+                lhsT=w2_codes[e][:, rows].bitcast(FP8X4),
+                lhsT_scale=w2_scales[e][:, rows],
+                rhs=packed[0][:].bitcast(FP8X4),
+                rhs_scale=packed[1][:],
+                start=True,
+                stop=True,
+            )
 
         def second_layer(e, packed):
-            banks = []
-            for half, (h_codes, h_scales) in enumerate(packed):
-                bank = psum.tile([P, N_TILES, HALF], F32, name=f"y_bank{half}")
-                for m in range(N_TILES):
-                    rows = slice(m * P, (m + 1) * P)
-                    nc.tensor.matmul_mx(
-                        out=bank[:, m, :],
-                        lhsT=w2_codes[e][:, rows].bitcast(FP8X4),
-                        lhsT_scale=w2_scales[e][:, rows],
-                        rhs=h_codes[:].bitcast(FP8X4),
-                        rhs_scale=h_scales[:],
-                        start=True,
-                        stop=True,
-                    )
-                banks.append(bank)
-            return banks
+            y = []
+            for half in range(2):
+                bank = psum.tile([P, 2, HALF], F32, name=f"y_bank{half}")
+                for m in range(2):
+                    second_layer_pass(bank[:, m, :], e, m, packed[half])
+                y.append(placed(work, f"y{e}_{half}", [P, 2, HALF], F32, (4 * KIB, 18 * KIB)[half]))
+                nc.scalar.activation(y[half][:], bank[:], COPY)
+            last_bank = psum.tile([P, C], F32, name="y_bank0")
+            for half in range(2):
+                second_layer_pass(last_bank[:, half * HALF : (half + 1) * HALF], e, 2, packed[half])
+            return y, last_bank
 
-        def take_y(y, banks):
-            for half, bank in enumerate(banks):
-                nc.scalar.activation(y[:, :, half * HALF : (half + 1) * HALF], bank[:], COPY)
+        def take_last_rows(e, bank, pool, at):
+            y = placed(pool, f"y{e}_last", [P, C], F32, at)
+            nc.scalar.activation(y[:], bank[:], COPY)
+            return y
 
-        def scatter(e, m, y, a=0, b=C):
-            first, end = e * C + a, e * C + b
+        def scatter(m, values, first, end):
             window = windows[m][:].indirect(offsets[:, first // 16 : end // 16])
-            nc.vector.tensor_tensor(window, y[:, m, a:b], gate_sb[:, first:end], MULT)
+            nc.vector.tensor_tensor(window, values, gate_sb[:, first:end], MULT)
 
-        def finish(m, parts=1):
-            width = T // parts
-            for a in range(0, T, width):
-                cols = slice(a, a + width)
-                nc.vector.tensor_tensor(residual[m][:, cols], windows[m][:, cols], residual[m][:, cols], ADD)
-                nc.sync.dma_start(out[m * P : (m + 1) * P, cols], residual[m][:, cols])
+        def scatter_first_rows(e, y):
+            for half in range(2):
+                for m in range(2):
+                    first = e * C + half * HALF
+                    scatter(m, y[half][:, m, :], first, first + HALF)
 
-        later_loads = [lambda key=key: load_chunk(*key) for key in (("w1", 1, 2), ("w3", 1, 0), ("w3", 1, 1), ("w3", 1, 2))]
-        later_loads.append(load_rest)
+        def finish(m, cuts=(0, T)):
+            for a, b in zip(cuts, cuts[1:]):
+                nc.vector.tensor_tensor(residual[m][:, a:b], windows[m][:, a:b], residual[m][:, a:b], ADD)
+                nc.sync.dma_start(out[m * P : (m + 1) * P, a:b], residual[m][:, a:b])
+
         for s in range(PASSES):
             load_tokens(s)
-            load_chunk("w1", 0, s)
-        for s in range(PASSES):
-            load_chunk("w3", 0, s)
-        load_w2(0, keep, "w2_raw0")
-        nc.sync.dma_start(gate_sb[:], gate[0:P, :])
-        load_chunk("w1", 1, 0)
-        load_chunk("w1", 1, 1)
+        for n, key in enumerate(chunks[0]):
+            load_chunk(key, 48 * KIB + 8 * KIB * n)
 
         for s in range(PASSES):
-            copy_tokens(s, 0, by_vector)
-            copy_tokens(s, T_HALF, by_scalar)
-            if s > 0:
-                gather_words(s - 1)
-                quantise_chunk(("w1", 0, s - 1))
+            copy_tokens(s, 0, by_vector, 4 * KIB * s)
+            copy_tokens(s, T_HALF, by_scalar, 4 * KIB * (s + 1))
             quantise_tokens(s, 0)
             quantise_tokens(s, T_HALF)
-            copy_chunk(("w1", 0, s), (by_scalar, 0, P))
-        copy_chunk(("w3", 0, 0), (by_scalar, 0, P))
-        gather_words(PASSES - 1)
-        quantise_chunk(("w1", 0, PASSES - 1))
+            gather_words(s)
         gather_scales()
-        copy_chunk(("w3", 0, 1), (by_vector, 0, P))
-        quantise_chunk(("w3", 0, 0))
-        copy_chunk(("w3", 0, 2), (by_vector, 0, P // 2), (by_scalar, P // 2, P))
-        quantise_chunk(("w3", 0, 1))
-        quantise_chunk(("w3", 0, 2))
 
-        ys = [mid.tile([P, N_TILES, C], F32, name="y") for e in range(E)]
+        load_chunk(chunks[1][0], 0)
+        load_w2(0, 8 * KIB)
+        gate_sb = placed(loads, "gate_sb", [P, SLOTS], F32, 14 * KIB)
+        nc.sync.dma_start(gate_sb[:], gate[0:P, :])
+        for n in range(1, 5):
+            load_chunk(chunks[1][n], 8 * KIB * (n + 1))
 
-        w1_banks = first_layer("w1", 0)
-        acts = silu_of(w1_banks)
-        packed = quantise_hidden(hidden(acts, first_layer("w3", 0)))
-        prepare_w2(0)
-        y_banks = second_layer(0, packed)
+        w3_0, w3_1, w3_2, w1_0, w1_1, w1_2 = chunks[0]
+        copy_chunk(w3_0, 0, 8 * KIB)
+        load_chunk(chunks[1][5], 48 * KIB)
+        copy_chunk(w3_1, 0, 12 * KIB)
+        quantise_chunk(w3_0)
+        copy_chunk(w3_2, P, 8 * KIB)
+        quantise_chunk(w3_1)
+        quantise_chunk(w3_2)
+        g_banks = linear_branch(0)
+        a_banks = silu_banks()
+        copy_chunk(w1_0, 48, 12 * KIB)
+        quantise_chunk(w1_0)
+        silu_branch_pass(a_banks, 0, 0)
+        copy_chunk(w1_1, 80, 8 * KIB)
+        quantise_chunk(w1_1)
+        silu_branch_pass(a_banks, 0, 1)
+        copy_chunk(w1_2, 80, 8 * KIB)
+        quantise_chunk(w1_2, pieces=H_TILES, at=20 * KIB)
+        silu_branch_pass(a_banks, 0, 2)
+        load_w2(1, 64 * KIB)
+        for m in range(N_TILES):
+            load_residual(m)
 
-        copy_chunk(("w1", 1, 0), (by_scalar, 0, P))
-        take_y(ys[0], y_banks)
-        quantise_chunk(("w1", 1, 0))
-        copy_chunk(("w1", 1, 1), (by_vector, 0, P))
-        scatter(0, 0, ys[0])
-        quantise_chunk(("w1", 1, 1))
-        copy_chunk(("w1", 1, 2), (by_scalar, 0, P))
-        scatter(0, 1, ys[0])
-        quantise_chunk(("w1", 1, 2))
-        w1_banks = first_layer("w1", 1)
-        copy_chunk(("w3", 1, 0), (by_scalar, 0, P))
-        acts = silu_of(w1_banks)
-        scatter(0, 2, ys[0])
-        quantise_chunk(("w3", 1, 0))
-        copy_chunk(("w3", 1, 1), (by_vector, 0, P))
-        quantise_chunk(("w3", 1, 1))
-        copy_chunk(("w3", 1, 2), (by_scalar, 0, 48), (by_vector, 48, P))
-        quantise_chunk(("w3", 1, 2), pieces=H_TILES)
-        packed = quantise_hidden(hidden(acts, first_layer("w3", 1)))
-        prepare_w2(1)
-        y_banks = second_layer(1, packed)
-        take_y(ys[1], y_banks)
-
+        w3_0, w3_1, w3_2, w1_0, w1_1, w1_2 = chunks[1]
+        copy_chunk(w3_0, P, 8 * KIB)
+        acts = silu_of(0, a_banks)
+        copy_w2(0, by_scalar, 20 * KIB)
+        halves = hidden(0, acts, g_banks)
+        packed = []
         for half in range(2):
-            for m in range(N_TILES - 1):
-                scatter(1, m, ys[1], half * HALF, (half + 1) * HALF)
-        last = N_TILES - 1
-        scatter(1, last, ys[1], 0, HALF)
+            packed.append(quantise_hidden(0, half, halves[half]))
+            quantise_w2(0, half)
+        y, last_bank = second_layer(0, packed)
+        quantise_chunk(w3_0, at=16 * KIB)
+
+        copy_chunk(w3_1, 0, 12 * KIB)
+        scatter_first_rows(0, y)
+        copy_chunk(w3_2, 80, 4 * KIB)
+        quantise_chunk(w3_1)
+        quantise_chunk(w3_2)
+        g_banks = linear_branch(1)
+        a_banks = silu_banks()
+        copy_chunk(w1_0, 0, 24 * KIB)
+        copy_chunk(w1_1, 80, 4 * KIB)
+        quantise_chunk(w1_0)
+        silu_branch_pass(a_banks, 1, 0)
+        quantise_chunk(w1_1)
+        silu_branch_pass(a_banks, 1, 1)
+        copy_chunk(w1_2, 80, 4 * KIB)
+        y_last = take_last_rows(0, last_bank, loads, 48 * KIB)
+        quantise_chunk(w1_2, pieces=H_TILES, at=20 * KIB)
+        silu_branch_pass(a_banks, 1, 2)
+        scatter(2, y_last[:], 0, C)
+        acts = silu_of(1, a_banks)
+        copy_w2(1, by_scalar, 20 * KIB)
+        halves = hidden(1, acts, g_banks)
+        packed = []
+        for half in range(2):
+            packed.append(quantise_hidden(1, half, halves[half]))
+            quantise_w2(1, half)
+        y, last_bank = second_layer(1, packed)
+
+        scatter_first_rows(1, y)
+        y_last = take_last_rows(1, last_bank, work, 18 * KIB)
         finish(0)
-        scatter(1, last, ys[1], HALF, C)
         finish(1)
-        finish(last, parts=2)
+        scatter(2, y_last[:], C, SLOTS)
+        finish(2, cuts=(0, 512, 768, T))

@@ -1,6 +1,7 @@
 from contextlib import ExitStack
 
 import concourse.mybir as mybir
+from concourse.masks import make_identity
 
 K, T, E, C, H, N = 1536, 1024, 2, 256, 512, 384
 
@@ -55,6 +56,8 @@ def tile_moe_res_glu_silu_kernel(tc, xT, xr, w1, w3, w2, gate, offs, out):
         windows = [keep.tile([P, T], F32, name=f"window{m}") for m in range(N_TILES)]
         for m in range(N_TILES):
             nc.gpsimd.memset(windows[m][:], 0.0)
+        identity = keep.tile([P, P], F32, name="identity")
+        make_identity(nc, identity[:])
         slot_words = [keep.tile([P, SLOTS], U32, name=f"slot_words{s}", align_bytes=64) for s in range(PASSES)]
         slot_scales = keep.tile([P, SLOTS], U8, name="slot_scales", align_bytes=64)
 
@@ -114,18 +117,17 @@ def tile_moe_res_glu_silu_kernel(tc, xT, xr, w1, w3, w2, gate, offs, out):
 
         W2_CUTS = ((0, 256), (256, N))
 
-        def copy_w2(e, copy, at):
-            grouped["w2", e] = placed(work, f"w2_grouped{e}", [P, N * PACK], BF16, at)
-            w2_codes[e] = placed(work, f"w2_codes{e}", [P, N], U32, 12 * KIB)
-            w2_scales[e] = keep.tile([P, N], U8, name=f"w2_scales{e}", align_bytes=64)
-            for a, b in W2_CUTS:
-                src = w2_raw[e][:, :, a:b].rearrange("p j (c i) -> p c j i", i=RUN)
-                copy(grouped["w2", e][:, PACK * a : PACK * b].rearrange("p (c i j) -> p c j i", i=RUN, j=PACK), src)
+        def copy_w2(e, part, copy, at):
+            a, b = W2_CUTS[part]
+            grouped["w2", e, part] = placed(work, f"w2_grouped{e}_{part}", [P, (b - a) * PACK], BF16, at)
+            src = w2_raw[e][:, :, a:b].rearrange("p j (c i) -> p c j i", i=RUN)
+            copy(grouped["w2", e, part][:].rearrange("p (c i j) -> p c j i", i=RUN, j=PACK), src)
 
         def quantise_w2(e, part):
             a, b = W2_CUTS[part]
-            source = grouped["w2", e][:, PACK * a : PACK * b]
-            nc.vector.quantize_mx(out=w2_codes[e][:, a:b].bitcast(FP8X4), scales=w2_scales[e][:, a:b], in_=source)
+            w2_codes[e, part] = placed(work, f"w2_codes{e}_{part}", [P, b - a], U32, (12 * KIB, 19 * KIB)[part])
+            w2_scales[e, part] = keep.tile([P, b - a], U8, name=f"w2_scales{e}_{part}", align_bytes=64)
+            nc.vector.quantize_mx(out=w2_codes[e, part][:].bitcast(FP8X4), scales=w2_scales[e, part][:], in_=grouped["w2", e, part][:])
 
         def gather_words(s):
             nc.vector.tensor_copy(slot_words[s][:], x_words[s][:].indirect(offsets[:]))
@@ -133,7 +135,7 @@ def tile_moe_res_glu_silu_kernel(tc, xT, xr, w1, w3, w2, gate, offs, out):
         def gather_scales():
             nc.vector.tensor_copy(slot_scales[:], x_scales[:].indirect(offsets[:]))
 
-        def first_layer_pass(bank, key, t, slots):
+        def first_layer_pass(bank, key, t, slots, first=True, last=True):
             s = key[2]
             channels = slice(t * P, (t + 1) * P)
             nc.tensor.matmul_mx(
@@ -142,19 +144,17 @@ def tile_moe_res_glu_silu_kernel(tc, xT, xr, w1, w3, w2, gate, offs, out):
                 lhsT_scale=scales[key][:, channels],
                 rhs=slot_words[s][:, slots].bitcast(FP8X4),
                 rhs_scale=slot_scales[4 * s : P, slots],
-                start=(s == 0),
-                stop=(s == PASSES - 1),
+                start=(s == 0 and first),
+                stop=(s == PASSES - 1 and last),
             )
 
         def linear_branch(e):
-            banks = []
-            for half in range(2):
-                bank = psum.tile([P, H_TILES, HALF], F32, name=f"g_bank{half}")
-                slots = slice(e * C + half * HALF, e * C + (half + 1) * HALF)
-                for t in range(H_TILES):
-                    for s in range(PASSES):
-                        first_layer_pass(bank[:, t, :], ("w3", e, s), t, slots)
-                banks.append(bank)
+            banks = [psum.tile([P, H_TILES, HALF], F32, name=f"g_bank{half}") for half in range(2)]
+            for s in range(PASSES):
+                for half in range(2):
+                    slots = slice(e * C + half * HALF, e * C + (half + 1) * HALF)
+                    for t in range(H_TILES):
+                        first_layer_pass(banks[half][:, t, :], ("w3", e, s), t, slots, t == 0, t == H_TILES - 1)
             return banks
 
         def silu_banks():
@@ -166,8 +166,8 @@ def tile_moe_res_glu_silu_kernel(tc, xT, xr, w1, w3, w2, gate, offs, out):
 
         def silu_of(e, banks):
             acts = [placed(work, f"act{e}_{half}", [P, H_TILES, HALF], F32, 2 * KIB * (1 - half)) for half in range(2)]
-            for t in range(H_TILES):
-                for half in range(2):
+            for half in range(2):
+                for t in range(H_TILES):
                     nc.scalar.activation(acts[half][:, t, :], banks[t][:, half * HALF : (half + 1) * HALF], SILU)
             return acts
 
@@ -191,11 +191,12 @@ def tile_moe_res_glu_silu_kernel(tc, xT, xr, w1, w3, w2, gate, offs, out):
             return h_codes, h_scales
 
         def second_layer_pass(bank, e, m, packed):
-            rows = slice(m * P, (m + 1) * P)
+            part = m // 2
+            rows = slice((m % 2) * P, (m % 2 + 1) * P)
             nc.tensor.matmul_mx(
                 out=bank,
-                lhsT=w2_codes[e][:, rows].bitcast(FP8X4),
-                lhsT_scale=w2_scales[e][:, rows],
+                lhsT=w2_codes[e, part][:, rows].bitcast(FP8X4),
+                lhsT_scale=w2_scales[e, part][:, rows],
                 rhs=packed[0][:].bitcast(FP8X4),
                 rhs_scale=packed[1][:],
                 start=True,
@@ -208,16 +209,16 @@ def tile_moe_res_glu_silu_kernel(tc, xT, xr, w1, w3, w2, gate, offs, out):
                 bank = psum.tile([P, 2, HALF], F32, name=f"y_bank{half}")
                 for m in range(2):
                     second_layer_pass(bank[:, m, :], e, m, packed[half])
-                y.append(placed(work, f"y{e}_{half}", [P, 2, HALF], F32, (4 * KIB, 18 * KIB)[half]))
+                y.append(placed(work, f"y{e}_{half}", [P, 2, HALF], F32, (4 * KIB, 26 * KIB)[half]))
                 nc.scalar.activation(y[half][:], bank[:], COPY)
-            last_bank = psum.tile([P, C], F32, name="y_bank0")
+            last_bank = psum.tile([P, C], F32, name=("y_bank1", "g_bank1")[e])
             for half in range(2):
                 second_layer_pass(last_bank[:, half * HALF : (half + 1) * HALF], e, 2, packed[half])
             return y, last_bank
 
-        def take_last_rows(e, bank, pool, at):
-            y = placed(pool, f"y{e}_last", [P, C], F32, at)
-            nc.scalar.activation(y[:], bank[:], COPY)
+        def take_last_rows(e, bank, a, b, pool, at):
+            y = placed(pool, f"y{e}_last{a}", [P, b - a], F32, at)
+            nc.scalar.activation(y[:], bank[:, a:b], COPY)
             return y
 
         def scatter(m, values, first, end):
@@ -226,7 +227,7 @@ def tile_moe_res_glu_silu_kernel(tc, xT, xr, w1, w3, w2, gate, offs, out):
 
         def scatter_first_rows(e, y):
             for half in range(2):
-                for m in range(2):
+                for m in (1, 0):
                     first = e * C + half * HALF
                     scatter(m, y[half][:, m, :], first, first + HALF)
 
@@ -234,6 +235,30 @@ def tile_moe_res_glu_silu_kernel(tc, xT, xr, w1, w3, w2, gate, offs, out):
             for a, b in zip(cuts, cuts[1:]):
                 nc.vector.tensor_tensor(residual[m][:, a:b], windows[m][:, a:b], residual[m][:, a:b], ADD)
                 nc.sync.dma_start(out[m * P : (m + 1) * P, a:b], residual[m][:, a:b])
+
+        def turn(bank, source, first, start, stop):
+            for b in range(4):
+                block = source[:, first + b * P : first + (b + 1) * P]
+                nc.tensor.matmul(bank[:, b * P : (b + 1) * P], block, identity[:], start=start and b == 0, stop=stop and b == 3, is_transpose=True)
+
+        def open_sums(m):
+            banks = [psum.tile([P, T_HALF], F32, name=f"a_bank{part}") for part in range(2)]
+            for part in range(2):
+                turn(banks[part], residual[m], part * T_HALF, True, False)
+            return banks
+
+        def finish_on_tensor(m, banks):
+            turned = []
+            for part in range(2):
+                turn(banks[part], windows[m], part * T_HALF, False, True)
+                turned.append(keep.tile([P, T_HALF], F32, name=f"turned{part}"))
+                nc.scalar.activation(turned[part][:], banks[part][:], COPY)
+            for part in range(2):
+                bank = psum.tile([P, T_HALF], F32, name=f"a_bank{2 + part}")
+                turn(bank, turned[part], 0, True, True)
+                result = keep.tile([P, T_HALF], F32, name=f"result{part}")
+                nc.scalar.activation(result[:], bank[:], COPY)
+                nc.scalar.dma_start(out[m * P : (m + 1) * P, part * T_HALF : (part + 1) * T_HALF], result[:])
 
         for s in range(PASSES):
             load_tokens(s)
@@ -248,8 +273,8 @@ def tile_moe_res_glu_silu_kernel(tc, xT, xr, w1, w3, w2, gate, offs, out):
             gather_words(s)
         gather_scales()
 
-        load_chunk(chunks[1][0], 0)
         load_w2(0, 8 * KIB)
+        load_chunk(chunks[1][0], 0)
         gate_sb = placed(loads, "gate_sb", [P, SLOTS], F32, 14 * KIB)
         nc.sync.dma_start(gate_sb[:], gate[0:P, :])
         for n in range(1, 5):
@@ -279,47 +304,50 @@ def tile_moe_res_glu_silu_kernel(tc, xT, xr, w1, w3, w2, gate, offs, out):
             load_residual(m)
 
         w3_0, w3_1, w3_2, w1_0, w1_1, w1_2 = chunks[1]
-        copy_chunk(w3_0, P, 8 * KIB)
+        for part in range(2):
+            copy_w2(0, part, by_vector, 8 * KIB + 2 * KIB * part)
+        for part in range(2):
+            quantise_w2(0, part)
         acts = silu_of(0, a_banks)
-        copy_w2(0, by_scalar, 20 * KIB)
+        copy_chunk(w3_0, 0, 20 * KIB)
         halves = hidden(0, acts, g_banks)
-        packed = []
-        for half in range(2):
-            packed.append(quantise_hidden(0, half, halves[half]))
-            quantise_w2(0, half)
+        packed = [quantise_hidden(0, half, halves[half]) for half in range(2)]
         y, last_bank = second_layer(0, packed)
         quantise_chunk(w3_0, at=16 * KIB)
 
         copy_chunk(w3_1, 0, 12 * KIB)
         scatter_first_rows(0, y)
-        copy_chunk(w3_2, 80, 4 * KIB)
+        copy_chunk(w3_2, 0, 4 * KIB)
+        y_last = take_last_rows(0, last_bank, 0, HALF, loads, 24 * KIB)
         quantise_chunk(w3_1)
         quantise_chunk(w3_2)
         g_banks = linear_branch(1)
+        scatter(2, y_last[:], 0, HALF)
         a_banks = silu_banks()
-        copy_chunk(w1_0, 0, 24 * KIB)
-        copy_chunk(w1_1, 80, 4 * KIB)
+        copy_chunk(w1_0, 32, 24 * KIB)
+        copy_chunk(w1_1, 56, 4 * KIB)
         quantise_chunk(w1_0)
         silu_branch_pass(a_banks, 1, 0)
         quantise_chunk(w1_1)
         silu_branch_pass(a_banks, 1, 1)
         copy_chunk(w1_2, 80, 4 * KIB)
-        y_last = take_last_rows(0, last_bank, loads, 48 * KIB)
         quantise_chunk(w1_2, pieces=H_TILES, at=20 * KIB)
         silu_branch_pass(a_banks, 1, 2)
-        scatter(2, y_last[:], 0, C)
+        copy_w2(1, 0, by_vector, 4 * KIB)
+        quantise_w2(1, 0)
         acts = silu_of(1, a_banks)
-        copy_w2(1, by_scalar, 20 * KIB)
+        copy_w2(1, 1, by_scalar, 20 * KIB)
         halves = hidden(1, acts, g_banks)
-        packed = []
-        for half in range(2):
-            packed.append(quantise_hidden(1, half, halves[half]))
-            quantise_w2(1, half)
+        y_last = take_last_rows(0, last_bank, HALF, C, work, 0)
+        packed = [quantise_hidden(1, half, halves[half]) for half in range(2)]
+        quantise_w2(1, 1)
+        scatter(2, y_last[:], HALF, C)
         y, last_bank = second_layer(1, packed)
+        sums = open_sums(1)
 
         scatter_first_rows(1, y)
-        y_last = take_last_rows(1, last_bank, work, 18 * KIB)
+        y_last = take_last_rows(1, last_bank, 0, C, work, 26 * KIB)
+        finish_on_tensor(1, sums)
         finish(0)
-        finish(1)
         scatter(2, y_last[:], C, SLOTS)
         finish(2, cuts=(0, 512, 768, T))

@@ -43,7 +43,6 @@ def tile_moe_res_glu_silu_kernel(tc, xT, xr, w1, w3, w2, gate, offs, out):
             return pool.tile(shape, dtype, name=name, offset=at, align_bytes=64)
 
         offsets = keep.tile([P, SLOTS // 16], U16, name="offsets")
-        nc.sync.dma_start(offsets[:], offs)
 
         warm = keep.tile([P, 1], F32, name="warm")
         nc.gpsimd.memset(warm[:], 0.0)
@@ -65,7 +64,7 @@ def tile_moe_res_glu_silu_kernel(tc, xT, xr, w1, w3, w2, gate, offs, out):
         chunks = [[(name, e, s) for name in ("w3", "w1") for s in range(PASSES)] for e in range(E)]
         raws, grouped, codes, scales = {}, {}, {}, {}
         w2_raw, w2_codes, w2_scales = {}, {}, {}
-        residual = []
+        residual, gates = [], []
 
         def load_tokens(s):
             raws["x", s] = placed(loads, f"tokens{s}", [P, PACK, T], F32, 16 * KIB * s)
@@ -80,6 +79,10 @@ def tile_moe_res_glu_silu_kernel(tc, xT, xr, w1, w3, w2, gate, offs, out):
         def load_w2(e, at):
             w2_raw[e] = placed(loads, f"w2_raw{e}", [P, PACK, N], F32, at)
             nc.sync.dma_start(w2_raw[e][:], w2[e].rearrange("(p j) n -> p j n", j=PACK))
+
+        def load_gate(e, at):
+            gates.append(placed(loads, f"gate{e}", [P, C], F32, at))
+            nc.sync.dma_start(gates[e][:], gate[0:P, e * C : (e + 1) * C])
 
         def load_residual(m):
             residual.append(placed(loads, f"residual{m}", [P, T], F32, 8 * KIB * (9 + m)))
@@ -223,7 +226,8 @@ def tile_moe_res_glu_silu_kernel(tc, xT, xr, w1, w3, w2, gate, offs, out):
 
         def scatter(m, values, first, end):
             window = windows[m][:].indirect(offsets[:, first // 16 : end // 16])
-            nc.vector.tensor_tensor(window, values, gate_sb[:, first:end], MULT)
+            e = first // C
+            nc.vector.tensor_tensor(window, values, gates[e][:, first - e * C : end - e * C], MULT)
 
         def scatter_first_rows(e, y):
             for half in range(2):
@@ -242,7 +246,7 @@ def tile_moe_res_glu_silu_kernel(tc, xT, xr, w1, w3, w2, gate, offs, out):
                 nc.tensor.matmul(bank[:, b * P : (b + 1) * P], block, identity[:], start=start and b == 0, stop=stop and b == 3, is_transpose=True)
 
         def open_sums(m):
-            banks = [psum.tile([P, T_HALF], F32, name=f"a_bank{part}") for part in range(2)]
+            banks = [psum.tile([P, T_HALF], F32, name=f"y_bank{part}") for part in range(2)]
             for part in range(2):
                 turn(banks[part], residual[m], part * T_HALF, True, False)
             return banks
@@ -254,7 +258,7 @@ def tile_moe_res_glu_silu_kernel(tc, xT, xr, w1, w3, w2, gate, offs, out):
                 turned.append(keep.tile([P, T_HALF], F32, name=f"turned{part}"))
                 nc.scalar.activation(turned[part][:], banks[part][:], COPY)
             for part in range(2):
-                bank = psum.tile([P, T_HALF], F32, name=f"a_bank{2 + part}")
+                bank = psum.tile([P, T_HALF], F32, name=f"a_bank{part}")
                 turn(bank, turned[part], 0, True, True)
                 result = keep.tile([P, T_HALF], F32, name=f"result{part}")
                 nc.scalar.activation(result[:], bank[:], COPY)
@@ -262,6 +266,8 @@ def tile_moe_res_glu_silu_kernel(tc, xT, xr, w1, w3, w2, gate, offs, out):
 
         for s in range(PASSES):
             load_tokens(s)
+            if s == 0:
+                nc.sync.dma_start(offsets[:], offs)
         for n, key in enumerate(chunks[0]):
             load_chunk(key, 48 * KIB + 8 * KIB * n)
 
@@ -275,8 +281,7 @@ def tile_moe_res_glu_silu_kernel(tc, xT, xr, w1, w3, w2, gate, offs, out):
 
         load_w2(0, 8 * KIB)
         load_chunk(chunks[1][0], 0)
-        gate_sb = placed(loads, "gate_sb", [P, SLOTS], F32, 14 * KIB)
-        nc.sync.dma_start(gate_sb[:], gate[0:P, :])
+        load_gate(0, 14 * KIB)
         for n in range(1, 5):
             load_chunk(chunks[1][n], 8 * KIB * (n + 1))
 
@@ -300,6 +305,7 @@ def tile_moe_res_glu_silu_kernel(tc, xT, xr, w1, w3, w2, gate, offs, out):
         quantise_chunk(w1_2, pieces=H_TILES, at=20 * KIB)
         silu_branch_pass(a_banks, 0, 2)
         load_w2(1, 64 * KIB)
+        load_gate(1, 70 * KIB)
         for m in range(N_TILES):
             load_residual(m)
 
@@ -346,8 +352,11 @@ def tile_moe_res_glu_silu_kernel(tc, xT, xr, w1, w3, w2, gate, offs, out):
         sums = open_sums(1)
 
         scatter_first_rows(1, y)
-        y_last = take_last_rows(1, last_bank, 0, C, work, 26 * KIB)
+        y_last = take_last_rows(1, last_bank, 0, HALF, work, 4 * KIB)
+        y_rest = take_last_rows(1, last_bank, HALF, C, work, 26 * KIB)
         finish_on_tensor(1, sums)
-        finish(0)
-        scatter(2, y_last[:], C, SLOTS)
+        scatter(2, y_last[:], C, C + HALF)
+        finish(0, cuts=(0, 768))
+        scatter(2, y_rest[:], C + HALF, SLOTS)
+        finish(0, cuts=(768, T))
         finish(2, cuts=(0, 512, 768, T))

@@ -44,11 +44,6 @@ def tile_moe_res_glu_silu_kernel(tc, xT, xr, w1, w3, w2, gate, offs, out):
 
         offsets = keep.tile([P, SLOTS // 16], U16, name="offsets")
 
-        warm = keep.tile([P, 1], F32, name="warm")
-        nc.gpsimd.memset(warm[:], 0.0)
-        warm_out = keep.tile([P, 1], F32, name="warm_out")
-        nc.scalar.activation(warm_out[:], warm[:], SILU)
-
         x_words = [keep.tile([P, T], U32, name=f"x_words{s}", align_bytes=64) for s in range(PASSES)]
         x_scales = keep.tile([P, T], U8, name="x_scales", align_bytes=64)
         nc.gpsimd.memset(x_scales[:], 0)
@@ -161,29 +156,25 @@ def tile_moe_res_glu_silu_kernel(tc, xT, xr, w1, w3, w2, gate, offs, out):
             return banks
 
         def silu_banks():
-            return [psum.tile([P, C], F32, name=f"a_bank{t}") for t in range(H_TILES)]
+            return [psum.tile([P, H_TILES, HALF], F32, name=f"a_bank{half}") for half in range(2)]
 
         def silu_branch_pass(banks, e, s):
             for t in range(H_TILES):
-                first_layer_pass(banks[t][:], ("w1", e, s), t, slice(e * C, (e + 1) * C))
+                for half in range(2):
+                    slots = slice(e * C + half * HALF, e * C + (half + 1) * HALF)
+                    first_layer_pass(banks[half][:, t, :], ("w1", e, s), t, slots, t == 0, t == H_TILES - 1)
 
         def silu_of(e, banks):
-            acts = [placed(work, f"act{e}_{half}", [P, H_TILES, HALF], F32, 2 * KIB * (1 - half)) for half in range(2)]
+            acts = [placed(work, f"act{e}_{half}", [P, HALF, H_TILES], F32, 2 * KIB * (1 - half)) for half in range(2)]
             for half in range(2):
-                for t in range(H_TILES):
-                    nc.scalar.activation(acts[half][:, t, :], banks[t][:, half * HALF : (half + 1) * HALF], SILU)
+                nc.scalar.activation(acts[half][:], banks[half][:].rearrange("p t n -> p n t"), SILU)
             return acts
 
         def hidden(e, acts, banks):
             halves = []
             for half in range(2):
                 h = placed(work, f"h{e}_{half}", [P, HALF * H_TILES], BF16, 16 * KIB + half * KIB)
-                nc.vector.tensor_tensor(
-                    h[:].rearrange("p (c i t) -> p c t i", i=2, t=H_TILES),
-                    banks[half][:].rearrange("p t (c i) -> p c t i", i=2),
-                    acts[half][:].rearrange("p t (c i) -> p c t i", i=2),
-                    MULT,
-                )
+                nc.vector.tensor_tensor(h[:].rearrange("p (n t) -> p n t", t=H_TILES), banks[half][:].rearrange("p t n -> p n t"), acts[half][:], MULT)
                 halves.append(h)
             return halves
 

@@ -24,7 +24,21 @@ SLOTS = E * C
 HALF = C // 2
 RUN = 4
 T_HALF = T // 2
+W2_PARTS = ((0, 256), (256, N))
 KIB = 1024
+
+TOKENS_AT = 0
+CHUNKS_AT = 48 * KIB
+TOKENS_BYTES, CHUNK_BYTES = 16 * KIB, 8 * KIB
+STAGE = [4 * KIB * n for n in range(4)]
+SILU_AT = (2 * KIB, 0)
+H_AT = 16 * KIB
+Y_REST_AT = 18 * KIB
+W2_CODES_AT = (STAGE[3], 19 * KIB)
+LAST_CODES_AT = 20 * KIB
+H_CODES_AT = 24 * KIB
+H_SCALES_AT = 25 * KIB
+Y_AT = (STAGE[1], 26 * KIB)
 
 FLOPS = 2 * SLOTS * (2 * K * H + H * N)
 BYTES = 4 * (K * T + 2 * N * T + E * (2 * K * H + H * N) + SLOTS) + 2 * P * SLOTS // 16
@@ -62,7 +76,7 @@ def tile_moe_res_glu_silu_kernel(tc, xT, xr, w1, w3, w2, gate, offs, out):
         residual, gates = [], []
 
         def load_tokens(s):
-            raws["x", s] = placed(loads, f"tokens{s}", [P, PACK, T], F32, 16 * KIB * s)
+            raws["x", s] = placed(loads, f"tokens{s}", [P, PACK, T], F32, TOKENS_AT + TOKENS_BYTES * s)
             nc.sync.dma_start(raws["x", s][:], xT[s * K_PASS : (s + 1) * K_PASS, :].rearrange("(p j) t -> p j t", j=PACK))
 
         def load_chunk(key, at):
@@ -79,8 +93,8 @@ def tile_moe_res_glu_silu_kernel(tc, xT, xr, w1, w3, w2, gate, offs, out):
             gates.append(placed(loads, f"gate{e}", [P, C], F32, at))
             nc.sync.dma_start(gates[e][:], gate[0:P, e * C : (e + 1) * C])
 
-        def load_residual(m):
-            residual.append(placed(loads, f"residual{m}", [P, T], F32, 8 * KIB * (9 + m)))
+        def load_residual(m, at):
+            residual.append(placed(loads, f"residual{m}", [P, T], F32, at))
             nc.sync.dma_start(residual[m][:], xr[m * P : (m + 1) * P, :])
 
         def copy_tokens(s, first, copy, at):
@@ -113,17 +127,15 @@ def tile_moe_res_glu_silu_kernel(tc, xT, xr, w1, w3, w2, gate, offs, out):
                 source = grouped[key][:, PACK * a : PACK * (a + width)]
                 nc.vector.quantize_mx(out=codes[key][:, cols].bitcast(FP8X4), scales=scales[key][:, cols], in_=source)
 
-        W2_CUTS = ((0, 256), (256, N))
-
         def copy_w2(e, part, copy, at):
-            a, b = W2_CUTS[part]
+            a, b = W2_PARTS[part]
             grouped["w2", e, part] = placed(work, f"w2_grouped{e}_{part}", [P, (b - a) * PACK], BF16, at)
             src = w2_raw[e][:, :, a:b].rearrange("p j (c i) -> p c j i", i=RUN)
             copy(grouped["w2", e, part][:].rearrange("p (c i j) -> p c j i", i=RUN, j=PACK), src)
 
         def quantise_w2(e, part):
-            a, b = W2_CUTS[part]
-            w2_codes[e, part] = placed(work, f"w2_codes{e}_{part}", [P, b - a], U32, (12 * KIB, 19 * KIB)[part])
+            a, b = W2_PARTS[part]
+            w2_codes[e, part] = placed(work, f"w2_codes{e}_{part}", [P, b - a], U32, W2_CODES_AT[part])
             w2_scales[e, part] = keep.tile([P, b - a], U8, name=f"w2_scales{e}_{part}", align_bytes=64)
             nc.vector.quantize_mx(out=w2_codes[e, part][:].bitcast(FP8X4), scales=w2_scales[e, part][:], in_=grouped["w2", e, part][:])
 
@@ -133,39 +145,38 @@ def tile_moe_res_glu_silu_kernel(tc, xT, xr, w1, w3, w2, gate, offs, out):
         def gather_scales():
             nc.vector.tensor_copy(slot_scales[:], x_scales[:].indirect(offsets[:]))
 
-        def first_layer_pass(bank, key, t, slots, first=True, last=True):
-            s = key[2]
+        def first_layer_pass(banks, key, t, half):
+            e, s = key[1:]
             channels = slice(t * P, (t + 1) * P)
+            slots = slice(e * C + half * HALF, e * C + (half + 1) * HALF)
             nc.tensor.matmul_mx(
-                out=bank,
+                out=banks[half][:, t, :],
                 lhsT=codes[key][:, channels].bitcast(FP8X4),
                 lhsT_scale=scales[key][:, channels],
                 rhs=slot_words[s][:, slots].bitcast(FP8X4),
                 rhs_scale=slot_scales[4 * s : P, slots],
-                start=(s == 0 and first),
-                stop=(s == PASSES - 1 and last),
+                start=(s == 0 and t == 0),
+                stop=(s == PASSES - 1 and t == H_TILES - 1),
             )
 
-        def linear_branch(e):
-            banks = [psum.tile([P, H_TILES, HALF], F32, name=f"g_bank{half}") for half in range(2)]
+        def first_layer_banks(name):
+            return [psum.tile([P, H_TILES, HALF], F32, name=f"{name}_bank{half}") for half in range(2)]
+
+        def w3_passes(e):
+            banks = first_layer_banks("g")
             for s in range(PASSES):
                 for half in range(2):
-                    slots = slice(e * C + half * HALF, e * C + (half + 1) * HALF)
                     for t in range(H_TILES):
-                        first_layer_pass(banks[half][:, t, :], ("w3", e, s), t, slots, t == 0, t == H_TILES - 1)
+                        first_layer_pass(banks, ("w3", e, s), t, half)
             return banks
 
-        def silu_banks():
-            return [psum.tile([P, H_TILES, HALF], F32, name=f"a_bank{half}") for half in range(2)]
-
-        def silu_branch_pass(banks, e, s):
+        def w1_pass(banks, key):
             for t in range(H_TILES):
                 for half in range(2):
-                    slots = slice(e * C + half * HALF, e * C + (half + 1) * HALF)
-                    first_layer_pass(banks[half][:, t, :], ("w1", e, s), t, slots, t == 0, t == H_TILES - 1)
+                    first_layer_pass(banks, key, t, half)
 
         def silu_of(e, banks):
-            acts = [placed(work, f"act{e}_{half}", [P, HALF, H_TILES], F32, 2 * KIB * (1 - half)) for half in range(2)]
+            acts = [placed(work, f"act{e}_{half}", [P, HALF, H_TILES], F32, SILU_AT[half]) for half in range(2)]
             for half in range(2):
                 nc.scalar.activation(acts[half][:], banks[half][:].rearrange("p t n -> p n t"), SILU)
             return acts
@@ -173,14 +184,14 @@ def tile_moe_res_glu_silu_kernel(tc, xT, xr, w1, w3, w2, gate, offs, out):
         def hidden(e, acts, banks):
             halves = []
             for half in range(2):
-                h = placed(work, f"h{e}_{half}", [P, HALF * H_TILES], BF16, 16 * KIB + half * KIB)
+                h = placed(work, f"h{e}_{half}", [P, HALF * H_TILES], BF16, H_AT + half * KIB)
                 nc.vector.tensor_tensor(h[:].rearrange("p (n t) -> p n t", t=H_TILES), banks[half][:].rearrange("p t n -> p n t"), acts[half][:], MULT)
                 halves.append(h)
             return halves
 
         def quantise_hidden(e, half, h):
-            h_codes = placed(work, f"h_codes{e}_{half}", [P, HALF], U32, 24 * KIB + half * 512)
-            h_scales = placed(work, f"h_scales{e}_{half}", [P, HALF], U8, 25 * KIB + half * 128)
+            h_codes = placed(work, f"h_codes{e}_{half}", [P, HALF], U32, H_CODES_AT + half * 4 * HALF)
+            h_scales = placed(work, f"h_scales{e}_{half}", [P, HALF], U8, H_SCALES_AT + half * HALF)
             nc.vector.quantize_mx(out=h_codes[:].bitcast(FP8X4), scales=h_scales[:], in_=h[:])
             return h_codes, h_scales
 
@@ -197,44 +208,47 @@ def tile_moe_res_glu_silu_kernel(tc, xT, xr, w1, w3, w2, gate, offs, out):
                 stop=True,
             )
 
-        def second_layer(e, packed):
+        def scalar_take(dst, bank):
+            nc.scalar.activation(dst, bank, COPY)
+
+        def second_layer(e, packed, takes, rest_name):
             y = []
             for half in range(2):
                 bank = psum.tile([P, 2, HALF], F32, name=f"y_bank{half}")
                 for m in range(2):
                     second_layer_pass(bank[:, m, :], e, m, packed[half])
-                y.append(placed(work, f"y{e}_{half}", [P, 2, HALF], F32, (4 * KIB, 26 * KIB)[half]))
-                nc.scalar.activation(y[half][:], bank[:], COPY)
-            last_bank = psum.tile([P, C], F32, name=("y_bank1", "g_bank1")[e])
+                y.append(placed(work, f"y{e}_{half}", [P, 2, HALF], F32, Y_AT[half]))
+                takes[half](y[half][:], bank[:])
+            rest_bank = psum.tile([P, C], F32, name=rest_name)
             for half in range(2):
-                second_layer_pass(last_bank[:, half * HALF : (half + 1) * HALF], e, 2, packed[half])
-            return y, last_bank
+                second_layer_pass(rest_bank[:, half * HALF : (half + 1) * HALF], e, 2, packed[half])
+            return y, rest_bank
 
-        def take_last_rows(e, bank, a, b, pool, at):
-            y = placed(pool, f"y{e}_last{a}", [P, b - a], F32, at)
-            nc.scalar.activation(y[:], bank[:, a:b], COPY)
-            return y
+        def take_rest(e, half, bank, at):
+            rest = placed(work, f"y{e}_last{half * HALF}", [P, HALF], F32, at)
+            scalar_take(rest[:], bank[:, half * HALF : (half + 1) * HALF])
+            return rest
 
-        def scatter(m, values, first, end):
-            window = windows[m][:].indirect(offsets[:, first // 16 : end // 16])
-            e = first // C
-            nc.vector.tensor_tensor(window, values, gates[e][:, first - e * C : end - e * C], MULT)
+        def scatter(m, e, half, values):
+            first = e * C + half * HALF
+            window = windows[m][:].indirect(offsets[:, first // 16 : (first + HALF) // 16])
+            nc.vector.tensor_tensor(window, values, gates[e][:, half * HALF : (half + 1) * HALF], MULT)
 
         def scatter_first_rows(e, y):
             for half in range(2):
                 for m in (1, 0):
-                    first = e * C + half * HALF
-                    scatter(m, y[half][:, m, :], first, first + HALF)
+                    scatter(m, e, half, y[half][:, m, :])
 
-        def finish(m, cuts=(0, T)):
+        def finish(m, cuts):
             for a, b in zip(cuts, cuts[1:]):
                 nc.vector.tensor_tensor(residual[m][:, a:b], windows[m][:, a:b], residual[m][:, a:b], ADD)
                 nc.sync.dma_start(out[m * P : (m + 1) * P, a:b], residual[m][:, a:b])
 
         def turn(bank, source, first, start, stop):
-            for b in range(4):
+            blocks = T_HALF // P
+            for b in range(blocks):
                 block = source[:, first + b * P : first + (b + 1) * P]
-                nc.tensor.matmul(bank[:, b * P : (b + 1) * P], block, identity[:], start=start and b == 0, stop=stop and b == 3, is_transpose=True)
+                nc.tensor.matmul(bank[:, b * P : (b + 1) * P], block, identity[:], start=start and b == 0, stop=stop and b == blocks - 1, is_transpose=True)
 
         def open_sums(m):
             banks = [psum.tile([P, T_HALF], F32, name=f"y_bank{part}") for part in range(2)]
@@ -247,12 +261,12 @@ def tile_moe_res_glu_silu_kernel(tc, xT, xr, w1, w3, w2, gate, offs, out):
             for part in range(2):
                 turn(banks[part], windows[m], part * T_HALF, False, True)
                 turned.append(keep.tile([P, T_HALF], F32, name=f"turned{part}"))
-                nc.scalar.activation(turned[part][:], banks[part][:], COPY)
+                scalar_take(turned[part][:], banks[part][:])
             for part in range(2):
                 bank = psum.tile([P, T_HALF], F32, name=f"a_bank{part}")
                 turn(bank, turned[part], 0, True, True)
                 result = keep.tile([P, T_HALF], F32, name=f"result{part}")
-                nc.scalar.activation(result[:], bank[:], COPY)
+                scalar_take(result[:], bank[:])
                 nc.scalar.dma_start(out[m * P : (m + 1) * P, part * T_HALF : (part + 1) * T_HALF], result[:])
 
         for s in range(PASSES):
@@ -260,94 +274,95 @@ def tile_moe_res_glu_silu_kernel(tc, xT, xr, w1, w3, w2, gate, offs, out):
             if s == 0:
                 nc.sync.dma_start(offsets[:], offs)
         for n, key in enumerate(chunks[0]):
-            load_chunk(key, 48 * KIB + 8 * KIB * n)
+            load_chunk(key, CHUNKS_AT + CHUNK_BYTES * n)
 
         for s in range(PASSES):
-            copy_tokens(s, 0, by_vector, 4 * KIB * s)
-            copy_tokens(s, T_HALF, by_scalar, 4 * KIB * (s + 1))
+            copy_tokens(s, 0, by_vector, STAGE[s])
+            copy_tokens(s, T_HALF, by_scalar, STAGE[s + 1])
             quantise_tokens(s, 0)
             quantise_tokens(s, T_HALF)
             gather_words(s)
         gather_scales()
 
-        load_w2(0, 8 * KIB)
-        load_chunk(chunks[1][0], 0)
-        load_gate(0, 14 * KIB)
+        load_w2(0, TOKENS_AT + CHUNK_BYTES)
+        load_chunk(chunks[1][0], TOKENS_AT)
+        load_gate(0, TOKENS_AT + CHUNK_BYTES + 4 * PACK * N)
         for n in range(1, 5):
-            load_chunk(chunks[1][n], 8 * KIB * (n + 1))
+            load_chunk(chunks[1][n], TOKENS_AT + CHUNK_BYTES * (n + 1))
 
         w3_0, w3_1, w3_2, w1_0, w1_1, w1_2 = chunks[0]
-        copy_chunk(w3_0, 0, 8 * KIB)
-        load_chunk(chunks[1][5], 48 * KIB)
-        copy_chunk(w3_1, 0, 12 * KIB)
+        copy_chunk(w3_0, 0, STAGE[2])
+        load_chunk(chunks[1][5], CHUNKS_AT)
+        copy_chunk(w3_1, 0, STAGE[3])
         quantise_chunk(w3_0)
-        copy_chunk(w3_2, P, 8 * KIB)
+        copy_chunk(w3_2, P, STAGE[2])
         quantise_chunk(w3_1)
         quantise_chunk(w3_2)
-        g_banks = linear_branch(0)
-        a_banks = silu_banks()
-        copy_chunk(w1_0, 48, 12 * KIB)
+        g_banks = w3_passes(0)
+        a_banks = first_layer_banks("a")
+        copy_chunk(w1_0, 48, STAGE[3])
         quantise_chunk(w1_0)
-        silu_branch_pass(a_banks, 0, 0)
-        copy_chunk(w1_1, 80, 8 * KIB)
+        w1_pass(a_banks, w1_0)
+        copy_chunk(w1_1, 80, STAGE[2])
         quantise_chunk(w1_1)
-        silu_branch_pass(a_banks, 0, 1)
-        copy_chunk(w1_2, 80, 8 * KIB)
-        quantise_chunk(w1_2, pieces=H_TILES, at=20 * KIB)
-        silu_branch_pass(a_banks, 0, 2)
-        load_w2(1, 64 * KIB)
-        load_gate(1, 70 * KIB)
+        w1_pass(a_banks, w1_1)
+        copy_chunk(w1_2, 104, STAGE[2])
+        quantise_chunk(w1_2, pieces=H_TILES, at=LAST_CODES_AT)
+        w1_pass(a_banks, w1_2)
+
+        load_w2(1, CHUNKS_AT + 2 * CHUNK_BYTES)
+        load_gate(1, CHUNKS_AT + 2 * CHUNK_BYTES + 4 * PACK * N)
         for m in range(N_TILES):
-            load_residual(m)
+            load_residual(m, CHUNKS_AT + CHUNK_BYTES * (3 + m))
 
         w3_0, w3_1, w3_2, w1_0, w1_1, w1_2 = chunks[1]
         for part in range(2):
-            copy_w2(0, part, by_vector, 8 * KIB + 2 * KIB * part)
+            copy_w2(0, part, by_vector, STAGE[2] + 2 * KIB * part)
         for part in range(2):
             quantise_w2(0, part)
         acts = silu_of(0, a_banks)
-        copy_chunk(w3_0, 0, 20 * KIB)
+        copy_chunk(w3_0, 0, LAST_CODES_AT)
         halves = hidden(0, acts, g_banks)
         packed = [quantise_hidden(0, half, halves[half]) for half in range(2)]
-        y, last_bank = second_layer(0, packed)
-        quantise_chunk(w3_0, at=16 * KIB)
+        y, rest_bank = second_layer(0, packed, (by_vector, scalar_take), "rest_bank")
+        rest = take_rest(0, 0, rest_bank, Y_REST_AT)
+        quantise_chunk(w3_0, at=H_AT)
 
-        copy_chunk(w3_1, 0, 12 * KIB)
+        copy_chunk(w3_1, 0, W2_CODES_AT[0])
         scatter_first_rows(0, y)
-        copy_chunk(w3_2, 0, 4 * KIB)
-        y_last = take_last_rows(0, last_bank, 0, HALF, loads, 24 * KIB)
+        scatter(2, 0, 0, rest[:])
+        copy_chunk(w3_2, 0, Y_AT[0])
         quantise_chunk(w3_1)
         quantise_chunk(w3_2)
-        g_banks = linear_branch(1)
-        scatter(2, y_last[:], 0, HALF)
-        a_banks = silu_banks()
-        copy_chunk(w1_0, 32, 24 * KIB)
-        copy_chunk(w1_1, 56, 4 * KIB)
+        g_banks = w3_passes(1)
+        a_banks = first_layer_banks("a")
+        copy_chunk(w1_0, 32, H_CODES_AT)
+        copy_chunk(w1_1, 56, STAGE[1])
         quantise_chunk(w1_0)
-        silu_branch_pass(a_banks, 1, 0)
+        w1_pass(a_banks, w1_0)
         quantise_chunk(w1_1)
-        silu_branch_pass(a_banks, 1, 1)
-        copy_chunk(w1_2, 80, 4 * KIB)
-        quantise_chunk(w1_2, pieces=H_TILES, at=20 * KIB)
-        silu_branch_pass(a_banks, 1, 2)
-        copy_w2(1, 0, by_vector, 4 * KIB)
+        w1_pass(a_banks, w1_1)
+        copy_chunk(w1_2, 80, STAGE[1])
+        quantise_chunk(w1_2, pieces=H_TILES, at=LAST_CODES_AT)
+        w1_pass(a_banks, w1_2)
+
+        copy_w2(1, 0, by_vector, STAGE[1])
         quantise_w2(1, 0)
         acts = silu_of(1, a_banks)
-        copy_w2(1, 1, by_scalar, 20 * KIB)
+        copy_w2(1, 1, by_scalar, LAST_CODES_AT)
         halves = hidden(1, acts, g_banks)
-        y_last = take_last_rows(0, last_bank, HALF, C, work, 0)
+        rest = take_rest(0, 1, rest_bank, SILU_AT[1])
         packed = [quantise_hidden(1, half, halves[half]) for half in range(2)]
         quantise_w2(1, 1)
-        scatter(2, y_last[:], HALF, C)
-        y, last_bank = second_layer(1, packed)
+        scatter(2, 0, 1, rest[:])
+        y, rest_bank = second_layer(1, packed, (scalar_take, scalar_take), "g_bank1")
         sums = open_sums(1)
 
         scatter_first_rows(1, y)
-        y_last = take_last_rows(1, last_bank, 0, HALF, work, 4 * KIB)
-        y_rest = take_last_rows(1, last_bank, HALF, C, work, 26 * KIB)
+        rests = [take_rest(1, half, rest_bank, Y_AT[half]) for half in range(2)]
         finish_on_tensor(1, sums)
-        scatter(2, y_last[:], C, C + HALF)
-        finish(0, cuts=(0, 768))
-        scatter(2, y_rest[:], C + HALF, SLOTS)
-        finish(0, cuts=(768, T))
-        finish(2, cuts=(0, 512, 768, T))
+        scatter(2, 1, 0, rests[0][:])
+        finish(0, (0, 768))
+        scatter(2, 1, 1, rests[1][:])
+        finish(0, (768, T))
+        finish(2, (0, 512, 768, T))

@@ -24,21 +24,13 @@ SLOTS = E * C
 HALF = C // 2
 RUN = 4
 T_HALF = T // 2
-W2_PARTS = ((0, 256), (256, N))
 KIB = 1024
 
+TOKENS_BYTES, CHUNK_BYTES, W2_BYTES, GATE_BYTES, RESIDUAL_BYTES = 16 * KIB, 8 * KIB, 6 * KIB, KIB, 4 * KIB
 TOKENS_AT = 0
-CHUNKS_AT = 48 * KIB
-TOKENS_BYTES, CHUNK_BYTES = 16 * KIB, 8 * KIB
+CHUNKS_AT = PASSES * TOKENS_BYTES
+FIRST_W2_AT = CHUNKS_AT + 9 * CHUNK_BYTES
 STAGE = [4 * KIB * n for n in range(4)]
-SILU_AT = (2 * KIB, 0)
-H_AT = 16 * KIB
-Y_REST_AT = 18 * KIB
-W2_CODES_AT = (STAGE[3], 19 * KIB)
-LAST_CODES_AT = 20 * KIB
-H_CODES_AT = 24 * KIB
-H_SCALES_AT = 25 * KIB
-Y_AT = (STAGE[1], 26 * KIB)
 
 FLOPS = 2 * SLOTS * (2 * K * H + H * N)
 BYTES = 4 * (K * T + 2 * N * T + E * (2 * K * H + H * N) + SLOTS) + 2 * P * SLOTS // 16
@@ -56,24 +48,27 @@ def tile_moe_res_glu_silu_kernel(tc, xT, xr, w1, w3, w2, gate, offs, out):
         def placed(pool, name, shape, dtype, at):
             return pool.tile(shape, dtype, name=name, offset=at, align_bytes=64)
 
+        def kept(name, shape, dtype):
+            return keep.tile(shape, dtype, name=name, align_bytes=64)
+
         offsets = keep.tile([P, SLOTS // 16], U16, name="offsets")
 
-        x_words = [keep.tile([P, T], U32, name=f"x_words{s}", align_bytes=64) for s in range(PASSES)]
-        x_scales = keep.tile([P, T], U8, name="x_scales", align_bytes=64)
-        nc.gpsimd.memset(x_scales[:], 0)
-        windows = [keep.tile([P, T], F32, name=f"window{m}") for m in range(N_TILES)]
+        x_words = [kept(f"x_words{s}", [P, T], U32) for s in range(PASSES)]
+        x_scales = kept("x_scales", [P, T], U8)
+        nc.vector.memset(x_scales[:].bitcast(U32), 0)
+        windows = [kept(f"window{m}", [P, T], F32) for m in range(N_TILES)]
         for m in range(N_TILES):
-            nc.gpsimd.memset(windows[m][:], 0.0)
-        identity = keep.tile([P, P], F32, name="identity")
+            nc.vector.memset(windows[m][:], 0.0)
+        identity = kept("identity", [P, P], F32)
         make_identity(nc, identity[:])
-        slot_words = [keep.tile([P, SLOTS], U32, name=f"slot_words{s}", align_bytes=64) for s in range(PASSES)]
-        slot_scales = keep.tile([P, SLOTS], U8, name="slot_scales", align_bytes=64)
+        slot_words = [kept(f"slot_words{s}", [P, SLOTS], U32) for s in range(PASSES)]
+        slot_scales = kept("slot_scales", [P, SLOTS], U8)
 
         weights = {"w1": w1, "w3": w3}
-        chunks = [[(name, e, s) for name in ("w3", "w1") for s in range(PASSES)] for e in range(E)]
+        chunks = [[(name, e, s) for name in ("w1", "w3") for s in range(PASSES)] for e in range(E)]
         raws, grouped, codes, scales = {}, {}, {}, {}
-        w2_raw, w2_codes, w2_scales = {}, {}, {}
-        residual, gates = [], []
+        w2_raw, w2_grouped, w2_codes, w2_scales = {}, {}, {}, {}
+        residual, gates = {}, {}
 
         def load_tokens(s):
             raws["x", s] = placed(loads, f"tokens{s}", [P, PACK, T], F32, TOKENS_AT + TOKENS_BYTES * s)
@@ -90,11 +85,11 @@ def tile_moe_res_glu_silu_kernel(tc, xT, xr, w1, w3, w2, gate, offs, out):
             nc.sync.dma_start(w2_raw[e][:], w2[e].rearrange("(p j) n -> p j n", j=PACK))
 
         def load_gate(e, at):
-            gates.append(placed(loads, f"gate{e}", [P, C], F32, at))
+            gates[e] = placed(loads, f"gate{e}", [P, C], F32, at)
             nc.sync.dma_start(gates[e][:], gate[0:P, e * C : (e + 1) * C])
 
         def load_residual(m, at):
-            residual.append(placed(loads, f"residual{m}", [P, T], F32, at))
+            residual[m] = placed(loads, f"residual{m}", [P, T], F32, at)
             nc.sync.dma_start(residual[m][:], xr[m * P : (m + 1) * P, :])
 
         def copy_tokens(s, first, copy, at):
@@ -106,8 +101,8 @@ def tile_moe_res_glu_silu_kernel(tc, xT, xr, w1, w3, w2, gate, offs, out):
             cols = slice(first, first + T_HALF)
             nc.vector.quantize_mx(out=x_words[s][:, cols].bitcast(FP8X4), scales=x_scales[4 * s : P, cols], in_=grouped["x", s, first][:])
 
-        def copy_chunk(key, vector_share, at):
-            grouped[key] = placed(work, "grouped_%s_%d_%d" % key, [P, H * PACK], BF16, at)
+        def copy_chunk(key, vector_share, at, pool=work):
+            grouped[key] = placed(pool, "grouped_%s_%d_%d" % key, [P, H * PACK], BF16, at)
             src = raws[key][:].rearrange("p j (m t) -> p m j t", t=H_TILES)
             dst = grouped[key][:].rearrange("p (t m j) -> p m j t", t=H_TILES, j=PACK)
             if vector_share > 0:
@@ -115,29 +110,34 @@ def tile_moe_res_glu_silu_kernel(tc, xT, xr, w1, w3, w2, gate, offs, out):
             if vector_share < P:
                 by_scalar(dst[:, vector_share:], src[:, vector_share:])
 
-        def quantise_chunk(key, pieces=1, at=None):
+        def quantise_chunk(key, pieces=1, at=None, pool=work):
+            name, e, s = key
             if at is None:
-                codes[key] = keep.tile([P, H], U32, name="codes_%s_%d_%d" % key, align_bytes=64)
+                codes[key] = kept(f"codes_{name}_{s}", [P, H], U32)
             else:
-                codes[key] = placed(work, "codes_%s_%d_%d" % key, [P, H], U32, at)
-            scales[key] = keep.tile([P, H], U8, name="scales_%s_%d_%d" % key, align_bytes=64)
+                codes[key] = placed(pool, f"codes_{name}_{e}_{s}", [P, H], U32, at)
+            scales[key] = kept(f"scales_{name}_{s}", [P, H], U8)
             width = H // pieces
             for a in range(0, H, width):
                 cols = slice(a, a + width)
                 source = grouped[key][:, PACK * a : PACK * (a + width)]
                 nc.vector.quantize_mx(out=codes[key][:, cols].bitcast(FP8X4), scales=scales[key][:, cols], in_=source)
 
-        def copy_w2(e, part, copy, at):
-            a, b = W2_PARTS[part]
-            grouped["w2", e, part] = placed(work, f"w2_grouped{e}_{part}", [P, (b - a) * PACK], BF16, at)
+        def copy_w2(e, a, b, copy, at):
+            w2_grouped[e, a] = placed(loads, f"w2_grouped{e}_{a}", [P, (b - a) * PACK], BF16, at)
             src = w2_raw[e][:, :, a:b].rearrange("p j (c i) -> p c j i", i=RUN)
-            copy(grouped["w2", e, part][:].rearrange("p (c i j) -> p c j i", i=RUN, j=PACK), src)
+            copy(w2_grouped[e, a][:].rearrange("p (c i j) -> p c j i", i=RUN, j=PACK), src)
 
-        def quantise_w2(e, part):
-            a, b = W2_PARTS[part]
-            w2_codes[e, part] = placed(work, f"w2_codes{e}_{part}", [P, b - a], U32, W2_CODES_AT[part])
-            w2_scales[e, part] = keep.tile([P, b - a], U8, name=f"w2_scales{e}_{part}", align_bytes=64)
-            nc.vector.quantize_mx(out=w2_codes[e, part][:].bitcast(FP8X4), scales=w2_scales[e, part][:], in_=grouped["w2", e, part][:])
+        def quantise_w2(e, a, b, at=None):
+            if at is None:
+                words = kept(f"w2_codes{e}_{a}", [P, b - a], U32)
+            else:
+                words = placed(work, f"w2_codes{e}_{a}", [P, b - a], U32, at)
+            planes = kept(f"w2_scales{e}_{a}", [P, b - a], U8)
+            nc.vector.quantize_mx(out=words[:].bitcast(FP8X4), scales=planes[:], in_=w2_grouped[e, a][:])
+            for first in range(a, b, P):
+                w2_codes[e, first // P] = words[:, first - a : first - a + P]
+                w2_scales[e, first // P] = planes[:, first - a : first - a + P]
 
         def gather_words(s):
             nc.vector.tensor_copy(slot_words[s][:], x_words[s][:].indirect(offsets[:]))
@@ -145,63 +145,56 @@ def tile_moe_res_glu_silu_kernel(tc, xT, xr, w1, w3, w2, gate, offs, out):
         def gather_scales():
             nc.vector.tensor_copy(slot_scales[:], x_scales[:].indirect(offsets[:]))
 
-        def first_layer_pass(banks, key, t, half):
-            e, s = key[1:]
-            channels = slice(t * P, (t + 1) * P)
-            slots = slice(e * C + half * HALF, e * C + (half + 1) * HALF)
-            nc.tensor.matmul_mx(
-                out=banks[half][:, t, :],
-                lhsT=codes[key][:, channels].bitcast(FP8X4),
-                lhsT_scale=scales[key][:, channels],
-                rhs=slot_words[s][:, slots].bitcast(FP8X4),
-                rhs_scale=slot_scales[4 * s : P, slots],
-                start=(s == 0 and t == 0),
-                stop=(s == PASSES - 1 and t == H_TILES - 1),
-            )
-
         def first_layer_banks(name):
             return [psum.tile([P, H_TILES, HALF], F32, name=f"{name}_bank{half}") for half in range(2)]
 
-        def w3_passes(e):
-            banks = first_layer_banks("g")
-            for s in range(PASSES):
-                for half in range(2):
-                    for t in range(H_TILES):
-                        first_layer_pass(banks, ("w3", e, s), t, half)
-            return banks
+        def first_layer_pass(banks, key):
+            e, s = key[1:]
+            for half in range(2):
+                slots = slice(e * C + half * HALF, e * C + (half + 1) * HALF)
+                for t in range(H_TILES):
+                    channels = slice(t * P, (t + 1) * P)
+                    nc.tensor.matmul_mx(
+                        out=banks[half][:, t, :],
+                        lhsT=codes[key][:, channels].bitcast(FP8X4),
+                        lhsT_scale=scales[key][:, channels],
+                        rhs=slot_words[s][:, slots].bitcast(FP8X4),
+                        rhs_scale=slot_scales[4 * s : P, slots],
+                        start=(s == 0 and t == 0),
+                        stop=(s == PASSES - 1 and t == H_TILES - 1),
+                    )
 
-        def w1_pass(banks, key):
-            for t in range(H_TILES):
-                for half in range(2):
-                    first_layer_pass(banks, key, t, half)
-
-        def silu_of(e, banks):
-            acts = [placed(work, f"act{e}_{half}", [P, HALF, H_TILES], F32, SILU_AT[half]) for half in range(2)]
+        def silu_of(banks, at=None):
+            if at is None:
+                acts = [kept(f"act{half}", [P, HALF, H_TILES], F32) for half in range(2)]
+            else:
+                acts = [placed(loads, f"act_held{half}", [P, HALF, H_TILES], F32, at + 2 * KIB * half) for half in range(2)]
             for half in range(2):
                 nc.scalar.activation(acts[half][:], banks[half][:].rearrange("p t n -> p n t"), SILU)
             return acts
 
-        def hidden(e, acts, banks):
-            halves = []
-            for half in range(2):
-                h = placed(work, f"h{e}_{half}", [P, HALF * H_TILES], BF16, H_AT + half * KIB)
-                nc.vector.tensor_tensor(h[:].rearrange("p (n t) -> p n t", t=H_TILES), banks[half][:].rearrange("p t n -> p n t"), acts[half][:], MULT)
-                halves.append(h)
-            return halves
+        def hidden(half, acts, banks, at=None):
+            if at is None:
+                h = kept(f"h{half}", [P, HALF * H_TILES], BF16)
+            else:
+                h = placed(loads, f"h_held{at}", [P, HALF * H_TILES], BF16, at)
+            nc.vector.tensor_tensor(h[:].rearrange("p (n t) -> p n t", t=H_TILES), banks[half][:].rearrange("p t n -> p n t"), acts[half][:], MULT)
+            return h
 
-        def quantise_hidden(e, half, h):
-            h_codes = placed(work, f"h_codes{e}_{half}", [P, HALF], U32, H_CODES_AT + half * 4 * HALF)
-            h_scales = placed(work, f"h_scales{e}_{half}", [P, HALF], U8, H_SCALES_AT + half * HALF)
+        def quantise_hidden(half, h, at=None):
+            if at is None:
+                h_codes = kept(f"h_codes{half}", [P, HALF], U32)
+            else:
+                h_codes = placed(work, f"h_codes_first{half}", [P, HALF], U32, at)
+            h_scales = kept(f"h_scales{half}", [P, HALF], U8)
             nc.vector.quantize_mx(out=h_codes[:].bitcast(FP8X4), scales=h_scales[:], in_=h[:])
             return h_codes, h_scales
 
         def second_layer_pass(bank, e, m, packed):
-            part = m // 2
-            rows = slice((m % 2) * P, (m % 2 + 1) * P)
             nc.tensor.matmul_mx(
                 out=bank,
-                lhsT=w2_codes[e, part][:, rows].bitcast(FP8X4),
-                lhsT_scale=w2_scales[e, part][:, rows],
+                lhsT=w2_codes[e, m].bitcast(FP8X4),
+                lhsT_scale=w2_scales[e, m],
                 rhs=packed[0][:].bitcast(FP8X4),
                 rhs_scale=packed[1][:],
                 start=True,
@@ -211,63 +204,39 @@ def tile_moe_res_glu_silu_kernel(tc, xT, xr, w1, w3, w2, gate, offs, out):
         def scalar_take(dst, bank):
             nc.scalar.activation(dst, bank, COPY)
 
-        def second_layer(e, packed, takes, rest_name):
-            y = []
-            for half in range(2):
-                bank = psum.tile([P, 2, HALF], F32, name=f"y_bank{half}")
-                for m in range(2):
-                    second_layer_pass(bank[:, m, :], e, m, packed[half])
-                y.append(placed(work, f"y{e}_{half}", [P, 2, HALF], F32, Y_AT[half]))
-                takes[half](y[half][:], bank[:])
-            rest_bank = psum.tile([P, C], F32, name=rest_name)
-            for half in range(2):
-                second_layer_pass(rest_bank[:, half * HALF : (half + 1) * HALF], e, 2, packed[half])
-            return y, rest_bank
-
-        def take_rest(e, half, bank, at):
-            rest = placed(work, f"y{e}_last{half * HALF}", [P, HALF], F32, at)
-            scalar_take(rest[:], bank[:, half * HALF : (half + 1) * HALF])
-            return rest
-
-        def scatter(m, e, half, values):
-            first = e * C + half * HALF
-            window = windows[m][:].indirect(offsets[:, first // 16 : (first + HALF) // 16])
-            nc.vector.tensor_tensor(window, values, gates[e][:, half * HALF : (half + 1) * HALF], MULT)
-
-        def scatter_first_rows(e, y):
-            for half in range(2):
-                for m in (1, 0):
-                    scatter(m, e, half, y[half][:, m, :])
+        def scatter(m, e, first, count, values):
+            slot = e * C + first
+            window = windows[m][:].indirect(offsets[:, slot // 16 : (slot + count) // 16])
+            nc.vector.tensor_tensor(window, values, gates[e][:, first : first + count], MULT)
 
         def finish(m, cuts):
             for a, b in zip(cuts, cuts[1:]):
                 nc.vector.tensor_tensor(residual[m][:, a:b], windows[m][:, a:b], residual[m][:, a:b], ADD)
                 nc.sync.dma_start(out[m * P : (m + 1) * P, a:b], residual[m][:, a:b])
 
-        def turn(bank, source, first, start, stop):
-            blocks = T_HALF // P
+        def turn(bank, source, first, width, start, stop):
+            blocks = width // P
             for b in range(blocks):
                 block = source[:, first + b * P : first + (b + 1) * P]
                 nc.tensor.matmul(bank[:, b * P : (b + 1) * P], block, identity[:], start=start and b == 0, stop=stop and b == blocks - 1, is_transpose=True)
 
-        def open_sums(m):
-            banks = [psum.tile([P, T_HALF], F32, name=f"y_bank{part}") for part in range(2)]
-            for part in range(2):
-                turn(banks[part], residual[m], part * T_HALF, True, False)
-            return banks
+        def open_sum(m, a, b, name):
+            bank = psum.tile([P, b - a], F32, name=name)
+            turn(bank, residual[m], a, b - a, True, False)
+            return bank
 
-        def finish_on_tensor(m, banks):
-            turned = []
-            for part in range(2):
-                turn(banks[part], windows[m], part * T_HALF, False, True)
-                turned.append(keep.tile([P, T_HALF], F32, name=f"turned{part}"))
-                scalar_take(turned[part][:], banks[part][:])
-            for part in range(2):
-                bank = psum.tile([P, T_HALF], F32, name=f"a_bank{part}")
-                turn(bank, turned[part], 0, True, True)
-                result = keep.tile([P, T_HALF], F32, name=f"result{part}")
-                scalar_take(result[:], bank[:])
-                nc.scalar.dma_start(out[m * P : (m + 1) * P, part * T_HALF : (part + 1) * T_HALF], result[:])
+        def close_sum(m, a, b, bank):
+            turn(bank, windows[m], a, b - a, False, True)
+            turned = kept(f"turned{m}_{a}", [P, b - a], F32)
+            scalar_take(turned[:], bank[:])
+            return turned
+
+        def turn_back(m, a, b, turned, name):
+            bank = psum.tile([P, b - a], F32, name=name)
+            turn(bank, turned, 0, b - a, True, True)
+            result = kept(f"result{m}_{a}", [P, b - a], F32)
+            scalar_take(result[:], bank[:])
+            nc.scalar.dma_start(out[m * P : (m + 1) * P, a:b], result[:])
 
         for s in range(PASSES):
             load_tokens(s)
@@ -275,6 +244,10 @@ def tile_moe_res_glu_silu_kernel(tc, xT, xr, w1, w3, w2, gate, offs, out):
                 nc.sync.dma_start(offsets[:], offs)
         for n, key in enumerate(chunks[0]):
             load_chunk(key, CHUNKS_AT + CHUNK_BYTES * n)
+        load_w2(0, FIRST_W2_AT)
+        load_gate(0, FIRST_W2_AT + W2_BYTES)
+        for n in range(PASSES):
+            load_chunk(chunks[1][n], CHUNKS_AT + CHUNK_BYTES * (6 + n))
 
         for s in range(PASSES):
             copy_tokens(s, 0, by_vector, STAGE[s])
@@ -284,85 +257,104 @@ def tile_moe_res_glu_silu_kernel(tc, xT, xr, w1, w3, w2, gate, offs, out):
             gather_words(s)
         gather_scales()
 
-        load_w2(0, TOKENS_AT + CHUNK_BYTES)
-        load_chunk(chunks[1][0], TOKENS_AT)
-        load_gate(0, TOKENS_AT + CHUNK_BYTES + 4 * PACK * N)
-        for n in range(1, 5):
-            load_chunk(chunks[1][n], TOKENS_AT + CHUNK_BYTES * (n + 1))
+        for n in range(PASSES):
+            load_chunk(chunks[1][PASSES + n], TOKENS_AT + CHUNK_BYTES * n)
+        at = TOKENS_AT + PASSES * CHUNK_BYTES
+        load_w2(1, at)
+        load_gate(1, at + W2_BYTES)
+        for n, m in enumerate((1, 0, 2)):
+            load_residual(m, TOKENS_AT + 2 * TOKENS_BYTES + n * RESIDUAL_BYTES)
 
-        w3_0, w3_1, w3_2, w1_0, w1_1, w1_2 = chunks[0]
-        copy_chunk(w3_0, 0, STAGE[2])
-        load_chunk(chunks[1][5], CHUNKS_AT)
-        copy_chunk(w3_1, 0, STAGE[3])
-        quantise_chunk(w3_0)
-        copy_chunk(w3_2, P, STAGE[2])
-        quantise_chunk(w3_1)
-        quantise_chunk(w3_2)
-        g_banks = w3_passes(0)
+        def chunk(key, vector_share, at, banks, pieces=1, codes_at=None):
+            copy_chunk(key, vector_share, at)
+            quantise_chunk(key, pieces, codes_at)
+            first_layer_pass(banks, key)
+
+        w1_0, w1_1, w1_2, w3_0, w3_1, w3_2 = chunks[0]
         a_banks = first_layer_banks("a")
-        copy_chunk(w1_0, 48, STAGE[3])
-        quantise_chunk(w1_0)
-        w1_pass(a_banks, w1_0)
-        copy_chunk(w1_1, 80, STAGE[2])
-        quantise_chunk(w1_1)
-        w1_pass(a_banks, w1_1)
-        copy_chunk(w1_2, 104, STAGE[2])
-        quantise_chunk(w1_2, pieces=H_TILES, at=LAST_CODES_AT)
-        w1_pass(a_banks, w1_2)
-
-        load_w2(1, CHUNKS_AT + 2 * CHUNK_BYTES)
-        load_gate(1, CHUNKS_AT + 2 * CHUNK_BYTES + 4 * PACK * N)
+        chunk(w1_0, 0, STAGE[2], a_banks)
+        chunk(w1_1, 0, STAGE[3], a_banks)
+        chunk(w1_2, P, STAGE[2], a_banks, codes_at=STAGE[0])
+        acts = silu_of(a_banks)
+        g_banks = first_layer_banks("g")
+        chunk(w3_0, P, STAGE[3], g_banks)
+        chunk(w3_1, 96, STAGE[0], g_banks)
+        chunk(w3_2, 84, STAGE[0], g_banks)
+        copy_w2(0, 0, 256, by_scalar, CHUNKS_AT + 5 * CHUNK_BYTES)
+        copy_w2(0, 256, N, by_scalar, CHUNKS_AT + 5 * CHUNK_BYTES + 2 * KIB)
+        w1_0, w1_1, w1_2, w3_0, w3_1, w3_2 = chunks[1]
+        copy_chunk(w1_0, 0, FIRST_W2_AT, loads)
+        h = hidden(0, acts, g_banks)
+        quantise_w2(0, 0, 256, STAGE[1])
+        packed = [quantise_hidden(0, h, STAGE[0])]
+        quantise_w2(0, 256, N)
+        h = hidden(1, acts, g_banks, CHUNKS_AT + 5 * CHUNK_BYTES)
+        y_banks = [psum.tile([P, N_TILES, HALF], F32, name=f"y_bank{half}") for half in range(2)]
         for m in range(N_TILES):
-            load_residual(m, CHUNKS_AT + CHUNK_BYTES * (3 + m))
+            second_layer_pass(y_banks[0][:, m, :], 0, m, packed[0])
+        y = placed(work, "y_first", [P, 2, HALF], F32, STAGE[2])
+        y_rest = kept("y_first_rest", [P, HALF], F32)
+        by_vector(y[:], y_banks[0][:, :2, :])
+        by_vector(y_rest[:], y_banks[0][:, 2, :])
+        packed.append(quantise_hidden(1, h, STAGE[0] + KIB))
+        for m in range(N_TILES):
+            second_layer_pass(y_banks[1][:, m, :], 0, m, packed[1])
 
-        w3_0, w3_1, w3_2, w1_0, w1_1, w1_2 = chunks[1]
-        for part in range(2):
-            copy_w2(0, part, by_vector, STAGE[2] + 2 * KIB * part)
-        for part in range(2):
-            quantise_w2(0, part)
-        acts = silu_of(0, a_banks)
-        copy_chunk(w3_0, 0, LAST_CODES_AT)
-        halves = hidden(0, acts, g_banks)
-        packed = [quantise_hidden(0, half, halves[half]) for half in range(2)]
-        y, rest_bank = second_layer(0, packed, (by_vector, scalar_take), "rest_bank")
-        rest = take_rest(0, 0, rest_bank, Y_REST_AT)
-        quantise_chunk(w3_0, at=H_AT)
-
-        copy_chunk(w3_1, 0, W2_CODES_AT[0])
-        scatter_first_rows(0, y)
-        scatter(2, 0, 0, rest[:])
-        copy_chunk(w3_2, 0, Y_AT[0])
-        quantise_chunk(w3_1)
-        quantise_chunk(w3_2)
-        g_banks = w3_passes(1)
         a_banks = first_layer_banks("a")
-        copy_chunk(w1_0, 32, H_CODES_AT)
-        copy_chunk(w1_1, 56, STAGE[1])
-        quantise_chunk(w1_0)
-        w1_pass(a_banks, w1_0)
-        quantise_chunk(w1_1)
-        w1_pass(a_banks, w1_1)
-        copy_chunk(w1_2, 80, STAGE[1])
-        quantise_chunk(w1_2, pieces=H_TILES, at=LAST_CODES_AT)
-        w1_pass(a_banks, w1_2)
+        scatter(0, 0, 0, HALF, y[:, 0, :])
+        scatter(1, 0, 0, HALF, y[:, 1, :])
+        scatter(2, 0, 0, HALF, y_rest[:])
+        quantise_chunk(w1_0, at=STAGE[2])
+        first_layer_pass(a_banks, w1_0)
+        y = placed(loads, "y_second", [P, 2, HALF], F32, CHUNKS_AT + 6 * CHUNK_BYTES)
+        scalar_take(y[:], y_banks[1][:, :2, :])
+        for m in range(2):
+            scatter(m, 0, HALF, HALF, y[:, m, :])
+        chunk(w1_1, 0, STAGE[0], a_banks)
+        chunk(w1_2, 0, STAGE[1], a_banks)
+        g_banks = first_layer_banks("g")
+        copy_chunk(w3_0, 40, STAGE[0])
+        copy_chunk(w3_1, 96, STAGE[1])
+        acts = silu_of(a_banks, TOKENS_AT + CHUNK_BYTES + 2 * KIB)
+        quantise_chunk(w3_0, at=TOKENS_AT + CHUNK_BYTES, pool=loads)
+        first_layer_pass(g_banks, w3_0)
+        quantise_chunk(w3_1)
+        first_layer_pass(g_banks, w3_1)
+        chunk(w3_2, 84, STAGE[0], g_banks)
+        y_rest = placed(loads, "y_second_rest", [P, HALF], F32, TOKENS_AT + 2 * CHUNK_BYTES + 4 * KIB)
+        scalar_take(y_rest[:], y_banks[1][:, 2, :])
+        scatter(2, 0, HALF, HALF, y_rest[:])
 
-        copy_w2(1, 0, by_vector, STAGE[1])
-        quantise_w2(1, 0)
-        acts = silu_of(1, a_banks)
-        copy_w2(1, 1, by_scalar, LAST_CODES_AT)
-        halves = hidden(1, acts, g_banks)
-        rest = take_rest(0, 1, rest_bank, SILU_AT[1])
-        packed = [quantise_hidden(1, half, halves[half]) for half in range(2)]
-        quantise_w2(1, 1)
-        scatter(2, 0, 1, rest[:])
-        y, rest_bank = second_layer(1, packed, (scalar_take, scalar_take), "g_bank1")
-        sums = open_sums(1)
-
-        scatter_first_rows(1, y)
-        rests = [take_rest(1, half, rest_bank, Y_AT[half]) for half in range(2)]
-        finish_on_tensor(1, sums)
-        scatter(2, 1, 0, rests[0][:])
-        finish(0, (0, 768))
-        scatter(2, 1, 1, rests[1][:])
-        finish(0, (768, T))
+        for m in range(N_TILES):
+            copy_w2(1, m * P, (m + 1) * P, by_scalar, TOKENS_AT + 2 * CHUNK_BYTES + m * KIB)
+        h = hidden(0, acts, g_banks)
+        quantise_w2(1, 0, P)
+        packed = [quantise_hidden(0, h)]
+        y_banks = [psum.tile([P, HALF], F32, name=f"y_bank{half}") for half in range(2)]
+        y_banks += [psum.tile([P, C], F32, name=f"y_bank{m + 1}") for m in range(1, N_TILES)]
+        y = [kept(f"y_last{half}", [P, HALF], F32) for half in range(2)] + [kept(f"y_last{m + 1}", [P, C], F32) for m in range(1, N_TILES)]
+        second_layer_pass(y_banks[0][:], 1, 0, packed[0])
+        scalar_take(y[0][:], y_banks[0][:])
+        h = hidden(1, acts, g_banks, TOKENS_AT + 2 * CHUNK_BYTES)
+        quantise_w2(1, P, 2 * P)
+        packed.append(quantise_hidden(1, h))
+        second_layer_pass(y_banks[1][:], 1, 0, packed[1])
+        scalar_take(y[1][:], y_banks[1][:])
+        scatter(0, 1, 0, HALF, y[0][:])
+        quantise_w2(1, 2 * P, N)
+        for m in range(1, N_TILES):
+            for half in range(2):
+                second_layer_pass(y_banks[m + 1][:, half * HALF : (half + 1) * HALF], 1, m, packed[half])
+            scalar_take(y[m + 1][:], y_banks[m + 1][:])
+        scatter(0, 1, HALF, HALF, y[1][:])
+        parts = ((0, 256), (256, 512), (512, T))
+        sums = [open_sum(0, a, b, name) for (a, b), name in zip(parts, ("a_bank0", "a_bank1", "g_bank0"))]
+        turned = [close_sum(0, a, b, bank) for (a, b), bank in zip(parts, sums)]
+        for (a, b), tile, name in zip(parts, turned, ("y_bank0", "y_bank1", "y_bank2")):
+            turn_back(0, a, b, tile, name)
+        scatter(1, 1, 0, C, y[2][:])
+        scatter(2, 1, 0, HALF, y[3][:, :HALF])
+        finish(1, (0, 768))
+        scatter(2, 1, HALF, HALF, y[3][:, HALF:])
+        finish(1, (768, T))
         finish(2, (0, 512, 768, T))

@@ -245,9 +245,10 @@ def tile_moe_res_glu_silu_kernel(tc, xT, xr, w1, w3, w2, gate, offs, out):
         for n, key in enumerate(chunks[0]):
             load_chunk(key, CHUNKS_AT + CHUNK_BYTES * n)
         load_w2(0, FIRST_W2_AT)
-        load_gate(0, FIRST_W2_AT + W2_BYTES)
         for n in range(PASSES):
             load_chunk(chunks[1][n], CHUNKS_AT + CHUNK_BYTES * (6 + n))
+            if n == 0:
+                load_gate(0, FIRST_W2_AT + W2_BYTES)
 
         for s in range(PASSES):
             copy_tokens(s, 0, by_vector, STAGE[s])
@@ -262,7 +263,7 @@ def tile_moe_res_glu_silu_kernel(tc, xT, xr, w1, w3, w2, gate, offs, out):
         at = TOKENS_AT + PASSES * CHUNK_BYTES
         load_w2(1, at)
         load_gate(1, at + W2_BYTES)
-        for n, m in enumerate((1, 0, 2)):
+        for n, m in enumerate((1, 2, 0)):
             load_residual(m, TOKENS_AT + 2 * TOKENS_BYTES + n * RESIDUAL_BYTES)
 
         def chunk(key, vector_share, at, banks, pieces=1, codes_at=None):
@@ -280,7 +281,7 @@ def tile_moe_res_glu_silu_kernel(tc, xT, xr, w1, w3, w2, gate, offs, out):
         chunk(w3_0, P, STAGE[3], g_banks)
         chunk(w3_1, 96, STAGE[0], g_banks)
         chunk(w3_2, 84, STAGE[0], g_banks)
-        copy_w2(0, 0, 256, by_scalar, CHUNKS_AT + 5 * CHUNK_BYTES)
+        copy_w2(0, 0, 256, by_vector, CHUNKS_AT + 5 * CHUNK_BYTES)
         copy_w2(0, 256, N, by_scalar, CHUNKS_AT + 5 * CHUNK_BYTES + 2 * KIB)
         w1_0, w1_1, w1_2, w3_0, w3_1, w3_2 = chunks[1]
         copy_chunk(w1_0, 0, FIRST_W2_AT, loads)
@@ -288,15 +289,15 @@ def tile_moe_res_glu_silu_kernel(tc, xT, xr, w1, w3, w2, gate, offs, out):
         quantise_w2(0, 0, 256, STAGE[1])
         packed = [quantise_hidden(0, h, STAGE[0])]
         quantise_w2(0, 256, N)
-        h = hidden(1, acts, g_banks, CHUNKS_AT + 5 * CHUNK_BYTES)
+        h = hidden(1, acts, g_banks)
         y_banks = [psum.tile([P, N_TILES, HALF], F32, name=f"y_bank{half}") for half in range(2)]
         for m in range(N_TILES):
             second_layer_pass(y_banks[0][:, m, :], 0, m, packed[0])
         y = placed(work, "y_first", [P, 2, HALF], F32, STAGE[2])
-        y_rest = kept("y_first_rest", [P, HALF], F32)
-        by_vector(y[:], y_banks[0][:, :2, :])
-        by_vector(y_rest[:], y_banks[0][:, 2, :])
         packed.append(quantise_hidden(1, h, STAGE[0] + KIB))
+        by_vector(y[:], y_banks[0][:, :2, :])
+        y_rest = placed(loads, "y_first_rest", [P, HALF], F32, CHUNKS_AT + 6 * CHUNK_BYTES + 2 * KIB)
+        scalar_take(y_rest[:], y_banks[0][:, 2, :])
         for m in range(N_TILES):
             second_layer_pass(y_banks[1][:, m, :], 0, m, packed[1])
 

@@ -68,7 +68,7 @@ def tile_moe_res_glu_silu_kernel(tc, xT, xr, w1, w3, w2, gate, offs, out):
         chunks = [[(name, e, s) for name in ("w1", "w3") for s in range(PASSES)] for e in range(E)]
         raws, grouped, codes, scales = {}, {}, {}, {}
         w2_raw, w2_grouped, w2_codes, w2_scales = {}, {}, {}, {}
-        residual, gates = {}, {}
+        residual = {}
 
         def load_tokens(s):
             raws["x", s] = placed(loads, f"tokens{s}", [P, PACK, T], F32, TOKENS_AT + TOKENS_BYTES * s)
@@ -84,9 +84,18 @@ def tile_moe_res_glu_silu_kernel(tc, xT, xr, w1, w3, w2, gate, offs, out):
             w2_raw[e] = placed(loads, f"w2_raw{e}", [P, PACK, N], F32, at)
             nc.sync.dma_start(w2_raw[e][:], w2[e].rearrange("(p j) n -> p j n", j=PACK))
 
-        def load_gate(e, at):
-            gates[e] = placed(loads, f"gate{e}", [P, C], F32, at)
-            nc.sync.dma_start(gates[e][:], gate[0:P, e * C : (e + 1) * C])
+        def load_gate():
+            column = kept("gate_column", [P, SLOTS // P], F32)
+            nc.sync.dma_start(column[:], gate[0].rearrange("(n r) -> n r", r=SLOTS // P))
+            return column
+
+        def spread_gate(column):
+            bank = psum.tile([P, SLOTS // P, P], F32, name="y_bank3")
+            for r in range(SLOTS // P):
+                nc.tensor.transpose(bank[:, r, :], column[:, r : r + 1].to_broadcast([P, P]), identity[:])
+            spread = kept("gates", [P, SLOTS], F32)
+            scalar_take(spread[:].rearrange("p (n r) -> p n r", r=SLOTS // P), bank[:].rearrange("p r n -> p n r"))
+            return spread
 
         def load_residual(m, at):
             residual[m] = placed(loads, f"residual{m}", [P, T], F32, at)
@@ -207,7 +216,7 @@ def tile_moe_res_glu_silu_kernel(tc, xT, xr, w1, w3, w2, gate, offs, out):
         def scatter(m, e, first, count, values):
             slot = e * C + first
             window = windows[m][:].indirect(offsets[:, slot // 16 : (slot + count) // 16])
-            nc.vector.tensor_tensor(window, values, gates[e][:, first : first + count], MULT)
+            nc.vector.tensor_tensor(window, values, gates[:, slot : slot + count], MULT)
 
         def finish(m, cuts):
             for a, b in zip(cuts, cuts[1:]):
@@ -242,14 +251,14 @@ def tile_moe_res_glu_silu_kernel(tc, xT, xr, w1, w3, w2, gate, offs, out):
             load_tokens(s)
             if s == 0:
                 nc.sync.dma_start(offsets[:], offs)
+                gate_column = load_gate()
         for n, key in enumerate(chunks[0]):
             load_chunk(key, CHUNKS_AT + CHUNK_BYTES * n)
         load_w2(0, FIRST_W2_AT)
         for n in range(PASSES):
             load_chunk(chunks[1][n], CHUNKS_AT + CHUNK_BYTES * (6 + n))
-            if n == 0:
-                load_gate(0, FIRST_W2_AT + W2_BYTES)
 
+        gates = spread_gate(gate_column)
         for s in range(PASSES):
             copy_tokens(s, 0, by_vector, STAGE[s])
             copy_tokens(s, T_HALF, by_scalar, STAGE[s + 1])
@@ -262,7 +271,6 @@ def tile_moe_res_glu_silu_kernel(tc, xT, xr, w1, w3, w2, gate, offs, out):
             load_chunk(chunks[1][PASSES + n], TOKENS_AT + CHUNK_BYTES * n)
         at = TOKENS_AT + PASSES * CHUNK_BYTES
         load_w2(1, at)
-        load_gate(1, at + W2_BYTES)
         for n, m in enumerate((1, 2, 0)):
             load_residual(m, TOKENS_AT + 2 * TOKENS_BYTES + n * RESIDUAL_BYTES)
 
@@ -312,7 +320,7 @@ def tile_moe_res_glu_silu_kernel(tc, xT, xr, w1, w3, w2, gate, offs, out):
         for m in range(2):
             scatter(m, 0, HALF, HALF, y[:, m, :])
         chunk(w1_1, 0, STAGE[0], a_banks)
-        chunk(w1_2, 0, STAGE[1], a_banks)
+        chunk(w1_2, 48, STAGE[1], a_banks)
         g_banks = first_layer_banks("g")
         copy_chunk(w3_0, 40, STAGE[0])
         copy_chunk(w3_1, 96, STAGE[1])

@@ -320,9 +320,9 @@ def tile_moe_res_glu_silu_kernel(tc, xT, xr, w1, w3, w2, gate, offs, out):
         for m in range(2):
             scatter(m, 0, HALF, HALF, y[:, m, :])
         chunk(w1_1, 0, STAGE[0], a_banks)
-        chunk(w1_2, 48, STAGE[1], a_banks)
+        chunk(w1_2, 0, STAGE[1], a_banks)
         g_banks = first_layer_banks("g")
-        copy_chunk(w3_0, 40, STAGE[0])
+        copy_chunk(w3_0, 0, STAGE[0])
         copy_chunk(w3_1, 96, STAGE[1])
         acts = silu_of(a_banks, TOKENS_AT + CHUNK_BYTES + 2 * KIB)
         quantise_chunk(w3_0, at=TOKENS_AT + CHUNK_BYTES, pool=loads)

@@ -26,11 +26,15 @@ RUN = 4
 T_HALF = T // 2
 KIB = 1024
 
-TOKENS_BYTES, CHUNK_BYTES, W2_BYTES, GATE_BYTES, RESIDUAL_BYTES = 16 * KIB, 8 * KIB, 6 * KIB, KIB, 4 * KIB
-TOKENS_AT = 0
+TOKENS_BYTES, CHUNK_BYTES, W2_BYTES, RESIDUAL_BYTES = 16 * KIB, 8 * KIB, 6 * KIB, 4 * KIB
 CHUNKS_AT = PASSES * TOKENS_BYTES
 FIRST_W2_AT = CHUNKS_AT + 9 * CHUNK_BYTES
-STAGE = [4 * KIB * n for n in range(4)]
+
+SHARES = (
+    ((0, 0), (16, 0), (16, 16), (16, 16), (16, 8), (16, 6)),
+    ((0, 0), (16, 16), (16, 16), (0, 6), (0, 16), (16, 6)),
+)
+BLOCKS = H // 32
 
 FLOPS = 2 * SLOTS * (2 * K * H + H * N)
 BYTES = 4 * (K * T + 2 * N * T + E * (2 * K * H + H * N) + SLOTS) + 2 * P * SLOTS // 16
@@ -42,7 +46,7 @@ def tile_moe_res_glu_silu_kernel(tc, xT, xr, w1, w3, w2, gate, offs, out):
     with ExitStack() as ctx:
         keep = ctx.enter_context(tc.tile_pool(name="keep", bufs=1))
         loads = ctx.enter_context(tc.tile_pool(name="loads", bufs=1))
-        work = ctx.enter_context(tc.tile_pool(name="work", bufs=1))
+        stage = ctx.enter_context(tc.tile_pool(name="stage", bufs=4))
         psum = ctx.enter_context(tc.psum_pool(name="psum", bufs=1))
 
         def placed(pool, name, shape, dtype, at):
@@ -52,7 +56,6 @@ def tile_moe_res_glu_silu_kernel(tc, xT, xr, w1, w3, w2, gate, offs, out):
             return keep.tile(shape, dtype, name=name, align_bytes=64)
 
         offsets = keep.tile([P, SLOTS // 16], U16, name="offsets")
-
         x_words = [kept(f"x_words{s}", [P, T], U32) for s in range(PASSES)]
         x_scales = kept("x_scales", [P, T], U8)
         nc.vector.memset(x_scales[:].bitcast(U32), 0)
@@ -64,306 +67,222 @@ def tile_moe_res_glu_silu_kernel(tc, xT, xr, w1, w3, w2, gate, offs, out):
         slot_words = [kept(f"slot_words{s}", [P, SLOTS], U32) for s in range(PASSES)]
         slot_scales = kept("slot_scales", [P, SLOTS], U8)
 
-        weights = {"w1": w1, "w3": w3}
-        chunks = [[(name, e, s) for name in ("w1", "w3") for s in range(PASSES)] for e in range(E)]
-        raws, grouped, codes, scales = {}, {}, {}, {}
-        w2_raw, w2_grouped, w2_codes, w2_scales = {}, {}, {}, {}
-        residual = {}
+        def load_rows(name, rows, at):
+            tile = placed(loads, name, [P, PACK, rows.shape[1]], F32, at)
+            nc.sync.dma_start(tile[:], rows.rearrange("(p j) c -> p j c", j=PACK))
+            return tile
 
-        def load_tokens(s):
-            raws["x", s] = placed(loads, f"tokens{s}", [P, PACK, T], F32, TOKENS_AT + TOKENS_BYTES * s)
-            nc.sync.dma_start(raws["x", s][:], xT[s * K_PASS : (s + 1) * K_PASS, :].rearrange("(p j) t -> p j t", j=PACK))
-
-        def load_chunk(key, at):
-            name, e, s = key
-            raws[key] = placed(loads, "raw_%s_%d_%d" % key, [P, PACK, H], F32, at)
-            rows = weights[name][e, s * K_PASS : (s + 1) * K_PASS, :]
-            nc.sync.dma_start(raws[key][:], rows.rearrange("(p j) i -> p j i", j=PACK))
+        def load_chunks(name, weight, e, at):
+            return [load_rows(f"{name}_{e}_{s}", weight[e, s * K_PASS : (s + 1) * K_PASS, :], at + s * CHUNK_BYTES) for s in range(PASSES)]
 
         def load_w2(e, at):
-            w2_raw[e] = placed(loads, f"w2_raw{e}", [P, PACK, N], F32, at)
-            nc.sync.dma_start(w2_raw[e][:], w2[e].rearrange("(p j) n -> p j n", j=PACK))
+            tile = placed(loads, f"w2_{e}", [P, PACK, N], F32, at)
+            rows = w2[e].rearrange("(g u r v) n -> u g r (v n)", u=2, r=8, v=2)
+            for u in range(2):
+                nc.sync.dma_start(tile[:, 2 * u : 2 * u + 2, :].rearrange("p v n -> p (v n)"), rows[u])
+            return tile
 
-        def load_gate():
-            column = kept("gate_column", [P, SLOTS // P], F32)
-            nc.sync.dma_start(column[:], gate[0].rearrange("(n r) -> n r", r=SLOTS // P))
-            return column
+        def load_residual(m, at):
+            tile = placed(loads, f"residual{m}", [P, T], F32, at)
+            nc.sync.dma_start(tile[:], xr[m * P : (m + 1) * P, :])
+            return tile
 
         def spread_gate(column):
             bank = psum.tile([P, SLOTS // P, P], F32, name="y_bank3")
             for r in range(SLOTS // P):
                 nc.tensor.transpose(bank[:, r, :], column[:, r : r + 1].to_broadcast([P, P]), identity[:])
             spread = kept("gates", [P, SLOTS], F32)
-            scalar_take(spread[:].rearrange("p (n r) -> p n r", r=SLOTS // P), bank[:].rearrange("p r n -> p n r"))
+            nc.scalar.activation(spread[:].rearrange("p (n r) -> p n r", r=SLOTS // P), bank[:].rearrange("p r n -> p n r"), COPY)
             return spread
 
-        def load_residual(m, at):
-            residual[m] = placed(loads, f"residual{m}", [P, T], F32, at)
-            nc.sync.dma_start(residual[m][:], xr[m * P : (m + 1) * P, :])
+        def interleave(copy, grouped, raw, a, b):
+            src = raw[:, :, a:b].rearrange("p j (c i) -> p c j i", i=RUN)
+            copy(grouped.rearrange("p (c i j) -> p c j i", i=RUN, j=PACK), src)
 
-        def copy_tokens(s, first, copy, at):
-            grouped["x", s, first] = placed(work, f"x_grouped{s}_{first}", [P, T_HALF * PACK], BF16, at)
-            src = raws["x", s][:, :, first : first + T_HALF].rearrange("p j (c i) -> p c j i", i=RUN)
-            copy(grouped["x", s, first][:].rearrange("p (c i j) -> p c j i", i=RUN, j=PACK), src)
+        def quantise(words, planes, grouped):
+            nc.vector.quantize_mx(out=words.bitcast(FP8X4), scales=planes, in_=grouped)
 
-        def quantise_tokens(s, first):
-            cols = slice(first, first + T_HALF)
-            nc.vector.quantize_mx(out=x_words[s][:, cols].bitcast(FP8X4), scales=x_scales[4 * s : P, cols], in_=grouped["x", s, first][:])
-
-        def copy_chunk(key, vector_share, at, pool=work):
-            grouped[key] = placed(pool, "grouped_%s_%d_%d" % key, [P, H * PACK], BF16, at)
-            src = raws[key][:].rearrange("p j (m t) -> p m j t", t=H_TILES)
-            dst = grouped[key][:].rearrange("p (t m j) -> p m j t", t=H_TILES, j=PACK)
-            if vector_share > 0:
-                by_vector(dst[:, :vector_share], src[:, :vector_share])
-            if vector_share < P:
-                by_scalar(dst[:, vector_share:], src[:, vector_share:])
-
-        def quantise_chunk(key, pieces=1, at=None, pool=work):
-            name, e, s = key
-            if at is None:
-                codes[key] = kept(f"codes_{name}_{s}", [P, H], U32)
-            else:
-                codes[key] = placed(pool, f"codes_{name}_{e}_{s}", [P, H], U32, at)
-            scales[key] = kept(f"scales_{name}_{s}", [P, H], U8)
-            width = H // pieces
-            for a in range(0, H, width):
-                cols = slice(a, a + width)
-                source = grouped[key][:, PACK * a : PACK * (a + width)]
-                nc.vector.quantize_mx(out=codes[key][:, cols].bitcast(FP8X4), scales=scales[key][:, cols], in_=source)
-
-        def copy_w2(e, a, b, copy, at):
-            w2_grouped[e, a] = placed(loads, f"w2_grouped{e}_{a}", [P, (b - a) * PACK], BF16, at)
-            src = w2_raw[e][:, :, a:b].rearrange("p j (c i) -> p c j i", i=RUN)
-            copy(w2_grouped[e, a][:].rearrange("p (c i j) -> p c j i", i=RUN, j=PACK), src)
-
-        def quantise_w2(e, a, b, at=None):
-            if at is None:
-                words = kept(f"w2_codes{e}_{a}", [P, b - a], U32)
-            else:
-                words = placed(work, f"w2_codes{e}_{a}", [P, b - a], U32, at)
-            planes = kept(f"w2_scales{e}_{a}", [P, b - a], U8)
-            nc.vector.quantize_mx(out=words[:].bitcast(FP8X4), scales=planes[:], in_=w2_grouped[e, a][:])
-            for first in range(a, b, P):
-                w2_codes[e, first // P] = words[:, first - a : first - a + P]
-                w2_scales[e, first // P] = planes[:, first - a : first - a + P]
-
-        def gather_words(s):
+        def token_pass(s, raw):
+            halves = []
+            for first, copy in ((0, by_vector), (T_HALF, by_scalar)):
+                grouped = stage.tile([P, T_HALF * PACK], BF16, name="grouped", align_bytes=64)
+                interleave(copy, grouped[:], raw, first, first + T_HALF)
+                halves.append((first, grouped))
+            for first, grouped in halves:
+                cols = slice(first, first + T_HALF)
+                quantise(x_words[s][:, cols], x_scales[4 * s : P, cols], grouped[:])
             nc.vector.tensor_copy(slot_words[s][:], x_words[s][:].indirect(offsets[:]))
-
-        def gather_scales():
-            nc.vector.tensor_copy(slot_scales[:], x_scales[:].indirect(offsets[:]))
 
         def first_layer_banks(name):
             return [psum.tile([P, H_TILES, HALF], F32, name=f"{name}_bank{half}") for half in range(2)]
 
-        def first_layer_pass(banks, key):
-            e, s = key[1:]
+        def copy_chunk(raw, share):
+            grouped = stage.tile([P, H * PACK], BF16, name="grouped", align_bytes=64)
+            src = raw[:].rearrange("p j (g u q a v) -> p u g q j a v", u=2, q=4, a=2, v=2)
+            dst = grouped[:].rearrange("p (u v g q a j) -> p u g q j a v", u=2, v=2, q=4, a=2, j=PACK)
+            for u in range(2):
+                if share[u] > 0:
+                    by_vector(dst[:, u, : share[u]], src[:, u, : share[u]])
+                if share[u] < BLOCKS:
+                    by_scalar(dst[:, u, share[u] :], src[:, u, share[u] :])
+            return grouped
+
+        def first_layer_pass(name, e, s, banks, grouped):
+            words = kept(f"{name}_words{s}", [P, H], U32)
+            planes = kept(f"{name}_scales{s}", [P, H], U8)
+            for a in (0, H // 2):
+                quantise(words[:, a : a + H // 2], planes[:, a : a + H // 2], grouped[:, PACK * a : PACK * (a + H // 2)])
             for half in range(2):
                 slots = slice(e * C + half * HALF, e * C + (half + 1) * HALF)
                 for t in range(H_TILES):
                     channels = slice(t * P, (t + 1) * P)
                     nc.tensor.matmul_mx(
                         out=banks[half][:, t, :],
-                        lhsT=codes[key][:, channels].bitcast(FP8X4),
-                        lhsT_scale=scales[key][:, channels],
+                        lhsT=words[:, channels].bitcast(FP8X4),
+                        lhsT_scale=planes[:, channels],
                         rhs=slot_words[s][:, slots].bitcast(FP8X4),
                         rhs_scale=slot_scales[4 * s : P, slots],
                         start=(s == 0 and t == 0),
                         stop=(s == PASSES - 1 and t == H_TILES - 1),
                     )
 
-        def silu_of(banks, at=None):
-            if at is None:
-                acts = [kept(f"act{half}", [P, HALF, H_TILES], F32) for half in range(2)]
-            else:
-                acts = [placed(loads, f"act_held{half}", [P, HALF, H_TILES], F32, at + 2 * KIB * half) for half in range(2)]
+        def silu_of(bank, at):
+            act = placed(loads, f"act{at}", [P, HALF, H_TILES], F32, at)
+            nc.scalar.activation(act[:], bank[:].rearrange("p t n -> p n t"), SILU)
+            return act
+
+        def prepare_w2(raw):
+            grouped = [kept(f"w2_grouped{m}", [P, P * PACK], BF16) for m in range(N_TILES)]
+            for m in range(N_TILES):
+                interleave(by_scalar, grouped[m][:], raw, m * P, (m + 1) * P)
+            words = [kept(f"w2_words{m}", [P, P], U32) for m in range(N_TILES)]
+            planes = [kept(f"w2_scales{m}", [P, P], U8) for m in range(N_TILES)]
+            for m in range(N_TILES):
+                quantise(words[m][:], planes[m][:], grouped[m][:])
+            return words, planes
+
+        def hidden(acts, g_banks):
+            words = kept("h_words", [P, C], U32)
+            planes = kept("h_scales", [P, C], U8)
+            h = [kept(f"h{half}", [P, HALF * H_TILES], BF16) for half in range(2)]
             for half in range(2):
-                nc.scalar.activation(acts[half][:], banks[half][:].rearrange("p t n -> p n t"), SILU)
-            return acts
+                nc.vector.tensor_tensor(h[half][:].rearrange("p (n t) -> p n t", t=H_TILES), g_banks[half][:].rearrange("p t n -> p n t"), acts[half][:], MULT)
+            for half in range(2):
+                cols = slice(half * HALF, (half + 1) * HALF)
+                quantise(words[:, cols], planes[:, cols], h[half][:])
+            return words, planes
 
-        def hidden(half, acts, banks, at=None):
-            if at is None:
-                h = kept(f"h{half}", [P, HALF * H_TILES], BF16)
-            else:
-                h = placed(loads, f"h_held{at}", [P, HALF * H_TILES], BF16, at)
-            nc.vector.tensor_tensor(h[:].rearrange("p (n t) -> p n t", t=H_TILES), banks[half][:].rearrange("p t n -> p n t"), acts[half][:], MULT)
-            return h
+        def second_layer(w2_packed, h_packed, tiles, first, count, bank_name):
+            cols = slice(first, first + count)
+            bank = psum.tile([P, len(tiles), count], F32, name=bank_name)
+            for n, m in enumerate(tiles):
+                nc.tensor.matmul_mx(
+                    out=bank[:, n, :], lhsT=w2_packed[0][m][:].bitcast(FP8X4), lhsT_scale=w2_packed[1][m][:],
+                    rhs=h_packed[0][:, cols].bitcast(FP8X4), rhs_scale=h_packed[1][:, cols], start=True, stop=True,
+                )
+            return bank
 
-        def quantise_hidden(half, h, at=None):
-            if at is None:
-                h_codes = kept(f"h_codes{half}", [P, HALF], U32)
-            else:
-                h_codes = placed(work, f"h_codes_first{half}", [P, HALF], U32, at)
-            h_scales = kept(f"h_scales{half}", [P, HALF], U8)
-            nc.vector.quantize_mx(out=h_codes[:].bitcast(FP8X4), scales=h_scales[:], in_=h[:])
-            return h_codes, h_scales
+        def take_gated(y, e, tiles, first, bank):
+            count = bank.shape[2]
+            cols = slice(first, first + count)
+            weights = gates[:, e * C + cols.start : e * C + cols.stop].unsqueeze(1).to_broadcast([P, len(tiles), count])
+            nc.vector.tensor_tensor(y[:, tiles.start : tiles.stop, cols], bank[:], weights, MULT)
 
-        def second_layer_pass(bank, e, m, packed):
-            nc.tensor.matmul_mx(
-                out=bank,
-                lhsT=w2_codes[e, m].bitcast(FP8X4),
-                lhsT_scale=w2_scales[e, m],
-                rhs=packed[0][:].bitcast(FP8X4),
-                rhs_scale=packed[1][:],
-                start=True,
-                stop=True,
-            )
+        def window_at(m, slot, count):
+            return windows[m][:].indirect(offsets[:, slot // 16 : (slot + count) // 16])
 
-        def scalar_take(dst, bank):
-            nc.scalar.activation(dst, bank, COPY)
+        def scalar_scatter(m, slot, values):
+            nc.scalar.activation(window_at(m, slot, values.shape[1]), values, COPY)
 
-        def scatter(m, e, first, count, values):
-            slot = e * C + first
-            window = windows[m][:].indirect(offsets[:, slot // 16 : (slot + count) // 16])
-            nc.vector.tensor_tensor(window, values, gates[:, slot : slot + count], MULT)
-
-        def finish(m, cuts):
-            for a, b in zip(cuts, cuts[1:]):
-                nc.vector.tensor_tensor(residual[m][:, a:b], windows[m][:, a:b], residual[m][:, a:b], ADD)
-                nc.sync.dma_start(out[m * P : (m + 1) * P, a:b], residual[m][:, a:b])
-
-        def turn(bank, source, first, width, start, stop):
-            blocks = width // P
+        def turn(bank, source, first, start, stop):
+            blocks = T_HALF // P
             for b in range(blocks):
                 block = source[:, first + b * P : first + (b + 1) * P]
                 nc.tensor.matmul(bank[:, b * P : (b + 1) * P], block, identity[:], start=start and b == 0, stop=stop and b == blocks - 1, is_transpose=True)
 
-        def open_sum(m, a, b, name):
-            bank = psum.tile([P, b - a], F32, name=name)
-            turn(bank, residual[m], a, b - a, True, False)
-            return bank
+        def finish(m, a, b, result):
+            nc.vector.tensor_tensor(result, windows[m][:, a:b], residual[m][:, a:b], ADD)
+            nc.sync.dma_start(out[m * P : (m + 1) * P, a:b], result)
 
-        def close_sum(m, a, b, bank):
-            turn(bank, windows[m], a, b - a, False, True)
-            turned = kept(f"turned{m}_{a}", [P, b - a], F32)
-            scalar_take(turned[:], bank[:])
-            return turned
-
-        def turn_back(m, a, b, turned, name):
-            bank = psum.tile([P, b - a], F32, name=name)
-            turn(bank, turned, 0, b - a, True, True)
-            result = kept(f"result{m}_{a}", [P, b - a], F32)
-            scalar_take(result[:], bank[:])
-            nc.scalar.dma_start(out[m * P : (m + 1) * P, a:b], result[:])
-
+        tokens = []
         for s in range(PASSES):
-            load_tokens(s)
+            tokens.append(load_rows(f"tokens{s}", xT[s * K_PASS : (s + 1) * K_PASS, :], s * TOKENS_BYTES))
             if s == 0:
                 nc.sync.dma_start(offsets[:], offs)
-                gate_column = load_gate()
-        for n, key in enumerate(chunks[0]):
-            load_chunk(key, CHUNKS_AT + CHUNK_BYTES * n)
-        load_w2(0, FIRST_W2_AT)
-        for n in range(PASSES):
-            load_chunk(chunks[1][n], CHUNKS_AT + CHUNK_BYTES * (6 + n))
+                gate_column = kept("gate_column", [P, SLOTS // P], F32)
+                nc.sync.dma_start(gate_column[:], gate[0].rearrange("(n r) -> n r", r=SLOTS // P))
+        w1_raw = [load_chunks("w1", w1, 0, CHUNKS_AT)]
+        w3_raw = [load_chunks("w3", w3, 0, CHUNKS_AT + 3 * CHUNK_BYTES)]
+        w2_raw = [load_w2(0, FIRST_W2_AT)]
+        w1_raw.append(load_chunks("w1", w1, 1, CHUNKS_AT + 6 * CHUNK_BYTES))
 
         gates = spread_gate(gate_column)
         for s in range(PASSES):
-            copy_tokens(s, 0, by_vector, STAGE[s])
-            copy_tokens(s, T_HALF, by_scalar, STAGE[s + 1])
-            quantise_tokens(s, 0)
-            quantise_tokens(s, T_HALF)
-            gather_words(s)
-        gather_scales()
+            token_pass(s, tokens[s])
+        nc.vector.tensor_copy(slot_scales[:], x_scales[:].indirect(offsets[:]))
 
-        for n in range(PASSES):
-            load_chunk(chunks[1][PASSES + n], TOKENS_AT + CHUNK_BYTES * n)
-        at = TOKENS_AT + PASSES * CHUNK_BYTES
-        load_w2(1, at)
-        for n, m in enumerate((1, 2, 0)):
-            load_residual(m, TOKENS_AT + 2 * TOKENS_BYTES + n * RESIDUAL_BYTES)
+        w3_raw.append(load_chunks("w3", w3, 1, 0))
+        w2_raw.append(load_w2(1, PASSES * CHUNK_BYTES))
+        residual = {m: load_residual(m, 2 * TOKENS_BYTES + m * RESIDUAL_BYTES) for m in range(N_TILES)}
 
-        def chunk(key, vector_share, at, banks, pieces=1, codes_at=None):
-            copy_chunk(key, vector_share, at)
-            quantise_chunk(key, pieces, codes_at)
-            first_layer_pass(banks, key)
+        a_banks, g_banks = first_layer_banks("a"), first_layer_banks("g")
+        for s in range(PASSES):
+            first_layer_pass("a", 0, s, a_banks, copy_chunk(w1_raw[0][s], SHARES[0][s]))
+        acts = [silu_of(a_banks[half], CHUNKS_AT + 2 * KIB * half) for half in range(2)]
+        for s in range(PASSES):
+            first_layer_pass("g", 0, s, g_banks, copy_chunk(w3_raw[0][s], SHARES[0][PASSES + s]))
+        w2_packed = prepare_w2(w2_raw[0])
+        h_packed = hidden(acts, g_banks)
+        next_w1_at = CHUNKS_AT + 6 * CHUNK_BYTES
+        next_grouped = copy_chunk(w1_raw[1][0], SHARES[1][0])
+        y = placed(loads, "y_first", [P, N_TILES, C], F32, next_w1_at)
+        for tiles, first, name in ((range(1), 0, "y_bank0"), (range(1, 3), 0, "y_bank2"), (range(2), HALF, "y_bank1")):
+            take_gated(y, 0, tiles, first, second_layer(w2_packed, h_packed, tiles, first, HALF, name))
+        waiting_bank = second_layer(w2_packed, h_packed, range(2, 3), HALF, HALF, "y_bank3")
+        scalar_scatter(0, 0, y[:, 0, :HALF])
+        scalar_scatter(0, HALF, y[:, 0, HALF:])
+        scalar_scatter(1, 0, y[:, 1, :])
+        scalar_scatter(2, 0, y[:, 2, :HALF])
 
-        w1_0, w1_1, w1_2, w3_0, w3_1, w3_2 = chunks[0]
-        a_banks = first_layer_banks("a")
-        chunk(w1_0, 0, STAGE[2], a_banks)
-        chunk(w1_1, 0, STAGE[3], a_banks)
-        chunk(w1_2, P, STAGE[2], a_banks, codes_at=STAGE[0])
-        acts = silu_of(a_banks)
-        g_banks = first_layer_banks("g")
-        chunk(w3_0, P, STAGE[3], g_banks)
-        chunk(w3_1, 96, STAGE[0], g_banks)
-        chunk(w3_2, 84, STAGE[0], g_banks)
-        copy_w2(0, 0, 256, by_vector, CHUNKS_AT + 5 * CHUNK_BYTES)
-        copy_w2(0, 256, N, by_scalar, CHUNKS_AT + 5 * CHUNK_BYTES + 2 * KIB)
-        w1_0, w1_1, w1_2, w3_0, w3_1, w3_2 = chunks[1]
-        copy_chunk(w1_0, 0, FIRST_W2_AT, loads)
-        h = hidden(0, acts, g_banks)
-        quantise_w2(0, 0, 256, STAGE[1])
-        packed = [quantise_hidden(0, h, STAGE[0])]
-        quantise_w2(0, 256, N)
-        h = hidden(1, acts, g_banks)
-        y_banks = [psum.tile([P, N_TILES, HALF], F32, name=f"y_bank{half}") for half in range(2)]
-        for m in range(N_TILES):
-            second_layer_pass(y_banks[0][:, m, :], 0, m, packed[0])
-        y = placed(work, "y_first", [P, 2, HALF], F32, STAGE[2])
-        packed.append(quantise_hidden(1, h, STAGE[0] + KIB))
-        by_vector(y[:], y_banks[0][:, :2, :])
-        y_rest = placed(loads, "y_first_rest", [P, HALF], F32, CHUNKS_AT + 6 * CHUNK_BYTES + 2 * KIB)
-        scalar_take(y_rest[:], y_banks[0][:, 2, :])
-        for m in range(N_TILES):
-            second_layer_pass(y_banks[1][:, m, :], 0, m, packed[1])
+        a_banks, g_banks = first_layer_banks("a"), first_layer_banks("g")
+        first_layer_pass("a", 1, 0, a_banks, next_grouped)
+        for s in range(1, PASSES):
+            first_layer_pass("a", 1, s, a_banks, copy_chunk(w1_raw[1][s], SHARES[1][s]))
+        acts = []
+        for s in range(PASSES):
+            grouped = copy_chunk(w3_raw[1][s], SHARES[1][PASSES + s])
+            if s == PASSES - 1:
+                waiting = placed(loads, "y_waiting", [P, HALF], F32, s * CHUNK_BYTES + 2 * KIB)
+                nc.scalar.activation(waiting[:], waiting_bank[:, 0, :], COPY)
+            if s > 0:
+                acts.append(silu_of(a_banks[s - 1], s * CHUNK_BYTES))
+            first_layer_pass("g", 1, s, g_banks, grouped)
+        nc.vector.tensor_tensor(window_at(2, HALF, HALF), waiting[:], gates[:, HALF:C], MULT)
+        w2_packed = prepare_w2(w2_raw[1])
+        h_packed = hidden(acts, g_banks)
+        y = [kept(name, [P, 1, C], F32) for name in ("y_last0", "first_part", "y_last2")]
+        take_gated(y[0], 1, range(1), 0, second_layer(w2_packed, h_packed, range(1), 0, HALF, "y_bank0"))
+        take_gated(y[0], 1, range(1), HALF, second_layer(w2_packed, h_packed, range(1), HALF, HALF, "y_bank1"))
+        take_gated(y[1], 1, range(1), 0, second_layer(w2_packed, h_packed, range(1, 2), 0, C, "y_bank2"))
+        take_gated(y[2], 1, range(1), 0, second_layer(w2_packed, h_packed, range(2, 3), 0, C, "a_bank0"))
+        scalar_scatter(0, C, y[0][:, 0, :HALF])
+        scalar_scatter(0, C + HALF, y[0][:, 0, HALF:])
+        scalar_scatter(2, C, y[2][:, 0, :])
+        nc.vector.tensor_copy(window_at(1, C, C), y[1][:, 0, :])
 
-        a_banks = first_layer_banks("a")
-        scatter(0, 0, 0, HALF, y[:, 0, :])
-        scatter(1, 0, 0, HALF, y[:, 1, :])
-        scatter(2, 0, 0, HALF, y_rest[:])
-        quantise_chunk(w1_0, at=STAGE[2])
-        first_layer_pass(a_banks, w1_0)
-        y = placed(loads, "y_second", [P, 2, HALF], F32, CHUNKS_AT + 6 * CHUNK_BYTES)
-        scalar_take(y[:], y_banks[1][:, :2, :])
-        for m in range(2):
-            scatter(m, 0, HALF, HALF, y[:, m, :])
-        chunk(w1_1, 0, STAGE[0], a_banks)
-        chunk(w1_2, 0, STAGE[1], a_banks)
-        g_banks = first_layer_banks("g")
-        copy_chunk(w3_0, 0, STAGE[0])
-        copy_chunk(w3_1, 96, STAGE[1])
-        acts = silu_of(a_banks, TOKENS_AT + CHUNK_BYTES + 2 * KIB)
-        quantise_chunk(w3_0, at=TOKENS_AT + CHUNK_BYTES, pool=loads)
-        first_layer_pass(g_banks, w3_0)
-        quantise_chunk(w3_1)
-        first_layer_pass(g_banks, w3_1)
-        chunk(w3_2, 84, STAGE[0], g_banks)
-        y_rest = placed(loads, "y_second_rest", [P, HALF], F32, TOKENS_AT + 2 * CHUNK_BYTES + 4 * KIB)
-        scalar_take(y_rest[:], y_banks[1][:, 2, :])
-        scatter(2, 0, HALF, HALF, y_rest[:])
-
-        for m in range(N_TILES):
-            copy_w2(1, m * P, (m + 1) * P, by_scalar, TOKENS_AT + 2 * CHUNK_BYTES + m * KIB)
-        h = hidden(0, acts, g_banks)
-        quantise_w2(1, 0, P)
-        packed = [quantise_hidden(0, h)]
-        y_banks = [psum.tile([P, HALF], F32, name=f"y_bank{half}") for half in range(2)]
-        y_banks += [psum.tile([P, C], F32, name=f"y_bank{m + 1}") for m in range(1, N_TILES)]
-        y = [kept(f"y_last{half}", [P, HALF], F32) for half in range(2)] + [kept(f"y_last{m + 1}", [P, C], F32) for m in range(1, N_TILES)]
-        second_layer_pass(y_banks[0][:], 1, 0, packed[0])
-        scalar_take(y[0][:], y_banks[0][:])
-        h = hidden(1, acts, g_banks, TOKENS_AT + 2 * CHUNK_BYTES)
-        quantise_w2(1, P, 2 * P)
-        packed.append(quantise_hidden(1, h))
-        second_layer_pass(y_banks[1][:], 1, 0, packed[1])
-        scalar_take(y[1][:], y_banks[1][:])
-        scatter(0, 1, 0, HALF, y[0][:])
-        quantise_w2(1, 2 * P, N)
-        for m in range(1, N_TILES):
-            for half in range(2):
-                second_layer_pass(y_banks[m + 1][:, half * HALF : (half + 1) * HALF], 1, m, packed[half])
-            scalar_take(y[m + 1][:], y_banks[m + 1][:])
-        scatter(0, 1, HALF, HALF, y[1][:])
-        parts = ((0, 256), (256, 512), (512, T))
-        sums = [open_sum(0, a, b, name) for (a, b), name in zip(parts, ("a_bank0", "a_bank1", "g_bank0"))]
-        turned = [close_sum(0, a, b, bank) for (a, b), bank in zip(parts, sums)]
-        for (a, b), tile, name in zip(parts, turned, ("y_bank0", "y_bank1", "y_bank2")):
-            turn_back(0, a, b, tile, name)
-        scatter(1, 1, 0, C, y[2][:])
-        scatter(2, 1, 0, HALF, y[3][:, :HALF])
-        finish(1, (0, 768))
-        scatter(2, 1, HALF, HALF, y[3][:, HALF:])
-        finish(1, (768, T))
-        finish(2, (0, 512, 768, T))
+        sums = psum.tile([P, T_HALF], F32, name="a_bank0")
+        turn(sums, residual[0], T_HALF, True, False)
+        turn(sums, windows[0], T_HALF, False, True)
+        turned = kept("turned", [P, T_HALF], F32)
+        nc.scalar.activation(turned[:], sums[:], COPY)
+        back = psum.tile([P, T_HALF], F32, name="a_bank1")
+        turn(back, turned, 0, True, True)
+        result = kept("result", [P, T_HALF], F32)
+        nc.scalar.activation(result[:], back[:], COPY)
+        nc.scalar.dma_start(out[0:P, T_HALF:], result[:])
+        first_part = kept("first_part", [P, T_HALF], F32)
+        for a in (0, C):
+            finish(0, a, a + C, first_part[:, a : a + C])
+        for m, cuts in ((1, (0, 512, T)), (2, (0, 512, 768, T))):
+            for a, b in zip(cuts, cuts[1:]):
+                finish(m, a, b, residual[m][:, a:b])

@@ -30,11 +30,7 @@ TOKENS_BYTES, CHUNK_BYTES, W2_BYTES, RESIDUAL_BYTES = 16 * KIB, 8 * KIB, 6 * KIB
 CHUNKS_AT = PASSES * TOKENS_BYTES
 FIRST_W2_AT = CHUNKS_AT + 9 * CHUNK_BYTES
 
-SHARES = (
-    ((0, 0), (16, 0), (16, 16), (16, 16), (16, 8), (16, 6)),
-    ((0, 0), (16, 16), (16, 16), (0, 6), (0, 16), (16, 6)),
-)
-BLOCKS = H // 32
+SHARES = ((0, 64, 128, 128, 96, 84), (0, 128, 128, 24, 56, 84))
 
 FLOPS = 2 * SLOTS * (2 * K * H + H * N)
 BYTES = 4 * (K * T + 2 * N * T + E * (2 * K * H + H * N) + SLOTS) + 2 * P * SLOTS // 16
@@ -75,13 +71,6 @@ def tile_moe_res_glu_silu_kernel(tc, xT, xr, w1, w3, w2, gate, offs, out):
         def load_chunks(name, weight, e, at):
             return [load_rows(f"{name}_{e}_{s}", weight[e, s * K_PASS : (s + 1) * K_PASS, :], at + s * CHUNK_BYTES) for s in range(PASSES)]
 
-        def load_w2(e, at):
-            tile = placed(loads, f"w2_{e}", [P, PACK, N], F32, at)
-            rows = w2[e].rearrange("(g u r v) n -> u g r (v n)", u=2, r=8, v=2)
-            for u in range(2):
-                nc.sync.dma_start(tile[:, 2 * u : 2 * u + 2, :].rearrange("p v n -> p (v n)"), rows[u])
-            return tile
-
         def load_residual(m, at):
             tile = placed(loads, f"residual{m}", [P, T], F32, at)
             nc.sync.dma_start(tile[:], xr[m * P : (m + 1) * P, :])
@@ -118,20 +107,18 @@ def tile_moe_res_glu_silu_kernel(tc, xT, xr, w1, w3, w2, gate, offs, out):
 
         def copy_chunk(raw, share):
             grouped = stage.tile([P, H * PACK], BF16, name="grouped", align_bytes=64)
-            src = raw[:].rearrange("p j (g u q a v) -> p u g q j a v", u=2, q=4, a=2, v=2)
-            dst = grouped[:].rearrange("p (u v g q a j) -> p u g q j a v", u=2, v=2, q=4, a=2, j=PACK)
-            for u in range(2):
-                if share[u] > 0:
-                    by_vector(dst[:, u, : share[u]], src[:, u, : share[u]])
-                if share[u] < BLOCKS:
-                    by_scalar(dst[:, u, share[u] :], src[:, u, share[u] :])
+            src = raw[:].rearrange("p j (m t) -> p m j t", t=H_TILES)
+            dst = grouped[:].rearrange("p (t m j) -> p m j t", t=H_TILES, j=PACK)
+            if share > 0:
+                by_vector(dst[:, :share], src[:, :share])
+            if share < P:
+                by_scalar(dst[:, share:], src[:, share:])
             return grouped
 
         def first_layer_pass(name, e, s, banks, grouped):
             words = kept(f"{name}_words{s}", [P, H], U32)
             planes = kept(f"{name}_scales{s}", [P, H], U8)
-            for a in (0, H // 2):
-                quantise(words[:, a : a + H // 2], planes[:, a : a + H // 2], grouped[:, PACK * a : PACK * (a + H // 2)])
+            quantise(words[:], planes[:], grouped[:])
             for half in range(2):
                 slots = slice(e * C + half * HALF, e * C + (half + 1) * HALF)
                 for t in range(H_TILES):
@@ -182,23 +169,16 @@ def tile_moe_res_glu_silu_kernel(tc, xT, xr, w1, w3, w2, gate, offs, out):
                 )
             return bank
 
-        def take_gated(y, e, tiles, first, bank):
-            count = bank.shape[2]
-            cols = slice(first, first + count)
-            weights = gates[:, e * C + cols.start : e * C + cols.stop].unsqueeze(1).to_broadcast([P, len(tiles), count])
-            nc.vector.tensor_tensor(y[:, tiles.start : tiles.stop, cols], bank[:], weights, MULT)
+        def take_gated(values, e, first, bank):
+            slot = e * C + first
+            weights = gates[:, slot : slot + bank.shape[2]].unsqueeze(1).to_broadcast(list(bank.shape))
+            nc.vector.tensor_tensor(values[:], bank[:], weights, MULT)
 
         def window_at(m, slot, count):
             return windows[m][:].indirect(offsets[:, slot // 16 : (slot + count) // 16])
 
         def scalar_scatter(m, slot, values):
             nc.scalar.activation(window_at(m, slot, values.shape[1]), values, COPY)
-
-        def turn(bank, source, first, start, stop):
-            blocks = T_HALF // P
-            for b in range(blocks):
-                block = source[:, first + b * P : first + (b + 1) * P]
-                nc.tensor.matmul(bank[:, b * P : (b + 1) * P], block, identity[:], start=start and b == 0, stop=stop and b == blocks - 1, is_transpose=True)
 
         def finish(m, a, b, result):
             nc.vector.tensor_tensor(result, windows[m][:, a:b], residual[m][:, a:b], ADD)
@@ -213,7 +193,7 @@ def tile_moe_res_glu_silu_kernel(tc, xT, xr, w1, w3, w2, gate, offs, out):
                 nc.sync.dma_start(gate_column[:], gate[0].rearrange("(n r) -> n r", r=SLOTS // P))
         w1_raw = [load_chunks("w1", w1, 0, CHUNKS_AT)]
         w3_raw = [load_chunks("w3", w3, 0, CHUNKS_AT + 3 * CHUNK_BYTES)]
-        w2_raw = [load_w2(0, FIRST_W2_AT)]
+        w2_raw = [load_rows("w2_0", w2[0], FIRST_W2_AT)]
         w1_raw.append(load_chunks("w1", w1, 1, CHUNKS_AT + 6 * CHUNK_BYTES))
 
         gates = spread_gate(gate_column)
@@ -222,7 +202,7 @@ def tile_moe_res_glu_silu_kernel(tc, xT, xr, w1, w3, w2, gate, offs, out):
         nc.vector.tensor_copy(slot_scales[:], x_scales[:].indirect(offsets[:]))
 
         w3_raw.append(load_chunks("w3", w3, 1, 0))
-        w2_raw.append(load_w2(1, PASSES * CHUNK_BYTES))
+        w2_raw.append(load_rows("w2_1", w2[1], PASSES * CHUNK_BYTES))
         residual = {m: load_residual(m, 2 * TOKENS_BYTES + m * RESIDUAL_BYTES) for m in range(N_TILES)}
 
         a_banks, g_banks = first_layer_banks("a"), first_layer_banks("g")
@@ -237,7 +217,7 @@ def tile_moe_res_glu_silu_kernel(tc, xT, xr, w1, w3, w2, gate, offs, out):
         next_grouped = copy_chunk(w1_raw[1][0], SHARES[1][0])
         y = placed(loads, "y_first", [P, N_TILES, C], F32, next_w1_at)
         for tiles, first, name in ((range(1), 0, "y_bank0"), (range(1, 3), 0, "y_bank2"), (range(2), HALF, "y_bank1")):
-            take_gated(y, 0, tiles, first, second_layer(w2_packed, h_packed, tiles, first, HALF, name))
+            take_gated(y[:, tiles.start : tiles.stop, first : first + HALF], 0, first, second_layer(w2_packed, h_packed, tiles, first, HALF, name))
         waiting_bank = second_layer(w2_packed, h_packed, range(2, 3), HALF, HALF, "y_bank3")
         scalar_scatter(0, 0, y[:, 0, :HALF])
         scalar_scatter(0, HALF, y[:, 0, HALF:])
@@ -260,29 +240,18 @@ def tile_moe_res_glu_silu_kernel(tc, xT, xr, w1, w3, w2, gate, offs, out):
         nc.vector.tensor_tensor(window_at(2, HALF, HALF), waiting[:], gates[:, HALF:C], MULT)
         w2_packed = prepare_w2(w2_raw[1])
         h_packed = hidden(acts, g_banks)
-        y = [kept(name, [P, 1, C], F32) for name in ("y_last0", "first_part", "y_last2")]
-        take_gated(y[0], 1, range(1), 0, second_layer(w2_packed, h_packed, range(1), 0, HALF, "y_bank0"))
-        take_gated(y[0], 1, range(1), HALF, second_layer(w2_packed, h_packed, range(1), HALF, HALF, "y_bank1"))
-        take_gated(y[1], 1, range(1), 0, second_layer(w2_packed, h_packed, range(1, 2), 0, C, "y_bank2"))
-        take_gated(y[2], 1, range(1), 0, second_layer(w2_packed, h_packed, range(2, 3), 0, C, "a_bank0"))
-        scalar_scatter(0, C, y[0][:, 0, :HALF])
-        scalar_scatter(0, C + HALF, y[0][:, 0, HALF:])
-        scalar_scatter(2, C, y[2][:, 0, :])
-        nc.vector.tensor_copy(window_at(1, C, C), y[1][:, 0, :])
+        pieces = {}
+        for m, first, name, bank in ((0, 0, "y_a", "y_bank0"), (0, HALF, "y_b", "y_bank1"), (1, 0, "y_c", "y_bank2"), (1, HALF, "y_d", "y_bank3")):
+            pieces[m, first] = kept(name, [P, 1, HALF], F32)
+            take_gated(pieces[m, first], 1, first, second_layer(w2_packed, h_packed, range(m, m + 1), first, HALF, bank))
+        scalar_scatter(0, C, pieces[0, 0][:, 0, :])
+        scalar_scatter(0, C + HALF, pieces[0, HALF][:, 0, :])
+        nc.vector.tensor_copy(window_at(1, C, HALF), pieces[1, 0][:, 0, :])
+        scalar_scatter(1, C + HALF, pieces[1, HALF][:, 0, :])
+        last = kept("y_c", [P, 1, C], F32)
+        take_gated(last, 1, 0, second_layer(w2_packed, h_packed, range(2, 3), 0, C, "a_bank0"))
+        scalar_scatter(2, C, last[:, 0, :])
 
-        sums = psum.tile([P, T_HALF], F32, name="a_bank0")
-        turn(sums, residual[0], T_HALF, True, False)
-        turn(sums, windows[0], T_HALF, False, True)
-        turned = kept("turned", [P, T_HALF], F32)
-        nc.scalar.activation(turned[:], sums[:], COPY)
-        back = psum.tile([P, T_HALF], F32, name="a_bank1")
-        turn(back, turned, 0, True, True)
-        result = kept("result", [P, T_HALF], F32)
-        nc.scalar.activation(result[:], back[:], COPY)
-        nc.scalar.dma_start(out[0:P, T_HALF:], result[:])
-        first_part = kept("first_part", [P, T_HALF], F32)
-        for a in (0, C):
-            finish(0, a, a + C, first_part[:, a : a + C])
-        for m, cuts in ((1, (0, 512, T)), (2, (0, 512, 768, T))):
+        for m, cuts in ((0, (0, 256, 512, T)), (1, (0, 512, T)), (2, (0, 512, 768, T))):
             for a, b in zip(cuts, cuts[1:]):
                 finish(m, a, b, residual[m][:, a:b])

@@ -30,7 +30,7 @@ TOKENS_BYTES, CHUNK_BYTES, W2_BYTES, RESIDUAL_BYTES = 16 * KIB, 8 * KIB, 6 * KIB
 CHUNKS_AT = PASSES * TOKENS_BYTES
 FIRST_W2_AT = CHUNKS_AT + 9 * CHUNK_BYTES
 
-SHARES = ((0, 64, 128, 128, 96, 84), (0, 128, 128, 24, 56, 84))
+SHARES = ((0, 64, 128, 128, 96, 84), (0, 128, 128, 72, 56, 84))
 
 FLOPS = 2 * SLOTS * (2 * K * H + H * N)
 BYTES = 4 * (K * T + 2 * N * T + E * (2 * K * H + H * N) + SLOTS) + 2 * P * SLOTS // 16
@@ -109,8 +109,8 @@ def tile_moe_res_glu_silu_kernel(tc, xT, xr, w1, w3, w2, gate, offs, out):
             grouped = stage.tile([P, H * PACK], BF16, name="grouped", align_bytes=64)
             src = raw[:].rearrange("p j (m t) -> p m j t", t=H_TILES)
             dst = grouped[:].rearrange("p (t m j) -> p m j t", t=H_TILES, j=PACK)
-            if share > 0:
-                by_vector(dst[:, :share], src[:, :share])
+            for pair in range(0, H_TILES if share > 0 else 0, 2):
+                by_vector(dst[:, :share, :, pair : pair + 2], src[:, :share, :, pair : pair + 2])
             if share < P:
                 by_scalar(dst[:, share:], src[:, share:])
             return grouped
@@ -118,7 +118,8 @@ def tile_moe_res_glu_silu_kernel(tc, xT, xr, w1, w3, w2, gate, offs, out):
         def first_layer_pass(name, e, s, banks, grouped):
             words = kept(f"{name}_words{s}", [P, H], U32)
             planes = kept(f"{name}_scales{s}", [P, H], U8)
-            quantise(words[:], planes[:], grouped[:])
+            for a in (0, H // 2):
+                quantise(words[:, a : a + H // 2], planes[:, a : a + H // 2], grouped[:, PACK * a : PACK * (a + H // 2)])
             for half in range(2):
                 slots = slice(e * C + half * HALF, e * C + (half + 1) * HALF)
                 for t in range(H_TILES):
@@ -190,7 +191,7 @@ def tile_moe_res_glu_silu_kernel(tc, xT, xr, w1, w3, w2, gate, offs, out):
             if s == 0:
                 nc.sync.dma_start(offsets[:], offs)
                 gate_column = kept("gate_column", [P, SLOTS // P], F32)
-                nc.sync.dma_start(gate_column[:], gate[0].rearrange("(n r) -> n r", r=SLOTS // P))
+                nc.scalar.dma_start(gate_column[:], gate[0].rearrange("(n r) -> n r", r=SLOTS // P))
         w1_raw = [load_chunks("w1", w1, 0, CHUNKS_AT)]
         w3_raw = [load_chunks("w3", w3, 0, CHUNKS_AT + 3 * CHUNK_BYTES)]
         w2_raw = [load_rows("w2_0", w2[0], FIRST_W2_AT)]
@@ -216,28 +217,22 @@ def tile_moe_res_glu_silu_kernel(tc, xT, xr, w1, w3, w2, gate, offs, out):
         next_w1_at = CHUNKS_AT + 6 * CHUNK_BYTES
         next_grouped = copy_chunk(w1_raw[1][0], SHARES[1][0])
         y = placed(loads, "y_first", [P, N_TILES, C], F32, next_w1_at)
-        for tiles, first, name in ((range(1), 0, "y_bank0"), (range(1, 3), 0, "y_bank2"), (range(2), HALF, "y_bank1")):
+        for tiles, first, name in ((range(1), 0, "y_bank0"), (range(1, 3), 0, "y_bank2"), (range(3), HALF, "y_bank1")):
             take_gated(y[:, tiles.start : tiles.stop, first : first + HALF], 0, first, second_layer(w2_packed, h_packed, tiles, first, HALF, name))
-        waiting_bank = second_layer(w2_packed, h_packed, range(2, 3), HALF, HALF, "y_bank3")
         scalar_scatter(0, 0, y[:, 0, :HALF])
         scalar_scatter(0, HALF, y[:, 0, HALF:])
         scalar_scatter(1, 0, y[:, 1, :])
-        scalar_scatter(2, 0, y[:, 2, :HALF])
+        scalar_scatter(2, 0, y[:, 2, :])
 
         a_banks, g_banks = first_layer_banks("a"), first_layer_banks("g")
         first_layer_pass("a", 1, 0, a_banks, next_grouped)
         for s in range(1, PASSES):
             first_layer_pass("a", 1, s, a_banks, copy_chunk(w1_raw[1][s], SHARES[1][s]))
-        acts = []
         for s in range(PASSES):
             grouped = copy_chunk(w3_raw[1][s], SHARES[1][PASSES + s])
             if s == PASSES - 1:
-                waiting = placed(loads, "y_waiting", [P, HALF], F32, s * CHUNK_BYTES + 2 * KIB)
-                nc.scalar.activation(waiting[:], waiting_bank[:, 0, :], COPY)
-            if s > 0:
-                acts.append(silu_of(a_banks[s - 1], s * CHUNK_BYTES))
+                acts = [silu_of(a_banks[half], s * CHUNK_BYTES + 2 * KIB * half) for half in range(2)]
             first_layer_pass("g", 1, s, g_banks, grouped)
-        nc.vector.tensor_tensor(window_at(2, HALF, HALF), waiting[:], gates[:, HALF:C], MULT)
         w2_packed = prepare_w2(w2_raw[1])
         h_packed = hidden(acts, g_banks)
         pieces = {}

@@ -30,7 +30,7 @@ TOKENS_BYTES, CHUNK_BYTES, W2_BYTES, RESIDUAL_BYTES = 16 * KIB, 8 * KIB, 6 * KIB
 CHUNKS_AT = PASSES * TOKENS_BYTES
 FIRST_W2_AT = CHUNKS_AT + 9 * CHUNK_BYTES
 
-SHARES = ((0, 64, 128, 128, 96, 84), (0, 128, 128, 72, 56, 84))
+SHARES = ((0, 64, 128, 128, 96, 84), (72, 128, 128, 48, 64, 84))
 
 FLOPS = 2 * SLOTS * (2 * K * H + H * N)
 BYTES = 4 * (K * T + 2 * N * T + E * (2 * K * H + H * N) + SLOTS) + 2 * P * SLOTS // 16
@@ -122,7 +122,8 @@ def tile_moe_res_glu_silu_kernel(tc, xT, xr, w1, w3, w2, gate, offs, out):
                 quantise(words[:, a : a + H // 2], planes[:, a : a + H // 2], grouped[:, PACK * a : PACK * (a + H // 2)])
             for half in range(2):
                 slots = slice(e * C + half * HALF, e * C + (half + 1) * HALF)
-                for t in range(H_TILES):
+                order = [(t + 2 * half) % H_TILES for t in range(H_TILES)]
+                for t in order:
                     channels = slice(t * P, (t + 1) * P)
                     nc.tensor.matmul_mx(
                         out=banks[half][:, t, :],
@@ -130,8 +131,8 @@ def tile_moe_res_glu_silu_kernel(tc, xT, xr, w1, w3, w2, gate, offs, out):
                         lhsT_scale=planes[:, channels],
                         rhs=slot_words[s][:, slots].bitcast(FP8X4),
                         rhs_scale=slot_scales[4 * s : P, slots],
-                        start=(s == 0 and t == 0),
-                        stop=(s == PASSES - 1 and t == H_TILES - 1),
+                        start=(s == 0 and t == order[0]),
+                        stop=(s == PASSES - 1 and t == order[-1]),
                     )
 
         def silu_of(bank, at):
@@ -183,7 +184,7 @@ def tile_moe_res_glu_silu_kernel(tc, xT, xr, w1, w3, w2, gate, offs, out):
 
         def finish(m, a, b, result):
             nc.vector.tensor_tensor(result, windows[m][:, a:b], residual[m][:, a:b], ADD)
-            nc.sync.dma_start(out[m * P : (m + 1) * P, a:b], result)
+            (nc.scalar if (m, a) == (2, 512) else nc.sync).dma_start(out[m * P : (m + 1) * P, a:b], result)
 
         tokens = []
         for s in range(PASSES):
@@ -228,22 +229,23 @@ def tile_moe_res_glu_silu_kernel(tc, xT, xr, w1, w3, w2, gate, offs, out):
         first_layer_pass("a", 1, 0, a_banks, next_grouped)
         for s in range(1, PASSES):
             first_layer_pass("a", 1, s, a_banks, copy_chunk(w1_raw[1][s], SHARES[1][s]))
+        acts = []
         for s in range(PASSES):
             grouped = copy_chunk(w3_raw[1][s], SHARES[1][PASSES + s])
-            if s == PASSES - 1:
-                acts = [silu_of(a_banks[half], s * CHUNK_BYTES + 2 * KIB * half) for half in range(2)]
+            if s != 1:
+                acts.append(silu_of(a_banks[s // 2], s * CHUNK_BYTES))
             first_layer_pass("g", 1, s, g_banks, grouped)
         w2_packed = prepare_w2(w2_raw[1])
         h_packed = hidden(acts, g_banks)
         pieces = {}
-        for m, first, name, bank in ((0, 0, "y_a", "y_bank0"), (0, HALF, "y_b", "y_bank1"), (1, 0, "y_c", "y_bank2"), (1, HALF, "y_d", "y_bank3")):
+        for m, first, name, bank in ((0, 0, "y_a", "y_bank0"), (1, 0, "y_c", "y_bank2"), (0, HALF, "y_b", "y_bank1"), (1, HALF, "y_d", "y_bank3")):
             pieces[m, first] = kept(name, [P, 1, HALF], F32)
             take_gated(pieces[m, first], 1, first, second_layer(w2_packed, h_packed, range(m, m + 1), first, HALF, bank))
         scalar_scatter(0, C, pieces[0, 0][:, 0, :])
         scalar_scatter(0, C + HALF, pieces[0, HALF][:, 0, :])
         nc.vector.tensor_copy(window_at(1, C, HALF), pieces[1, 0][:, 0, :])
         scalar_scatter(1, C + HALF, pieces[1, HALF][:, 0, :])
-        last = kept("y_c", [P, 1, C], F32)
+        last = kept("y_e", [P, 1, C], F32)
         take_gated(last, 1, 0, second_layer(w2_packed, h_packed, range(2, 3), 0, C, "a_bank0"))
         scalar_scatter(2, C, last[:, 0, :])
 

@@ -140,33 +140,31 @@ def tile_moe_res_glu_silu_kernel(tc, xT, xr, w1, w3, w2, gate, offs, out):
             nc.scalar.activation(act[:], bank[:].rearrange("p t n -> p n t"), SILU)
             return act
 
-        def prepare_w2(raw):
-            grouped = [kept(f"w2_grouped{m}", [P, P * PACK], BF16) for m in range(N_TILES)]
-            for m in range(N_TILES):
-                interleave(by_scalar, grouped[m][:], raw, m * P, (m + 1) * P)
-            words = [kept(f"w2_words{m}", [P, P], U32) for m in range(N_TILES)]
-            planes = [kept(f"w2_scales{m}", [P, P], U8) for m in range(N_TILES)]
-            for m in range(N_TILES):
-                quantise(words[m][:], planes[m][:], grouped[m][:])
+        def prepare_w2(m, raw, first):
+            grouped = kept(f"w2_grouped{m}", [P, P * PACK], BF16)
+            interleave(by_scalar, grouped[:], raw, first, first + P)
+            words = kept(f"w2_words{m}", [P, P], U32)
+            planes = kept(f"w2_scales{m}", [P, P], U8)
+            quantise(words[:], planes[:], grouped[:])
             return words, planes
 
-        def hidden(acts, g_banks):
-            words = kept("h_words", [P, C], U32)
-            planes = kept("h_scales", [P, C], U8)
-            h = [kept(f"h{half}", [P, HALF * H_TILES], BF16) for half in range(2)]
-            for half in range(2):
-                nc.vector.tensor_tensor(h[half][:].rearrange("p (n t) -> p n t", t=H_TILES), g_banks[half][:].rearrange("p t n -> p n t"), acts[half][:], MULT)
-            for half in range(2):
-                cols = slice(half * HALF, (half + 1) * HALF)
-                quantise(words[:, cols], planes[:, cols], h[half][:])
-            return words, planes
+        def hidden(name, acts, g_banks, first, count):
+            half, a = divmod(first, HALF)
+            h = kept(name, [P, count * H_TILES], BF16)
+            sums = g_banks[half][:, :, a : a + count].rearrange("p t n -> p n t")
+            nc.vector.tensor_tensor(h[:].rearrange("p (n t) -> p n t", t=H_TILES), sums, acts[half][:, a : a + count, :], MULT)
+            return h
+
+        def quantise_hidden(h_packed, h, first):
+            cols = slice(first, first + h.shape[1] // H_TILES)
+            quantise(h_packed[0][:, cols], h_packed[1][:, cols], h[:])
 
         def second_layer(w2_packed, h_packed, tiles, first, count, bank_name):
             cols = slice(first, first + count)
             bank = psum.tile([P, len(tiles), count], F32, name=bank_name)
             for n, m in enumerate(tiles):
                 nc.tensor.matmul_mx(
-                    out=bank[:, n, :], lhsT=w2_packed[0][m][:].bitcast(FP8X4), lhsT_scale=w2_packed[1][m][:],
+                    out=bank[:, n, :], lhsT=w2_packed[m][0][:].bitcast(FP8X4), lhsT_scale=w2_packed[m][1][:],
                     rhs=h_packed[0][:, cols].bitcast(FP8X4), rhs_scale=h_packed[1][:, cols], start=True, stop=True,
                 )
             return bank
@@ -184,7 +182,7 @@ def tile_moe_res_glu_silu_kernel(tc, xT, xr, w1, w3, w2, gate, offs, out):
 
         def finish(m, a, b, result):
             nc.vector.tensor_tensor(result, windows[m][:, a:b], residual[m][:, a:b], ADD)
-            (nc.scalar if (m, a) == (2, 512) else nc.sync).dma_start(out[m * P : (m + 1) * P, a:b], result)
+            nc.sync.dma_start(out[m * P : (m + 1) * P, a:b], result)
 
         tokens = []
         for s in range(PASSES):
@@ -204,7 +202,9 @@ def tile_moe_res_glu_silu_kernel(tc, xT, xr, w1, w3, w2, gate, offs, out):
         nc.vector.tensor_copy(slot_scales[:], x_scales[:].indirect(offsets[:]))
 
         w3_raw.append(load_chunks("w3", w3, 1, 0))
-        w2_raw.append(load_rows("w2_1", w2[1], PASSES * CHUNK_BYTES))
+        last_w2_at = PASSES * CHUNK_BYTES
+        w2_first = load_rows("w2_first", w2[1, :, :P], last_w2_at)
+        w2_rest = load_rows("w2_rest", w2[1, :, P:], last_w2_at + 2 * KIB)
         residual = {m: load_residual(m, 2 * TOKENS_BYTES + m * RESIDUAL_BYTES) for m in range(N_TILES)}
 
         a_banks, g_banks = first_layer_banks("a"), first_layer_banks("g")
@@ -213,8 +213,11 @@ def tile_moe_res_glu_silu_kernel(tc, xT, xr, w1, w3, w2, gate, offs, out):
         acts = [silu_of(a_banks[half], CHUNKS_AT + 2 * KIB * half) for half in range(2)]
         for s in range(PASSES):
             first_layer_pass("g", 0, s, g_banks, copy_chunk(w3_raw[0][s], SHARES[0][PASSES + s]))
-        w2_packed = prepare_w2(w2_raw[0])
-        h_packed = hidden(acts, g_banks)
+        w2_packed = [prepare_w2(m, w2_raw[0], m * P) for m in range(N_TILES)]
+        h_packed = kept("h_words", [P, C], U32), kept("h_scales", [P, C], U8)
+        h = [hidden(f"h{half}", acts, g_banks, half * HALF, HALF) for half in range(2)]
+        for half in range(2):
+            quantise_hidden(h_packed, h[half], half * HALF)
         next_w1_at = CHUNKS_AT + 6 * CHUNK_BYTES
         next_grouped = copy_chunk(w1_raw[1][0], SHARES[1][0])
         y = placed(loads, "y_first", [P, N_TILES, C], F32, next_w1_at)
@@ -232,11 +235,19 @@ def tile_moe_res_glu_silu_kernel(tc, xT, xr, w1, w3, w2, gate, offs, out):
         acts = []
         for s in range(PASSES):
             grouped = copy_chunk(w3_raw[1][s], SHARES[1][PASSES + s])
-            if s != 1:
-                acts.append(silu_of(a_banks[s // 2], s * CHUNK_BYTES))
+            if s == 0:
+                acts.append(silu_of(a_banks[0], 0))
             first_layer_pass("g", 1, s, g_banks, grouped)
-        w2_packed = prepare_w2(w2_raw[1])
-        h_packed = hidden(acts, g_banks)
+        w2_packed = [prepare_w2(0, w2_first, 0)]
+        acts.append(silu_of(a_banks[1], last_w2_at))
+        h_packed = kept("h_words", [P, C], U32), kept("h_scales", [P, C], U8)
+        quarter = HALF // 2
+        h = [hidden("h0", acts, g_banks, 0, HALF), hidden("h1", acts, g_banks, HALF, quarter)]
+        quantise_hidden(h_packed, h[0], 0)
+        quantise_hidden(h_packed, h[1], HALF)
+        w2_packed += [prepare_w2(m, w2_rest, (m - 1) * P) for m in range(1, N_TILES)]
+        h.append(hidden("h0", acts, g_banks, HALF + quarter, quarter))
+        quantise_hidden(h_packed, h[2], HALF + quarter)
         pieces = {}
         for m, first, name, bank in ((0, 0, "y_a", "y_bank0"), (1, 0, "y_c", "y_bank2"), (0, HALF, "y_b", "y_bank1"), (1, HALF, "y_d", "y_bank3")):
             pieces[m, first] = kept(name, [P, 1, HALF], F32)
@@ -249,6 +260,6 @@ def tile_moe_res_glu_silu_kernel(tc, xT, xr, w1, w3, w2, gate, offs, out):
         take_gated(last, 1, 0, second_layer(w2_packed, h_packed, range(2, 3), 0, C, "a_bank0"))
         scalar_scatter(2, C, last[:, 0, :])
 
-        for m, cuts in ((0, (0, 256, 512, T)), (1, (0, 512, T)), (2, (0, 512, 768, T))):
+        for m, cuts in ((0, (0, 256, 640, T)), (1, (0, 512, T)), (2, (0, 512, T))):
             for a, b in zip(cuts, cuts[1:]):
                 finish(m, a, b, residual[m][:, a:b])

@@ -30,7 +30,7 @@ TOKENS_BYTES, CHUNK_BYTES, W2_BYTES, RESIDUAL_BYTES = 16 * KIB, 8 * KIB, 6 * KIB
 CHUNKS_AT = PASSES * TOKENS_BYTES
 FIRST_W2_AT = CHUNKS_AT + 9 * CHUNK_BYTES
 
-SHARES = ((0, 64, 128, 128, 96, 84), (72, 128, 128, 48, 64, 84))
+SHARES = ((0, 64, 128, 128, 96, 84), (72, 128, 128, 48, 92, 84))
 
 FLOPS = 2 * SLOTS * (2 * K * H + H * N)
 BYTES = 4 * (K * T + 2 * N * T + E * (2 * K * H + H * N) + SLOTS) + 2 * P * SLOTS // 16
@@ -232,14 +232,12 @@ def tile_moe_res_glu_silu_kernel(tc, xT, xr, w1, w3, w2, gate, offs, out):
         first_layer_pass("a", 1, 0, a_banks, next_grouped)
         for s in range(1, PASSES):
             first_layer_pass("a", 1, s, a_banks, copy_chunk(w1_raw[1][s], SHARES[1][s]))
-        acts = []
         for s in range(PASSES):
             grouped = copy_chunk(w3_raw[1][s], SHARES[1][PASSES + s])
             if s == 0:
-                acts.append(silu_of(a_banks[0], 0))
+                acts = [silu_of(a_banks[half], 2 * KIB * half) for half in range(2)]
             first_layer_pass("g", 1, s, g_banks, grouped)
         w2_packed = [prepare_w2(0, w2_first, 0)]
-        acts.append(silu_of(a_banks[1], last_w2_at))
         h_packed = kept("h_words", [P, C], U32), kept("h_scales", [P, C], U8)
         quarter = HALF // 2
         h = [hidden("h0", acts, g_banks, 0, HALF), hidden("h1", acts, g_banks, HALF, quarter)]

@@ -30,7 +30,9 @@ TOKENS_BYTES, CHUNK_BYTES, W2_BYTES, RESIDUAL_BYTES = 16 * KIB, 8 * KIB, 6 * KIB
 CHUNKS_AT = PASSES * TOKENS_BYTES
 FIRST_W2_AT = CHUNKS_AT + 9 * CHUNK_BYTES
 
-SHARES = ((0, 64, 128, 128, 96, 84), (72, 128, 128, 48, 92, 84))
+SHARES = ((0, 64, 128, 128, 96, 84), (72, 128, 128, 64, 92))
+PIECE = P // 2
+PIECE_SHARES = (28, 36)
 
 FLOPS = 2 * SLOTS * (2 * K * H + H * N)
 BYTES = 4 * (K * T + 2 * N * T + E * (2 * K * H + H * N) + SLOTS) + 2 * P * SLOTS // 16
@@ -135,14 +137,44 @@ def tile_moe_res_glu_silu_kernel(tc, xT, xr, w1, w3, w2, gate, offs, out):
                         stop=(s == PASSES - 1 and t == order[-1]),
                     )
 
+        def last_pass(e, banks, pieces):
+            s = PASSES - 1
+            words = kept("last_words", [P, H], U32)
+            planes = kept("last_scales", [P, H], U8)
+            for n, raw in enumerate(pieces):
+                share = PIECE_SHARES[n]
+                grouped = kept(f"piece_grouped{n}", [P, H_TILES, PIECE * PACK], BF16)
+                src = raw[:].rearrange("p j (m t) -> p m j t", t=H_TILES)
+                dst = grouped[:].rearrange("p t (m j) -> p m j t", j=PACK)
+                for pair in range(0, H_TILES, 2):
+                    by_vector(dst[:, :share, :, pair : pair + 2], src[:, :share, :, pair : pair + 2])
+                by_scalar(dst[:, share:], src[:, share:])
+                for t in range(H_TILES):
+                    cols = slice(t * P + n * PIECE, t * P + (n + 1) * PIECE)
+                    quantise(words[:, cols], planes[:, cols], grouped[:, t, :])
+            for half in range(2):
+                slots = slice(e * C + half * HALF, e * C + (half + 1) * HALF)
+                order = list(range(H_TILES)) if half == 0 else list(reversed(range(H_TILES)))
+                for t in order:
+                    channels = slice(t * P, (t + 1) * P)
+                    nc.tensor.matmul_mx(
+                        out=banks[half][:, t, :],
+                        lhsT=words[:, channels].bitcast(FP8X4),
+                        lhsT_scale=planes[:, channels],
+                        rhs=slot_words[s][:, slots].bitcast(FP8X4),
+                        rhs_scale=slot_scales[4 * s : P, slots],
+                        start=False,
+                        stop=(t == order[-1]),
+                    )
+
         def silu_of(bank, at):
             act = placed(loads, f"act{at}", [P, HALF, H_TILES], F32, at)
             nc.scalar.activation(act[:], bank[:].rearrange("p t n -> p n t"), SILU)
             return act
 
-        def prepare_w2(m, raw, first):
+        def prepare_w2(m, raw, first, copy=by_scalar):
             grouped = kept(f"w2_grouped{m}", [P, P * PACK], BF16)
-            interleave(by_scalar, grouped[:], raw, first, first + P)
+            interleave(copy, grouped[:], raw, first, first + P)
             words = kept(f"w2_words{m}", [P, P], U32)
             planes = kept(f"w2_scales{m}", [P, P], U8)
             quantise(words[:], planes[:], grouped[:])
@@ -201,10 +233,12 @@ def tile_moe_res_glu_silu_kernel(tc, xT, xr, w1, w3, w2, gate, offs, out):
             token_pass(s, tokens[s])
         nc.vector.tensor_copy(slot_scales[:], x_scales[:].indirect(offsets[:]))
 
-        w3_raw.append(load_chunks("w3", w3, 1, 0))
+        w3_raw.append([load_rows(f"w3_1_{s}", w3[1, s * K_PASS : (s + 1) * K_PASS, :], s * CHUNK_BYTES) for s in range(PASSES - 1)])
+        last_rows = w3[1, (PASSES - 1) * K_PASS :, :]
+        last_at = (PASSES - 1) * CHUNK_BYTES
+        last_pieces = [load_rows(f"w3_last{n}", last_rows[:, n * H // 2 : (n + 1) * H // 2], last_at + n * CHUNK_BYTES // 2) for n in range(2)]
         last_w2_at = PASSES * CHUNK_BYTES
-        w2_first = load_rows("w2_first", w2[1, :, :P], last_w2_at)
-        w2_rest = load_rows("w2_rest", w2[1, :, P:], last_w2_at + 2 * KIB)
+        w2_tiles = [load_rows(f"w2_tile{m}", w2[1, :, m * P : (m + 1) * P], last_w2_at + m * 2 * KIB) for m in range(N_TILES)]
         residual = {m: load_residual(m, 2 * TOKENS_BYTES + m * RESIDUAL_BYTES) for m in range(N_TILES)}
 
         a_banks, g_banks = first_layer_banks("a"), first_layer_banks("g")
@@ -232,32 +266,41 @@ def tile_moe_res_glu_silu_kernel(tc, xT, xr, w1, w3, w2, gate, offs, out):
         first_layer_pass("a", 1, 0, a_banks, next_grouped)
         for s in range(1, PASSES):
             first_layer_pass("a", 1, s, a_banks, copy_chunk(w1_raw[1][s], SHARES[1][s]))
-        for s in range(PASSES):
+        for s in range(PASSES - 1):
             grouped = copy_chunk(w3_raw[1][s], SHARES[1][PASSES + s])
             if s == 0:
-                acts = [silu_of(a_banks[half], 2 * KIB * half) for half in range(2)]
+                acts = [silu_of(a_banks[0], 0)]
             first_layer_pass("g", 1, s, g_banks, grouped)
-        w2_packed = [prepare_w2(0, w2_first, 0)]
+        last_pass(1, g_banks, last_pieces)
+        acts.append(silu_of(a_banks[1], last_at + CHUNK_BYTES // 2))
         h_packed = kept("h_words", [P, C], U32), kept("h_scales", [P, C], U8)
+        pieces = {}
+
+        def take(m, first, count, name, bank):
+            pieces[m, first] = kept(name, [P, 1, count], F32)
+            take_gated(pieces[m, first], 1, first, second_layer(w2_packed, h_packed, range(m, m + 1), first, count, bank))
+
+        w2_packed = [prepare_w2(0, w2_tiles[0], 0, by_vector)]
         quarter = HALF // 2
         h = [hidden("h0", acts, g_banks, 0, HALF), hidden("h1", acts, g_banks, HALF, quarter)]
         quantise_hidden(h_packed, h[0], 0)
         quantise_hidden(h_packed, h[1], HALF)
-        w2_packed += [prepare_w2(m, w2_rest, (m - 1) * P) for m in range(1, N_TILES)]
         h.append(hidden("h0", acts, g_banks, HALF + quarter, quarter))
+        w2_packed.append(prepare_w2(1, w2_tiles[1], 0))
         quantise_hidden(h_packed, h[2], HALF + quarter)
-        pieces = {}
-        for m, first, name, bank in ((0, 0, "y_a", "y_bank0"), (1, 0, "y_c", "y_bank2"), (0, HALF, "y_b", "y_bank1"), (1, HALF, "y_d", "y_bank3")):
-            pieces[m, first] = kept(name, [P, 1, HALF], F32)
-            take_gated(pieces[m, first], 1, first, second_layer(w2_packed, h_packed, range(m, m + 1), first, HALF, bank))
+        take(0, 0, HALF, "y_a", "y_bank0")
         scalar_scatter(0, C, pieces[0, 0][:, 0, :])
+        w2_packed.append(prepare_w2(2, w2_tiles[2], 0))
+        take(1, 0, HALF, "y_c", "y_bank2")
+        take(0, HALF, HALF, "y_b", "y_bank1")
         scalar_scatter(0, C + HALF, pieces[0, HALF][:, 0, :])
         nc.vector.tensor_copy(window_at(1, C, HALF), pieces[1, 0][:, 0, :])
+        take(1, HALF, HALF, "y_d", "y_bank3")
         scalar_scatter(1, C + HALF, pieces[1, HALF][:, 0, :])
-        last = kept("y_e", [P, 1, C], F32)
-        take_gated(last, 1, 0, second_layer(w2_packed, h_packed, range(2, 3), 0, C, "a_bank0"))
-        scalar_scatter(2, C, last[:, 0, :])
+        finish(0, 0, 256, residual[0][:, 0:256])
+        take(2, 0, C, "y_e", "a_bank0")
+        scalar_scatter(2, C, pieces[2, 0][:, 0, :])
 
-        for m, cuts in ((0, (0, 256, 640, T)), (1, (0, 512, T)), (2, (0, 512, T))):
+        for m, cuts in ((0, (256, 640, T)), (1, (0, 512, T)), (2, (0, 512, T))):
             for a, b in zip(cuts, cuts[1:]):
                 finish(m, a, b, residual[m][:, a:b])

@@ -30,7 +30,7 @@ TOKENS_BYTES, CHUNK_BYTES, W2_BYTES, RESIDUAL_BYTES = 16 * KIB, 8 * KIB, 6 * KIB
 CHUNKS_AT = PASSES * TOKENS_BYTES
 FIRST_W2_AT = CHUNKS_AT + 9 * CHUNK_BYTES
 
-SHARES = ((0, 64, 128, 128, 96, 84), (72, 128, 128, 64, 92))
+SHARES = ((0, 52, 64, 84, 84, 84), (72, 128, 128, 64, 92))
 PIECE = P // 2
 PIECE_SHARES = (28, 36)
 
@@ -56,10 +56,10 @@ def tile_moe_res_glu_silu_kernel(tc, xT, xr, w1, w3, w2, gate, offs, out):
         offsets = keep.tile([P, SLOTS // 16], U16, name="offsets")
         x_words = [kept(f"x_words{s}", [P, T], U32) for s in range(PASSES)]
         x_scales = kept("x_scales", [P, T], U8)
-        nc.vector.memset(x_scales[:].bitcast(U32), 0)
+        nc.gpsimd.memset(x_scales[:].bitcast(U32), 0)
         windows = [kept(f"window{m}", [P, T], F32) for m in range(N_TILES)]
         for m in range(N_TILES):
-            nc.vector.memset(windows[m][:], 0.0)
+            nc.gpsimd.memset(windows[m][:], 0.0)
         identity = kept("identity", [P, P], F32)
         make_identity(nc, identity[:])
         slot_words = [kept(f"slot_words{s}", [P, SLOTS], U32) for s in range(PASSES)]
@@ -107,21 +107,21 @@ def tile_moe_res_glu_silu_kernel(tc, xT, xr, w1, w3, w2, gate, offs, out):
         def first_layer_banks(name):
             return [psum.tile([P, H_TILES, HALF], F32, name=f"{name}_bank{half}") for half in range(2)]
 
-        def copy_chunk(raw, share):
+        def copy_chunk(raw, share, tiles=2):
             grouped = stage.tile([P, H * PACK], BF16, name="grouped", align_bytes=64)
             src = raw[:].rearrange("p j (m t) -> p m j t", t=H_TILES)
             dst = grouped[:].rearrange("p (t m j) -> p m j t", t=H_TILES, j=PACK)
-            for pair in range(0, H_TILES if share > 0 else 0, 2):
-                by_vector(dst[:, :share, :, pair : pair + 2], src[:, :share, :, pair : pair + 2])
+            for first in range(0, H_TILES if share > 0 else 0, tiles):
+                by_vector(dst[:, :share, :, first : first + tiles], src[:, :share, :, first : first + tiles])
             if share < P:
                 by_scalar(dst[:, share:], src[:, share:])
             return grouped
 
-        def first_layer_pass(name, e, s, banks, grouped):
+        def first_layer_pass(name, e, s, banks, grouped, width=H // 2):
             words = kept(f"{name}_words{s}", [P, H], U32)
             planes = kept(f"{name}_scales{s}", [P, H], U8)
-            for a in (0, H // 2):
-                quantise(words[:, a : a + H // 2], planes[:, a : a + H // 2], grouped[:, PACK * a : PACK * (a + H // 2)])
+            for a in range(0, H, width):
+                quantise(words[:, a : a + width], planes[:, a : a + width], grouped[:, PACK * a : PACK * (a + width)])
             for half in range(2):
                 slots = slice(e * C + half * HALF, e * C + (half + 1) * HALF)
                 order = [(t + 2 * half) % H_TILES for t in range(H_TILES)]
@@ -228,6 +228,8 @@ def tile_moe_res_glu_silu_kernel(tc, xT, xr, w1, w3, w2, gate, offs, out):
         w2_raw = [load_rows("w2_0", w2[0], FIRST_W2_AT)]
         w1_raw.append(load_chunks("w1", w1, 1, CHUNKS_AT + 6 * CHUNK_BYTES))
 
+        warm = kept("warm", [P, 1], F32)
+        nc.scalar.activation(warm[:], identity[:, 0:1], SILU)
         gates = spread_gate(gate_column)
         for s in range(PASSES):
             token_pass(s, tokens[s])
@@ -243,10 +245,13 @@ def tile_moe_res_glu_silu_kernel(tc, xT, xr, w1, w3, w2, gate, offs, out):
 
         a_banks, g_banks = first_layer_banks("a"), first_layer_banks("g")
         for s in range(PASSES):
-            first_layer_pass("a", 0, s, a_banks, copy_chunk(w1_raw[0][s], SHARES[0][s]))
-        acts = [silu_of(a_banks[half], CHUNKS_AT + 2 * KIB * half) for half in range(2)]
-        for s in range(PASSES):
-            first_layer_pass("g", 0, s, g_banks, copy_chunk(w3_raw[0][s], SHARES[0][PASSES + s]))
+            first_layer_pass("a", 0, s, a_banks, copy_chunk(w1_raw[0][s], SHARES[0][s], H_TILES), H)
+        for s in range(PASSES - 1):
+            grouped = copy_chunk(w3_raw[0][s], SHARES[0][PASSES + s], H_TILES)
+            if s == 0:
+                acts = [silu_of(a_banks[half], CHUNKS_AT + 3 * CHUNK_BYTES + 2 * KIB * half) for half in range(2)]
+            first_layer_pass("g", 0, s, g_banks, grouped, H)
+        first_layer_pass("g", 0, PASSES - 1, g_banks, copy_chunk(w3_raw[0][-1], SHARES[0][-1]))
         w2_packed = [prepare_w2(m, w2_raw[0], m * P) for m in range(N_TILES)]
         h_packed = kept("h_words", [P, C], U32), kept("h_scales", [P, C], U8)
         h = [hidden(f"h{half}", acts, g_banks, half * HALF, HALF) for half in range(2)]
@@ -289,8 +294,8 @@ def tile_moe_res_glu_silu_kernel(tc, xT, xr, w1, w3, w2, gate, offs, out):
         w2_packed.append(prepare_w2(1, w2_tiles[1], 0))
         quantise_hidden(h_packed, h[2], HALF + quarter)
         take(0, 0, HALF, "y_a", "y_bank0")
-        scalar_scatter(0, C, pieces[0, 0][:, 0, :])
         w2_packed.append(prepare_w2(2, w2_tiles[2], 0))
+        scalar_scatter(0, C, pieces[0, 0][:, 0, :])
         take(1, 0, HALF, "y_c", "y_bank2")
         take(0, HALF, HALF, "y_b", "y_bank1")
         scalar_scatter(0, C + HALF, pieces[0, HALF][:, 0, :])

@@ -73,10 +73,10 @@ def tile_moe_res_glu_silu_kernel(tc, xT, xr, w1, w3, w2, gate, offs, out):
         def load_chunks(name, weight, e, at):
             return [load_rows(f"{name}_{e}_{s}", weight[e, s * K_PASS : (s + 1) * K_PASS, :], at + s * CHUNK_BYTES) for s in range(PASSES)]
 
-        def load_residual(m, at):
-            tile = placed(loads, f"residual{m}", [P, T], F32, at)
-            nc.sync.dma_start(tile[:], xr[m * P : (m + 1) * P, :])
-            return tile
+        def load_residual(first, tiles, at):
+            tile = placed(loads, f"residual{first}", [P, tiles, T], F32, at)
+            nc.sync.dma_start(tile[:], xr[first * P : (first + tiles) * P, :].rearrange("(m p) t -> p m t", p=P))
+            return [tile[:, n, :] for n in range(tiles)]
 
         def spread_gate(column):
             bank = psum.tile([P, SLOTS // P, P], F32, name="y_bank3")
@@ -204,7 +204,7 @@ def tile_moe_res_glu_silu_kernel(tc, xT, xr, w1, w3, w2, gate, offs, out):
         def take_gated(values, e, first, bank):
             slot = e * C + first
             weights = gates[:, slot : slot + bank.shape[2]].unsqueeze(1).to_broadcast(list(bank.shape))
-            nc.vector.tensor_tensor(values[:], bank[:], weights, MULT)
+            nc.vector.tensor_tensor(values, bank[:], weights, MULT)
 
         def window_at(m, slot, count):
             return windows[m][:].indirect(offsets[:, slot // 16 : (slot + count) // 16])
@@ -241,7 +241,7 @@ def tile_moe_res_glu_silu_kernel(tc, xT, xr, w1, w3, w2, gate, offs, out):
         last_pieces = [load_rows(f"w3_last{n}", last_rows[:, n * H // 2 : (n + 1) * H // 2], last_at + n * CHUNK_BYTES // 2) for n in range(2)]
         last_w2_at = PASSES * CHUNK_BYTES
         w2_tiles = [load_rows(f"w2_tile{m}", w2[1, :, m * P : (m + 1) * P], last_w2_at + m * 2 * KIB) for m in range(N_TILES)]
-        residual = {m: load_residual(m, 2 * TOKENS_BYTES + m * RESIDUAL_BYTES) for m in range(N_TILES)}
+        residual = load_residual(0, 1, 2 * TOKENS_BYTES) + load_residual(1, 2, 2 * TOKENS_BYTES + RESIDUAL_BYTES)
 
         a_banks, g_banks = first_layer_banks("a"), first_layer_banks("g")
         for s in range(PASSES):
@@ -258,7 +258,7 @@ def tile_moe_res_glu_silu_kernel(tc, xT, xr, w1, w3, w2, gate, offs, out):
         for half in range(2):
             quantise_hidden(h_packed, h[half], half * HALF)
         next_w1_at = CHUNKS_AT + 6 * CHUNK_BYTES
-        next_grouped = copy_chunk(w1_raw[1][0], SHARES[1][0])
+        next_grouped = copy_chunk(w1_raw[1][0], SHARES[1][0], H_TILES)
         y = placed(loads, "y_first", [P, N_TILES, C], F32, next_w1_at)
         for tiles, first, name in ((range(1), 0, "y_bank0"), (range(1, 3), 0, "y_bank2"), (range(3), HALF, "y_bank1")):
             take_gated(y[:, tiles.start : tiles.stop, first : first + HALF], 0, first, second_layer(w2_packed, h_packed, tiles, first, HALF, name))
@@ -268,7 +268,7 @@ def tile_moe_res_glu_silu_kernel(tc, xT, xr, w1, w3, w2, gate, offs, out):
         scalar_scatter(2, 0, y[:, 2, :])
 
         a_banks, g_banks = first_layer_banks("a"), first_layer_banks("g")
-        first_layer_pass("a", 1, 0, a_banks, next_grouped)
+        first_layer_pass("a", 1, 0, a_banks, next_grouped, H)
         for s in range(1, PASSES):
             first_layer_pass("a", 1, s, a_banks, copy_chunk(w1_raw[1][s], SHARES[1][s]))
         for s in range(PASSES - 1):
@@ -283,7 +283,7 @@ def tile_moe_res_glu_silu_kernel(tc, xT, xr, w1, w3, w2, gate, offs, out):
 
         def take(m, first, count, name, bank):
             pieces[m, first] = kept(name, [P, 1, count], F32)
-            take_gated(pieces[m, first], 1, first, second_layer(w2_packed, h_packed, range(m, m + 1), first, count, bank))
+            take_gated(pieces[m, first][:], 1, first, second_layer(w2_packed, h_packed, range(m, m + 1), first, count, bank))
 
         w2_packed = [prepare_w2(0, w2_tiles[0], 0, by_vector)]
         quarter = HALF // 2
@@ -296,6 +296,8 @@ def tile_moe_res_glu_silu_kernel(tc, xT, xr, w1, w3, w2, gate, offs, out):
         take(0, 0, HALF, "y_a", "y_bank0")
         w2_packed.append(prepare_w2(2, w2_tiles[2], 0))
         scalar_scatter(0, C, pieces[0, 0][:, 0, :])
+        last = kept("y_e", [P, 1, C], F32)
+        take_gated(last[:, :, :HALF], 1, 0, second_layer(w2_packed, h_packed, range(2, 3), 0, HALF, "a_bank0"))
         take(1, 0, HALF, "y_c", "y_bank2")
         take(0, HALF, HALF, "y_b", "y_bank1")
         scalar_scatter(0, C + HALF, pieces[0, HALF][:, 0, :])
@@ -303,9 +305,9 @@ def tile_moe_res_glu_silu_kernel(tc, xT, xr, w1, w3, w2, gate, offs, out):
         take(1, HALF, HALF, "y_d", "y_bank3")
         scalar_scatter(1, C + HALF, pieces[1, HALF][:, 0, :])
         finish(0, 0, 256, residual[0][:, 0:256])
-        take(2, 0, C, "y_e", "a_bank0")
-        scalar_scatter(2, C, pieces[2, 0][:, 0, :])
+        take_gated(last[:, :, HALF:], 1, HALF, second_layer(w2_packed, h_packed, range(2, 3), HALF, HALF, "a_bank1"))
+        scalar_scatter(2, C, last[:, 0, :])
 
-        for m, cuts in ((0, (256, 640, T)), (1, (0, 512, T)), (2, (0, 512, T))):
+        for m, cuts in ((0, (256, 640, T)), (1, (0, 512, T)), (2, (0, 384, 768, T))):
             for a, b in zip(cuts, cuts[1:]):
                 finish(m, a, b, residual[m][:, a:b])

from contextlib import ExitStack

import concourse.mybir as mybir
from concourse.masks import make_identity

K, T, E, C, H, N = 1536, 1024, 2, 256, 512, 384

F32 = mybir.dt.float32
BF16 = mybir.dt.bfloat16
U32 = mybir.dt.uint32
U16 = mybir.dt.uint16
U8 = mybir.dt.uint8
FP8X4 = mybir.dt.float8_e4m3fn_x4
MULT, ADD = mybir.AluOpType.mult, mybir.AluOpType.add
SILU, COPY = mybir.ActivationFunctionType.Silu, mybir.ActivationFunctionType.Copy

P = 128
PACK = 4
K_PASS = P * PACK
PASSES = K // K_PASS
H_TILES = H // P
N_TILES = N // P
SLOTS = E * C
HALF = C // 2
RUN = 4
T_HALF = T // 2
KIB = 1024

TOKENS_BYTES, CHUNK_BYTES, W2_BYTES, RESIDUAL_BYTES = 16 * KIB, 8 * KIB, 6 * KIB, 4 * KIB
CHUNKS_AT = PASSES * TOKENS_BYTES
FIRST_W2_AT = CHUNKS_AT + 9 * CHUNK_BYTES

SHARES = ((0, 52, 64, 84, 84, 84), (72, 128, 128, 64, 92))
PIECE = P // 2
PIECE_SHARES = (28, 36)

FLOPS = 2 * SLOTS * (2 * K * H + H * N)
BYTES = 4 * (K * T + 2 * N * T + E * (2 * K * H + H * N) + SLOTS) + 2 * P * SLOTS // 16


def tile_moe_res_glu_silu_kernel(tc, xT, xr, w1, w3, w2, gate, offs, out):
    nc = tc.nc
    by_vector, by_scalar = nc.vector.tensor_copy, nc.scalar.copy
    with ExitStack() as ctx:
        keep = ctx.enter_context(tc.tile_pool(name="keep", bufs=1))
        loads = ctx.enter_context(tc.tile_pool(name="loads", bufs=1))
        stage = ctx.enter_context(tc.tile_pool(name="stage", bufs=4))
        psum = ctx.enter_context(tc.psum_pool(name="psum", bufs=1))

        def placed(pool, name, shape, dtype, at):
            return pool.tile(shape, dtype, name=name, offset=at, align_bytes=64)

        def kept(name, shape, dtype):
            return keep.tile(shape, dtype, name=name, align_bytes=64)

        offsets = keep.tile([P, SLOTS // 16], U16, name="offsets")
        x_words = [kept(f"x_words{s}", [P, T], U32) for s in range(PASSES)]
        x_scales = kept("x_scales", [P, T], U8)
        nc.gpsimd.memset(x_scales[:].bitcast(U32), 0)
        windows = [kept(f"window{m}", [P, T], F32) for m in range(N_TILES)]
        for m in range(N_TILES):
            nc.gpsimd.memset(windows[m][:], 0.0)
        identity = kept("identity", [P, P], F32)
        make_identity(nc, identity[:])
        slot_words = [kept(f"slot_words{s}", [P, SLOTS], U32) for s in range(PASSES)]
        slot_scales = kept("slot_scales", [P, SLOTS], U8)

        def load_rows(name, rows, at):
            tile = placed(loads, name, [P, PACK, rows.shape[1]], F32, at)
            nc.sync.dma_start(tile[:], rows.rearrange("(p j) c -> p j c", j=PACK))
            return tile

        def load_chunks(name, weight, e, at):
            return [load_rows(f"{name}_{e}_{s}", weight[e, s * K_PASS : (s + 1) * K_PASS, :], at + s * CHUNK_BYTES) for s in range(PASSES)]

        def load_residual(first, tiles, at):
            tile = placed(loads, f"residual{first}", [P, tiles, T], F32, at)
            nc.sync.dma_start(tile[:], xr[first * P : (first + tiles) * P, :].rearrange("(m p) t -> p m t", p=P))
            return [tile[:, n, :] for n in range(tiles)]

        def spread_gate(column):
            bank = psum.tile([P, SLOTS // P, P], F32, name="y_bank3")
            for r in range(SLOTS // P):
                nc.tensor.transpose(bank[:, r, :], column[:, r : r + 1].to_broadcast([P, P]), identity[:])
            spread = kept("gates", [P, SLOTS], F32)
            nc.scalar.activation(spread[:].rearrange("p (n r) -> p n r", r=SLOTS // P), bank[:].rearrange("p r n -> p n r"), COPY)
            return spread

        def interleave(copy, grouped, raw, a, b):
            src = raw[:, :, a:b].rearrange("p j (c i) -> p c j i", i=RUN)
            copy(grouped.rearrange("p (c i j) -> p c j i", i=RUN, j=PACK), src)

        def quantise(words, planes, grouped):
            nc.vector.quantize_mx(out=words.bitcast(FP8X4), scales=planes, in_=grouped)

        def token_pass(s, raw):
            halves = []
            for first, copy in ((0, by_vector), (T_HALF, by_scalar)):
                grouped = stage.tile([P, T_HALF * PACK], BF16, name="grouped", align_bytes=64)
                interleave(copy, grouped[:], raw, first, first + T_HALF)
                halves.append((first, grouped))
            for first, grouped in halves:
                cols = slice(first, first + T_HALF)
                quantise(x_words[s][:, cols], x_scales[4 * s : P, cols], grouped[:])
            nc.vector.tensor_copy(slot_words[s][:], x_words[s][:].indirect(offsets[:]))

        def first_layer_banks(name):
            return [psum.tile([P, H_TILES, HALF], F32, name=f"{name}_bank{half}") for half in range(2)]

        def copy_chunk(raw, share, tiles=2):
            grouped = stage.tile([P, H * PACK], BF16, name="grouped", align_bytes=64)
            src = raw[:].rearrange("p j (m t) -> p m j t", t=H_TILES)
            dst = grouped[:].rearrange("p (t m j) -> p m j t", t=H_TILES, j=PACK)
            for first in range(0, H_TILES if share > 0 else 0, tiles):
                by_vector(dst[:, :share, :, first : first + tiles], src[:, :share, :, first : first + tiles])
            if share < P:
                by_scalar(dst[:, share:], src[:, share:])
            return grouped

        def first_layer_pass(name, e, s, banks, grouped, width=H // 2):
            words = kept(f"{name}_words{s}", [P, H], U32)
            planes = kept(f"{name}_scales{s}", [P, H], U8)
            for a in range(0, H, width):
                quantise(words[:, a : a + width], planes[:, a : a + width], grouped[:, PACK * a : PACK * (a + width)])
            for half in range(2):
                slots = slice(e * C + half * HALF, e * C + (half + 1) * HALF)
                order = [(t + 2 * half) % H_TILES for t in range(H_TILES)]
                for t in order:
                    channels = slice(t * P, (t + 1) * P)
                    nc.tensor.matmul_mx(
                        out=banks[half][:, t, :],
                        lhsT=words[:, channels].bitcast(FP8X4),
                        lhsT_scale=planes[:, channels],
                        rhs=slot_words[s][:, slots].bitcast(FP8X4),
                        rhs_scale=slot_scales[4 * s : P, slots],
                        start=(s == 0 and t == order[0]),
                        stop=(s == PASSES - 1 and t == order[-1]),
                    )

        def last_pass(e, banks, pieces):
            s = PASSES - 1
            words = kept("last_words", [P, H], U32)
            planes = kept("last_scales", [P, H], U8)
            for n, raw in enumerate(pieces):
                share = PIECE_SHARES[n]
                grouped = kept(f"piece_grouped{n}", [P, H_TILES, PIECE * PACK], BF16)
                src = raw[:].rearrange("p j (m t) -> p m j t", t=H_TILES)
                dst = grouped[:].rearrange("p t (m j) -> p m j t", j=PACK)
                for pair in range(0, H_TILES, 2):
                    by_vector(dst[:, :share, :, pair : pair + 2], src[:, :share, :, pair : pair + 2])
                by_scalar(dst[:, share:], src[:, share:])
                for t in range(H_TILES):
                    cols = slice(t * P + n * PIECE, t * P + (n + 1) * PIECE)
                    quantise(words[:, cols], planes[:, cols], grouped[:, t, :])
            for half in range(2):
                slots = slice(e * C + half * HALF, e * C + (half + 1) * HALF)
                order = list(range(H_TILES)) if half == 0 else list(reversed(range(H_TILES)))
                for t in order:
                    channels = slice(t * P, (t + 1) * P)
                    nc.tensor.matmul_mx(
                        out=banks[half][:, t, :],
                        lhsT=words[:, channels].bitcast(FP8X4),
                        lhsT_scale=planes[:, channels],
                        rhs=slot_words[s][:, slots].bitcast(FP8X4),
                        rhs_scale=slot_scales[4 * s : P, slots],
                        start=False,
                        stop=(t == order[-1]),
                    )

        def silu_of(bank, at):
            act = placed(loads, f"act{at}", [P, HALF, H_TILES], F32, at)
            nc.scalar.activation(act[:], bank[:].rearrange("p t n -> p n t"), SILU)
            return act

        def prepare_w2(m, raw, first, copy=by_scalar):
            grouped = kept(f"w2_grouped{m}", [P, P * PACK], BF16)
            interleave(copy, grouped[:], raw, first, first + P)
            words = kept(f"w2_words{m}", [P, P], U32)
            planes = kept(f"w2_scales{m}", [P, P], U8)
            quantise(words[:], planes[:], grouped[:])
            return words, planes

        def hidden(name, acts, g_banks, first, count):
            half, a = divmod(first, HALF)
            h = kept(name, [P, count * H_TILES], BF16)
            sums = g_banks[half][:, :, a : a + count].rearrange("p t n -> p n t")
            nc.vector.tensor_tensor(h[:].rearrange("p (n t) -> p n t", t=H_TILES), sums, acts[half][:, a : a + count, :], MULT)
            return h

        def quantise_hidden(h_packed, h, first):
            cols = slice(first, first + h.shape[1] // H_TILES)
            quantise(h_packed[0][:, cols], h_packed[1][:, cols], h[:])

        def second_layer(w2_packed, h_packed, tiles, first, count, bank_name):
            cols = slice(first, first + count)
            bank = psum.tile([P, len(tiles), count], F32, name=bank_name)
            for n, m in enumerate(tiles):
                nc.tensor.matmul_mx(
                    out=bank[:, n, :], lhsT=w2_packed[m][0][:].bitcast(FP8X4), lhsT_scale=w2_packed[m][1][:],
                    rhs=h_packed[0][:, cols].bitcast(FP8X4), rhs_scale=h_packed[1][:, cols], start=True, stop=True,
                )
            return bank

        def take_gated(values, e, first, bank):
            slot = e * C + first
            weights = gates[:, slot : slot + bank.shape[2]].unsqueeze(1).to_broadcast(list(bank.shape))
            nc.vector.tensor_tensor(values, bank[:], weights, MULT)

        def window_at(m, slot, count):
            return windows[m][:].indirect(offsets[:, slot // 16 : (slot + count) // 16])

        def scalar_scatter(m, slot, values):
            nc.scalar.activation(window_at(m, slot, values.shape[1]), values, COPY)

        def finish(m, a, b, result):
            nc.vector.tensor_tensor(result, windows[m][:, a:b], residual[m][:, a:b], ADD)
            nc.sync.dma_start(out[m * P : (m + 1) * P, a:b], result)

        tokens = []
        for s in range(PASSES):
            tokens.append(load_rows(f"tokens{s}", xT[s * K_PASS : (s + 1) * K_PASS, :], s * TOKENS_BYTES))
            if s == 0:
                nc.sync.dma_start(offsets[:], offs)
                gate_column = kept("gate_column", [P, SLOTS // P], F32)
                nc.scalar.dma_start(gate_column[:], gate[0].rearrange("(n r) -> n r", r=SLOTS // P))
        w1_raw = [load_chunks("w1", w1, 0, CHUNKS_AT)]
        w3_raw = [load_chunks("w3", w3, 0, CHUNKS_AT + 3 * CHUNK_BYTES)]
        w2_raw = [load_rows("w2_0", w2[0], FIRST_W2_AT)]
        w1_raw.append(load_chunks("w1", w1, 1, CHUNKS_AT + 6 * CHUNK_BYTES))

        warm = kept("warm", [P, 1], F32)
        nc.scalar.activation(warm[:], identity[:, 0:1], SILU)
        gates = spread_gate(gate_column)
        for s in range(PASSES):
            token_pass(s, tokens[s])
        nc.vector.tensor_copy(slot_scales[:], x_scales[:].indirect(offsets[:]))

        w3_raw.append([load_rows(f"w3_1_{s}", w3[1, s * K_PASS : (s + 1) * K_PASS, :], s * CHUNK_BYTES) for s in range(PASSES - 1)])
        last_rows = w3[1, (PASSES - 1) * K_PASS :, :]
        last_at = (PASSES - 1) * CHUNK_BYTES
        last_pieces = [load_rows(f"w3_last{n}", last_rows[:, n * H // 2 : (n + 1) * H // 2], last_at + n * CHUNK_BYTES // 2) for n in range(2)]
        last_w2_at = PASSES * CHUNK_BYTES
        w2_tiles = [load_rows(f"w2_tile{m}", w2[1, :, m * P : (m + 1) * P], last_w2_at + m * 2 * KIB) for m in range(N_TILES)]
        residual = load_residual(0, 1, 2 * TOKENS_BYTES) + load_residual(1, 2, 2 * TOKENS_BYTES + RESIDUAL_BYTES)

        a_banks, g_banks = first_layer_banks("a"), first_layer_banks("g")
        for s in range(PASSES):
            first_layer_pass("a", 0, s, a_banks, copy_chunk(w1_raw[0][s], SHARES[0][s], H_TILES), H)
        for s in range(PASSES - 1):
            grouped = copy_chunk(w3_raw[0][s], SHARES[0][PASSES + s], H_TILES)
            if s == 0:
                acts = [silu_of(a_banks[half], CHUNKS_AT + 3 * CHUNK_BYTES + 2 * KIB * half) for half in range(2)]
            first_layer_pass("g", 0, s, g_banks, grouped, H)
        first_layer_pass("g", 0, PASSES - 1, g_banks, copy_chunk(w3_raw[0][-1], SHARES[0][-1]))
        w2_packed = [prepare_w2(m, w2_raw[0], m * P) for m in range(N_TILES)]
        h_packed = kept("h_words", [P, C], U32), kept("h_scales", [P, C], U8)
        h = [hidden(f"h{half}", acts, g_banks, half * HALF, HALF) for half in range(2)]
        for half in range(2):
            quantise_hidden(h_packed, h[half], half * HALF)
        next_w1_at = CHUNKS_AT + 6 * CHUNK_BYTES
        next_grouped = copy_chunk(w1_raw[1][0], SHARES[1][0], H_TILES)
        y = placed(loads, "y_first", [P, N_TILES, C], F32, next_w1_at)
        for tiles, first, name in ((range(1), 0, "y_bank0"), (range(1, 3), 0, "y_bank2"), (range(3), HALF, "y_bank1")):
            take_gated(y[:, tiles.start : tiles.stop, first : first + HALF], 0, first, second_layer(w2_packed, h_packed, tiles, first, HALF, name))
        scalar_scatter(0, 0, y[:, 0, :HALF])
        scalar_scatter(0, HALF, y[:, 0, HALF:])
        scalar_scatter(1, 0, y[:, 1, :])
        scalar_scatter(2, 0, y[:, 2, :])

        a_banks, g_banks = first_layer_banks("a"), first_layer_banks("g")
        first_layer_pass("a", 1, 0, a_banks, next_grouped, H)
        for s in range(1, PASSES):
            first_layer_pass("a", 1, s, a_banks, copy_chunk(w1_raw[1][s], SHARES[1][s]))
        for s in range(PASSES - 1):
            grouped = copy_chunk(w3_raw[1][s], SHARES[1][PASSES + s])
            if s == 0:
                acts = [silu_of(a_banks[0], 0)]
            first_layer_pass("g", 1, s, g_banks, grouped)
        last_pass(1, g_banks, last_pieces)
        acts.append(silu_of(a_banks[1], last_at + CHUNK_BYTES // 2))
        h_packed = kept("h_words", [P, C], U32), kept("h_scales", [P, C], U8)
        pieces = {}

        def take(m, first, count, name, bank):
            pieces[m, first] = kept(name, [P, 1, count], F32)
            take_gated(pieces[m, first][:], 1, first, second_layer(w2_packed, h_packed, range(m, m + 1), first, count, bank))

        w2_packed = [prepare_w2(0, w2_tiles[0], 0, by_vector)]
        quarter = HALF // 2
        h = [hidden("h0", acts, g_banks, 0, HALF), hidden("h1", acts, g_banks, HALF, quarter)]
        quantise_hidden(h_packed, h[0], 0)
        quantise_hidden(h_packed, h[1], HALF)
        h.append(hidden("h0", acts, g_banks, HALF + quarter, quarter))
        w2_packed.append(prepare_w2(1, w2_tiles[1], 0))
        quantise_hidden(h_packed, h[2], HALF + quarter)
        take(0, 0, HALF, "y_a", "y_bank0")
        w2_packed.append(prepare_w2(2, w2_tiles[2], 0))
        scalar_scatter(0, C, pieces[0, 0][:, 0, :])
        last = kept("y_e", [P, 1, C], F32)
        take_gated(last[:, :, :HALF], 1, 0, second_layer(w2_packed, h_packed, range(2, 3), 0, HALF, "a_bank0"))
        take(1, 0, HALF, "y_c", "y_bank2")
        take(0, HALF, HALF, "y_b", "y_bank1")
        scalar_scatter(0, C + HALF, pieces[0, HALF][:, 0, :])
        nc.vector.tensor_copy(window_at(1, C, HALF), pieces[1, 0][:, 0, :])
        take(1, HALF, HALF, "y_d", "y_bank3")
        scalar_scatter(1, C + HALF, pieces[1, HALF][:, 0, :])
        finish(0, 0, 256, residual[0][:, 0:256])
        take_gated(last[:, :, HALF:], 1, HALF, second_layer(w2_packed, h_packed, range(2, 3), HALF, HALF, "a_bank1"))
        scalar_scatter(2, C, last[:, 0, :])

        for m, cuts in ((0, (256, 640, T)), (1, (0, 512, T)), (2, (0, 384, 768, T))):
            for a, b in zip(cuts, cuts[1:]):
                finish(m, a, b, residual[m][:, a:b])
